import numpy as np, ml_dtypes
CORES = [6,15,38,47]
N = 4
BF = ml_dtypes.bfloat16
def gentries(a):
    return np.ascontiguousarray(a.reshape(8, 16, -1).transpose(0, 2, 1)).reshape(8, -1)
def gtable(e):
    e = np.asarray(e); return np.ascontiguousarray(e.reshape(8, -1, 16).transpose(0, 2, 1)).reshape(128, -1).astype(np.int32)
BASE, K, E, CL, RO = 4096, 2048, 2048, 2, 4
W = BASE + 2 * K
def injections(rng, share):
    v = np.argsort(rng.random((N, 8, W, 16), dtype=np.float32), axis=3)
    return np.where(rng.random((N, 8, W, 16), dtype=np.float32) < share, -1, v)
def parts(rng, v):
    return {"idm": v, "par": rng.integers(0, W, (N, 8, W)), "mnt": rng.integers(0, W, (N, 8, E)), "ac": rng.integers(0, E, (N, 8, 16, E)),
            "ns0": rng.integers(0, W, (N, 8, K)), "u0": rng.integers(0, 16, (N, 8, K)), "e0": rng.integers(0, E, (N, 8, K))}
def pack(d):
    return {"idm": np.ascontiguousarray(d["idm"].transpose(0, 1, 3, 2).reshape(N, 128, W)).astype(np.float32).astype(BF), "par": d["par"].astype(np.int32), "mnt": d["mnt"].astype(np.int32),
            "ac": np.ascontiguousarray(d["ac"].reshape(N, 128, E)).astype(np.int32), "ns0": np.stack([gtable(a) for a in d["ns0"]]), "u0": d["u0"].astype(np.int32), "e0": np.stack([gtable(a) for a in d["e0"]])}
def setup_inputs(rng):
    return pack(parts(rng, injections(rng, rng.choice(np.array([0.03125, 0.0625, 0.125, 0.25]), (N, 8, W, 1)))))
def skew(rng, hi, shape):
    v = np.minimum((hi * rng.random(shape) ** 3).astype(np.int64), hi - 1); s = rng.random(shape[:2] + (1,) * (len(shape) - 2)) < 0.5
    return np.where(s, v, hi - 1 - v)
def setup_inputs_spread(rng):
    return pack({"idm": injections(rng, 0.5 * rng.random((N, 8, W, 1)) ** 2), "par": skew(rng, W, (N, 8, W)), "mnt": skew(rng, W, (N, 8, E)), "ac": skew(rng, E, (N, 8, 16, E)),
                 "ns0": skew(rng, W, (N, 8, K)), "u0": skew(rng, 16, (N, 8, K)), "e0": skew(rng, E, (N, 8, K))})
def atends(rng, hi, shape):
    return np.where(rng.random(shape) < 0.8, (hi - 1) * rng.integers(0, 2, shape), rng.integers(0, hi, shape))
def setup_inputs_ends(rng):
    full = injections(rng, 0.0625); sp = np.full((N, 8, W, 16), -1); z = rng.random((N, 8, W)) < 0.75
    sp[..., 15] = np.where(z, 15, -1); sp[..., 0] = np.where(z, -1, 15)
    v = np.where(rng.random((N, 8, W, 1)) < 0.7, sp, full)
    mid = np.argsort(rng.random((N, 8, 2, 14)), axis=3) + 1
    v[:, :, [0, W - 1], 1:15] = np.where(rng.random(mid.shape) < 0.125, -1, mid); v[:, :, [0, W - 1], 0] = 0; v[:, :, [0, W - 1], 15] = 15
    d = {"idm": v, "par": atends(rng, W, (N, 8, W)), "mnt": atends(rng, W, (N, 8, E)), "ac": atends(rng, E, (N, 8, 16, E)),
         "ns0": atends(rng, W, (N, 8, K)), "u0": atends(rng, 16, (N, 8, K)), "e0": atends(rng, E, (N, 8, K))}
    d["par"][:, :, 0] = 0; d["par"][:, :, W - 1] = W - 1; d["mnt"][:, :, 0] = 0; d["mnt"][:, :, E - 1] = W - 1; d["ac"][:, :, 0, 0] = 0; d["ac"][:, :, 15, E - 1] = E - 1
    x = rng.random((N, 8, K)); top = x < 0.125; low = x > 0.875
    top[..., [1, 2, K - 1]] = True; low[..., [1, 2, K - 1]] = False; top[..., 0] = False; low[..., 0] = True
    for k, hi in (("ns0", W - 1), ("u0", 15), ("e0", E - 1)): d[k] = np.where(top, hi, np.where(low, 0, d[k]))
    return pack(d)
def setup_inputs_corners(rng):
    full = injections(rng, 0.0); v = np.where(rng.random(full.shape, dtype=np.float32) < 0.0625, -1, full); d = parts(rng, v); num = np.arange(W); row = np.arange(16)
    for r in range(N):
        for g in range(8):
            s = (g + 3 * r) % 8
            if s == 0:
                c = rng.integers(0, 3, (W, 1)); v[r, g] = np.where(c == 0, -1, np.where(c == 1, row, full[r, g]))
            if s == 1:
                one = row == rng.integers(0, 16, (W, 1)); v[r, g] = np.where(one | (rng.random((W, 1)) < 0.5), full[r, g], -1)
            if s in (2, 3, 4): v[r, g] = full[r, g]; d["par"][r, g] = (num, 0 * num, 0 * num + W - 1)[s - 2]
            if s == 5: d["par"][r, g] = np.maximum(num - 1, 0)
            if s == 6: d["par"][r, g] = rng.integers(BASE, W, W); d["mnt"][r, g] = rng.integers(BASE, W, E)
            if s == 7:
                hc = rng.permutation(BASE)[:64]; v[r, g, hc] = -1
                d["mnt"][r, g] = np.where((rng.random(E) < 0.0625) & (r % 2 == 0), d["mnt"][r, g], hc[rng.integers(0, 64, E)])
    z = rng.random((N, 8, K)); own = BASE + K * rng.integers(0, 2, (N, 8, K)) + np.arange(K); edge = rng.choice(np.array([0, W - 1, BASE - 1, BASE, BASE + K - 1, BASE + K]), (N, 8, K))
    d["ns0"] = np.where(z < 0.25, own, np.where(z < 0.5, edge, d["ns0"])); d["u0"] = np.where(rng.random((N, 8, K)) < 0.5, 15 * rng.integers(0, 2, (N, 8, K)), d["u0"])
    return pack(d)
def setup_inputs_alike(rng):
    d = parts(rng, injections(rng, 0.0625))
    for r in range(N):
        for g in range(8):
            s = (g + r) % 4
            for k, hi in (("ns0", W), ("e0", E)):
                old = d[k][r, g].copy(); few = rng.integers(0, hi, 4)
                if s < 2: d[k][r, g] = few[0]
                if s == 1: d[k][r, g, K - 1 - r] = old[K - 1 - r]
                if s == 2: d[k][r, g] = few[rng.integers(0, 4, K)]
            if s == 0: d["u0"][r, g] = rng.integers(0, 16)
        d["ac"][r, 2] = rng.integers(0, E); d["mnt"][r, 4] = rng.integers(0, W); d["par"][r, 6] = rng.integers(0, W)
    d["ac"][:, 1::2] = rng.choice(np.array([0, E - 1, E // 2, 3]), (N, 4, 16, E)); d["mnt"][:, 5] = rng.choice(np.array([0, W - 1, BASE, BASE + K]), (N, E))
    return pack(d)
def setup_inputs_calm(rng):
    v = (np.argsort(rng.random((N, 8, W, 4, 4), dtype=np.float32), axis=4) + 4 * np.arange(4)[:, None]).reshape(N, 8, W, 16)
    d = parts(rng, np.where(rng.random(v.shape, dtype=np.float32) < 0.05, -1, v))
    for g in range(8):
        h = (g + 1) % 8
        if g % 2 == 0:
            d["ns0"][:, g] = rng.integers(0, 4, (N, K)); d["u0"][:, g] = rng.integers(0, 4, (N, K)); d["e0"][:, g] = rng.integers(0, 4, (N, K)); d["par"][:, g] = rng.integers(0, 4, (N, W))
            d["ac"][:, h] = rng.integers(0, 4, (N, 16, E)); d["mnt"][:, h] = rng.choice(np.array([0, 1, 2, 3, BASE, BASE + 1, BASE + K, BASE + K + 1]), (N, E))
        else:
            d["ns0"][:, g] = W - 1 - rng.integers(0, 2, (N, K)); d["u0"][:, g] = 15 - rng.integers(0, 2, (N, K)); d["e0"][:, g] = E - 1 - rng.integers(0, 2, (N, K)); d["par"][:, g] = W - 1 - rng.integers(0, 2, (N, W))
            d["ac"][:, h] = E - 1 - rng.integers(0, 2, (N, 16, E)); d["mnt"][:, h] = rng.choice(np.array([W - 1, W - 2, BASE + K - 1, BASE + K - 2, BASE - 1, BASE - 2]), (N, E))
    return pack(d)
def check_inputs(d):
    bad = []
    for k, lo, hi in (("idm", -1, 15), ("par", 0, W - 1), ("mnt", 0, W - 1), ("ac", 0, E - 1), ("ns0", 0, W - 1), ("u0", 0, 15), ("e0", 0, E - 1)):
        v = np.asarray(d[k]).astype(np.float64)
        if not (np.min(v) >= lo and np.max(v) <= hi): bad.append("range of " + k)
    v = np.asarray(d["idm"]).astype(np.float32)
    if not np.all(v == np.rint(v)): bad.append("whole numbers in idm")
    s = np.sort(v.reshape(-1, 8, 16, W), axis=2)
    if np.any((s[:, :, 1:] == s[:, :, :-1]) & (s[:, :, 1:] >= 0)): bad.append("an id twice in a column of idm")
    return bad
def reference(idm, par, mnt, ac, ns0, u0, e0):
    a = np.ascontiguousarray(idm.astype(np.float32).astype(np.int64).reshape(N, 8, 16, W).transpose(0, 1, 3, 2))
    p = par.astype(np.int64); mt = mnt.astype(np.int64); mv = ac.astype(np.int64).reshape(N, 8, 16, E)
    ns = np.stack([gentries(x) for x in ns0]).astype(np.int64); e = np.stack([gentries(x) for x in e0]).astype(np.int64); u = u0.astype(np.int64)
    R = np.arange(N)[:, None, None]; G = np.arange(8)[None, :, None]; H = (G + 1) % 8
    for t in range(RO):
        w = u; n = ns
        for step in range(CL):
            w = np.where(w >= 0, a[R, G, n, np.maximum(w, 0)], -1); n = p[R, G, n]
        Q = (R + 1 + t % (N - 1)) % N
        col = a[Q, H, mt[Q, H, e]]
        hit = (col == w[..., None]) & (w[..., None] >= 0); ok = np.any(hit, axis=3); k = np.argmax(hit, axis=3)
        e2 = mv[Q, H, k, e]; up = p[R, G, ns]; S = BASE + K * (t % 2)
        if t < RO - 1:
            a[:, :, S:S + K] = np.where(ok[..., None], col, a[:, :, S:S + K]); p[:, :, S:S + K] = np.where(ok, ns, p[:, :, S:S + K])
        ns = np.where(ok, S + e2 % K, up); u = np.where(ok, k, u); e = np.where(ok, e2, e)
    return {"yn": np.stack([gtable(x) for x in ns]).astype(np.float32), "yu": u.astype(np.float32), "ye": np.stack([gtable(x) for x in e]).astype(np.float32)}

@@ -1,0 +1,492 @@
+from concourse.bass import DstId, RemoteDMATransfer
+from concourse.mybir import dt, AluOpType, AxisListType, ActivationFunctionType
+
+ALU = AluOpType
+AF = ActivationFunctionType
+N, W, K, BASE, RO = 4, 8192, 2048, 4096, 4
+CH = 512
+OPT = {
+    "dm": [(0, 768, "a"), (768, 1536, "a"), (1536, 2048, "a")],
+    "op3a": (2, 3),
+    "insv": 512,
+    "colv": (),
+    "vlate": (3,),
+    "ac": (0, 2, -1, 3),
+    "v0": 4, "op3l": (2, 3),
+    "pre7": 1,
+}
+ACCH = [(0, 1024), (1024, 2048)]
+
+SCRATCH = {
+    "M": ("sbuf", [128, W], "bfloat16"), "P": ("sbuf", [128, W], "bfloat16"),
+    "V": ("sbuf", [128, K], "bfloat16"), "m1": ("sbuf", [128, K], "bfloat16"),
+    "mk": ("sbuf", [128, K], "bfloat16"), "m2": ("sbuf", [128, K], "bfloat16"),
+    "col": ("sbuf", [128, K], "bfloat16"), "hit": ("sbuf", [128, K], "bfloat16"),
+    "acm": ("sbuf", [128, K], "float16"), "pg": ("sbuf", [128, K], "bfloat16"),
+    "aco": ("sbuf", [128, K], "int32"),
+    "xp": ("sbuf", [128, 2, 16, 16], "int32"), "xpf": ("sbuf", [128, 16, 2, 16], "float32"),
+    "xpt": ("sbuf", [128, 512], "float32"), "pl": ("sbuf", [128, 512], "float32"), "Lt": ("sbuf", [128, 32], "uint16"),
+    "xm": ("sbuf", [128, 2, 4, 16], "int32"), "xmf": ("sbuf", [128, 4, 2, 16], "float32"), "xmt": ("sbuf", [128, 128], "float32"),
+    "ui": ("sbuf", [128, K], "int32"), "ur": ("sbuf", [128, K], "bfloat16"),
+    "ei": ("sbuf", [128, 128], "int32"),
+    "hi": ("sbuf", [128, 512], "bfloat16"), "lo": ("sbuf", [128, 512], "bfloat16"),
+    "ns": ("sbuf", [128, 128], "int32"), "yi": ("sbuf", [128, 128], "int32"),
+    "xg": ("sbuf", [128, 128], "float32"), "xs": ("sbuf", [128, 144], "float32"),
+    "ci": ("sbuf", [128, 4], "int32"), "cj": ("sbuf", [128, 8], "int32"), "cf": ("sbuf", [128, 16], "float32"),
+    "ahi": ("sbuf", [128, 128], "bfloat16"), "alo": ("sbuf", [128, 128], "bfloat16"),
+    "WS": ("sbuf", [128, 144], "bfloat16"), "WZ": ("sbuf", [128, 144], "bfloat16"),
+    "WA": ("sbuf", [128, 144], "float16"), "WY": ("sbuf", [128, 144], "bfloat16"),
+    "RF": ("sbuf", [128, 128], "float32"),
+}
+for _n in ("BO", "BR", "BN", "ZT", "HI", "G8", "za", "zr"):
+    SCRATCH[_n] = ("sbuf", [128, 128], "bfloat16")
+for _n in ("e", "n1s", "dn", "f0", "f1", "f2", "t1", "t2", "oy", "ou"):
+    SCRATCH[_n] = ("sbuf", [128, 128], "float32")
+for _n in ("Lns", "Lp", "Ln1", "Le", "Lin", "Lm"):
+    SCRATCH[_n] = ("sbuf", [128, 128], "uint16")
+for _t in range(RO):
+    SCRATCH["dmo%d" % _t] = ("sbuf", [128, K], "bfloat16")
+    SCRATCH["dmi%d" % _t] = ("sbuf", [128, K], "bfloat16")
+for _t in range(RO - 1):
+    SCRATCH["win%d" % _t] = ("sbuf", [128, 2 * K], "bfloat16")
+    SCRATCH["acr%d" % _t] = ("sbuf", [128, K], "int32")
+for _t in range(8):
+    SCRATCH["B%d" % _t] = ("psum", [128, CH], "float32")
+
+SEMAPHORES = (["cv", "ca", "cp", "cg", "sent", "hsent"] + ["dm%d" % t for t in range(RO)] + ["acs%d" % t for t in range(3)]
+              + ["h%d" % t for t in range(len(ACCH))] + ["d%d" % i for i in range(48)])
+
+
+def helper_of(T, topo, r):
+    c = T.cores[r]
+    for h in topo.cores_of(c):
+        if T.rank_of(h) is None and topo.die(h) != topo.die(c) and all(topo.may_write(h, o) for o in T.cores if o != c):
+            return h
+    raise ValueError("no helper")
+
+
+def bits(m):
+    return bin(m).count("1")
+
+
+def helper_program(g, core, T, topo, r):
+    src = T.cores[r]
+    far = T.cores[(r + 1) % N]
+    m_in = topo.mask(src, core) & ~topo.mask(src, far)
+    total = 0
+    for s in range(3):
+        dst = T.cores[(r - 1 - s) % N]
+        rid, pid, _ = topo.addr(dst)
+        m = topo.mask(core, dst)
+        for i, (a, b) in enumerate(ACCH):
+            if s == 0:
+                g.wait_ge(T.sem["h%d" % i], bits(m_in))
+            g.remote_dma(T["acr%d" % s][:, a:b], T.aco[:, a:b], T.sem["acs%d" % s], T.sem.hsent, pid, rid, m)
+            total += bits(m)
+    g.wait_ge(T.sem.hsent, total)
+
+
+def rank_program(g, core, T, topo):
+    r = T.rank_of(core)
+    if r is None:
+        for q in range(N):
+            if helper_of(T, topo, q) == core:
+                helper_program(g, core, T, topo, q)
+        return
+
+    Q = {"v": g.vector, "a": g.scalar, "p": g.tensor, "s": g.sync, "g": g}
+    cnt = {"v": 0, "a": 0, "p": 0, "g": 0}
+    waited = {q: {} for q in Q}
+    regs = {}
+    toks = {}
+    nd = [0]
+
+    def rng(x):
+        if isinstance(x, str):
+            return (x, 0, 1 << 30)
+        return x
+
+    def sync(q, reads, writes):
+        need = {}
+        for kind, lst in (("r", reads), ("w", writes)):
+            for x in lst:
+                n, lo, hi = rng(x)
+                ps = SCRATCH[n][0] == "psum"
+                for (l2, h2, k2, tok, q2) in regs.get(n, []):
+                    if q == "p" and q2 == "p":
+                        continue
+                    whole = ps and q2 != q
+                    if not whole and (h2 <= lo or hi <= l2):
+                        continue
+                    if kind == "r" and k2 == "r" and not whole:
+                        continue
+                    need[tok[0]] = max(need.get(tok[0], 0), tok[1])
+        for s, v in need.items():
+            if waited[q].get(s, 0) < v:
+                Q[q].wait_ge(T.sem[s], v)
+                waited[q][s] = v
+
+    def note(q, reads, writes, tok):
+        toks[tok[0]] = max(toks.get(tok[0], 0), tok[1])
+        for x in writes:
+            n, lo, hi = rng(x)
+            regs[n] = [z for z in regs.get(n, []) if not (lo <= z[0] and z[1] <= hi)] + [(lo, hi, "w", tok, q)]
+        for x in reads:
+            n, lo, hi = rng(x)
+            regs[n] = [z for z in regs.get(n, []) if not (z[2] == "r" and z[3][0] == tok[0] and lo <= z[0] and z[1] <= hi)] + [(lo, hi, "r", tok, q)]
+
+    def op(q, reads, writes, fn):
+        sync(q, reads, writes)
+        cnt[q] += 1
+        fn().then_inc(T.sem["c" + q], 1)
+        note(q, reads, writes, ("c" + q, cnt[q]))
+
+    def dma(q, reads, writes, pairs):
+        sync(q, reads, writes)
+        s = "d%d" % nd[0]
+        nd[0] += 1
+        for o, i in pairs:
+            Q[q].dma_start(o, i).then_inc(T.sem[s], 16)
+        note("dma", reads, writes, (s, 16 * len(pairs)))
+
+    sent = [0]
+
+    def remote(reads, out, in_, sem, dst, m):
+        sync("g", reads, [])
+        rid, pid, _ = topo.addr(dst)
+        g.remote_dma(out, in_, T.sem[sem], T.sem.sent, pid, rid, m)
+        sent[0] += bits(m)
+
+    v, a, pe = g.vector, g.scalar, g.tensor
+
+    def ts(out, in0, s1, s2, o0, o1, reads, writes):
+        if s2 is None:
+            op("v", reads, writes, lambda: v.tensor_scalar(out, in0, s1, None, o0))
+        else:
+            op("v", reads, writes, lambda: v.tensor_scalar(out, in0, s1, s2, o0, o1))
+
+    def tt(out, in0, in1, o, reads, writes):
+        op("v", reads, writes, lambda: v.tensor_tensor(out, in0, in1, o))
+
+    def cp(out, in_, reads, writes):
+        op("v", reads, writes, lambda: v.tensor_copy(out, in_))
+
+    def act(out, in_, f, reads, writes, bias=0.0, scale=1.0):
+        op("a", reads, writes, lambda: a.activation(out, in_, f, bias=bias, scale=scale))
+
+    def gather(q, out, in_, reads, writes):
+        if q == "a":
+            act(out, in_, AF.Copy, reads, writes)
+        else:
+            cp(out, in_, reads, writes)
+
+    def mm(out, l, rh, st, sp, reads, writes):
+        op("p", reads, writes, lambda: pe.matmul(out, l, rh, st, sp))
+
+    def ind(win, width, lst, lo, hi):
+        return T[win][:, 0:width].indirect(T[lst][:, lo // 16:hi // 16])
+
+    def L(lst, lo, hi):
+        return (lst, lo // 16, hi // 16)
+
+    def listpass(bank, half, Wn, src, first=True):
+        o = T[bank][:, 64 * half:64 * half + 64]
+        for i in range(16):
+            mm(o, T[Wn][:, 15 - i:143 - i], T[src][:, 1024 * half + i:1024 * (half + 1):16], first and i == 0, i == 15,
+               [Wn, (src, 1024 * half, 1024 * (half + 1))], [bank])
+
+    hp = helper_of(T, topo, r)
+    DM = OPT["dm"]
+    for t in range(RO):
+        src = T.cores[(r + 1 + t % 3) % N]
+        note("rem", [], ["dmi%d" % t], ("dm%d" % t, len(DM) * bits(topo.mask(src, core))))
+    for s in range(3):
+        src = helper_of(T, topo, (r + 1 + s) % N)
+        note("rem", [], ["acr%d" % s], ("acs%d" % s, len(ACCH) * bits(topo.mask(src, core))))
+
+    def ld_idm(q, c):
+        dma(q, [], [("M", K * c, K * c + K)], [(T.M[:, K * c:K * c + K], T.idm[:, K * c:K * c + K])])
+
+    def ld_ac(i):
+        lo, hi = ACCH[i]
+        dma("s", [], [("aco", lo, hi)], [(T.aco[:, lo:hi], T.ac[:, lo:hi])])
+
+    AO = OPT["ac"]
+    dma("a", [], ["xp"], [(T.xp[:, j, :, :], T.par[j:8:2, :]) for j in range(2)])
+    dma("s", [], ["ui"], [(T.ui[0:8, :], T.u0[:])])
+    dma("s", [], ["xm"], [(T.xm[:, j, :, :], T.mnt[j:8:2, :]) for j in range(2)])
+    dma("a", [], ["ns"], [(T.ns[:], T.ns0[:])])
+    dma("a", [], ["ei"], [(T.ei[:], T.e0[:])])
+    for i in range(2):
+        if AO[i] == 0:
+            ld_ac(i)
+    ld_idm("a", 2)
+    ld_idm("s", 3)
+    ld_idm("a", 0)
+    ld_idm("s", 1)
+    for i in range(2):
+        if AO[i] == 1:
+            ld_ac(i)
+    op("v", [], [("P", 0, W // 2)], lambda: v.memset(T.P[:, 0:W // 2], 0.0))
+    op("g", [], ["ci"], lambda: g.iota(T.ci[:, 0:3], [[-16, 3]], 144, 1))
+    op("g", [], ["xs"], lambda: g.iota(T.xs[:], [[1, 144]], -15, 0, allow_small_or_imprecise_dtypes=True))
+    op("g", [], ["xg"], lambda: g.iota(T.xg[:], [[16, 8], [0, 16]], 0, 0, allow_small_or_imprecise_dtypes=True))
+    op("g", [], ["ahi"], lambda: g.iota(T.ahi[:], [[32, 128]], 2 * K, 0, allow_small_or_imprecise_dtypes=True))
+    op("g", [], [("P", W // 2, W)], lambda: g.iota(T.P[:, W // 2:W], [[0, W // 2]], 0, 0, allow_small_or_imprecise_dtypes=True))
+    m_on = topo.mask(core, hp) & ~topo.mask(core, T.cores[(r + 1) % N])
+
+    def ac_on(i):
+        lo, hi = ACCH[i]
+        remote([("aco", lo, hi)], T.aco[:, lo:hi], T.aco[:, lo:hi], "h%d" % i, hp, m_on)
+
+    for i in range(2):
+        if AO[2 + i] == 0:
+            ac_on(i)
+
+    ts(T.cj[:, 0:3], T.ci[:, 0:3], 127, None, ALU.bitwise_and, None, ["ci"], [("cj", 0, 3)])
+    ts(T.cj[:, 3:6], T.ci[:, 0:3], 112, None, ALU.bitwise_and, None, ["ci"], [("cj", 3, 6)])
+    ts(T.cj[:, 6:7], T.ci[:, 0:1], 15, None, ALU.bitwise_and, None, ["ci"], [("cj", 6, 7)])
+    cp(T.cf[:, 0:7], T.cj[:, 0:7], ["cj"], [("cf", 0, 7)])
+    C = lambda j: T.cf[:, j:j + 1]
+    R = lambda j: ("cf", j, j + 1)
+    xm_ = T.xs[:, 15:143]
+    ts(C(11), C(1), 16.0, None, ALU.mult, None, [R(1)], [R(11)])
+    ts(C(15), C(6), 32.0, None, ALU.mult, None, [R(6)], [R(15)])
+    ts(T.G8[0:8, :], T.xg[0:8, :], T.cf[0:8, 11:12], None, ALU.is_equal, None, ["xg", R(11)], ["G8"])
+    ts(T.Lt[:], T.xs[:, 15:47], C(15), None, ALU.add, None, ["xs", R(15)], ["Lt"])
+
+    def consts_climb():
+        ts(T.RF[:], xm_, C(0), None, ALU.is_equal, None, ["xs", R(0)], ["RF"])
+        ts(T.BO[:], T.xg[:], C(4), None, ALU.is_equal, None, ["xg", R(4)], ["BO"])
+        ts(T.WS[:], T.xs[:], C(4), None, ALU.is_equal, None, ["xs", R(4)], ["WS"])
+        ts(C(7), C(6), 1.0 / 32, 0.75 / 32 - 7.5, ALU.mult, ALU.add, [R(6)], [R(7)])
+        ts(C(13), C(6), -1.0, 240.0 - 0.75, ALU.mult, ALU.add, [R(6)], [R(13)])
+        ts(T.BR[:], T.xg[:], C(3), None, ALU.is_equal, None, ["xg", R(3)], ["BR"])
+        ts(T.BN[:], T.xg[:], C(3), -1.0, ALU.is_equal, ALU.mult, ["xg", R(3)], ["BN"])
+
+    def consts_abroad():
+        ts(C(8), C(6), 1.0 / 32, 0.75 / 32 - 15.0, ALU.mult, ALU.add, [R(6)], [R(8)])
+        ts(C(9), C(6), 2.0, None, ALU.mult, None, [R(6)], [R(9)])
+        ts(C(10), C(6), 0.5, None, ALU.mult, None, [R(6)], [R(10)])
+        ts(C(14), C(6), -1.0, 480.0 - 0.75, ALU.mult, ALU.add, [R(6)], [R(14)])
+        ts(T.WZ[:], T.xs[:], C(5), -4096.0, ALU.is_equal, ALU.mult, ["xs", R(5)], ["WZ"])
+        ts(T.WA[:], T.xs[:], C(5), None, ALU.is_equal, None, ["xs", R(5)], ["WA"])
+        ts(T.za[:], T.xg[:], C(5), None, ALU.is_equal, None, ["xg", R(5)], ["za"])
+        ts(T.zr[:], xm_, C(2), 2.0, ALU.is_equal, ALU.mult, ["xs", R(2)], ["zr"])
+        ts(T.HI[:], xm_, C(1), 0.5, ALU.is_equal, ALU.mult, ["xs", R(1)], ["HI"])
+        ts(T.alo[:], T.xg[:], 0.0, C(9), ALU.mult, ALU.add, ["xg", R(9)], ["alo"])
+        ts(T.WY[:], T.xs[:], C(4), C(10), ALU.is_equal, ALU.mult, ["xs", R(4), R(10)], ["WY"])
+        tt(T.ZT[:], T.zr[:], T.za[:], ALU.subtract, ["zr", "za"], ["ZT"])
+
+    def p_rows():
+        dma("s", ["hi", "lo"], ["P"], [(T.P[0:128:16, :], T.hi[:]), (T.P[1:128:16, :], T.lo[:])])
+
+    for j in range(2):
+        cp(T.xpf[:, :, j, :], T.xp[:, j, :, :], ["xp"], [("xpf", j, j + 1)])
+    for j in range(2):
+        cp(T.xmf[:, :, j, :], T.xm[:, j, :, :], ["xm"], [("xmf", j, j + 1)])
+    op("v", ["xpf"], ["xpt"], lambda: v.transpose(T.xpt[:], T.xpf[:]))
+    op("v", ["xmf"], ["xmt"], lambda: v.transpose(T.xmt[:], T.xmf[:]))
+    cp(T.pl[:], ind("xpt", 512, "Lt", 0, 512), ["xpt", "Lt"], ["pl"])
+    for b in range(4):
+        cp(T.Lm[:, b:128:4], T.xmt[:, 32 * b:32 * b + 32], ["xmt"], [("Lm", b, b + 1)])
+    cp(T.hi[:], T.pl[:], ["pl"], ["hi"])
+    cp(T.B6[:, 256:512], T.pl[:, 256:512], ["pl"], [("B6", 256, 512)])
+    tt(T.lo[:], T.pl[:], T.hi[:], ALU.subtract, ["pl", "hi"], ["lo"])
+    p_rows()
+    for i in range(2):
+        if AO[i] == 2:
+            ld_ac(i)
+    if AO[2] == -1:
+        sync("g", ["lo"], [])
+        ac_on(0)
+    cp(T.ur[0:8, :], T.ui[0:8, :], ["ui"], ["ur"])
+    for c in range(4):
+        mm(T["B%d" % c][:], T.G8[0:8, :], T.ur[0:8, CH * c:CH * c + CH], True, True, ["G8", "ur"], ["B%d" % c])
+    cp(T.e[:], T.ei[:], ["ei"], ["e"])
+    cp(T.Lns[:], T.ns[:], ["ns"], ["Lns"])
+    consts_climb()
+
+    def conv(q, lo, hi):
+        o, w = T.M[:, lo:hi], ("M", lo, hi)
+        if q == "a":
+            act(o, o, AF.Identity, [w], [w], bias=0.75 / 32, scale=1.0 / 32)
+        else:
+            ts(o, o, 0.75, 1.0 / 32, ALU.add, ALU.mult, [w], [w])
+
+    for c in (2, 3, 0):
+        conv("a", K * c, K * c + K)
+    conv("a", K, K + 640)
+    for c in range(OPT["v0"]):
+        ts(T.V[:, CH * c:CH * c + CH], T["B%d" % c][:], C(6), 0.5, ALU.is_equal, ALU.subtract,
+           ["B%d" % c, R(6)], [("V", CH * c, CH * c + CH)])
+    conv("v", K + 640, 2 * K)
+    for c in range(OPT["v0"], 4):
+        ts(T.V[:, CH * c:CH * c + CH], T["B%d" % c][:], C(6), 0.5, ALU.is_equal, ALU.subtract,
+           ["B%d" % c, R(6)], [("V", CH * c, CH * c + CH)])
+
+    chunks = [(CH * c, CH * c + CH) for c in range(4)]
+    z, nok, sc = T.B4[:, 0:128], T.B6[:, 0:128], T.B6[:, 128:256]
+    NOK, SC = ("B6", 0, 128), ("B6", 128, 256)
+    late = []
+
+    def vsign(c):
+        lo, hi = chunks[c]
+        act(T.V[:, lo:hi], T["B%d" % c][:], AF.Sign, ["B%d" % c], [("V", lo, hi)])
+
+    for t in range(RO):
+        last = t == RO - 1
+        S = BASE + K * (t % 2)
+        dmo, dmi, acr = "dmo%d" % t, "dmi%d" % t, "acr%d" % (t % 3)
+        dst = T.cores[(r - 1 - t % 3) % N]
+        for i, (lo, hi, q) in enumerate(DM):
+            gather(q, T[dmo][:, lo:hi], ind("M", W, "Lm", lo, hi), ["M", "Lm"], [(dmo, lo, hi)])
+            remote([(dmo, lo, hi)], T[dmi][:, lo:hi], T[dmo][:, lo:hi], "dm%d" % t, dst, topo.mask(core, dst))
+            if t == 0:
+                for j in range(2):
+                    if AO[j] == 3 + i:
+                        sync("s", [(dmo, lo, hi)], [])
+                        ld_ac(j)
+                for j in range(2):
+                    if AO[2 + j] == i + 1:
+                        ac_on(j)
+        for c in late:
+            vsign(c)
+
+        def op2(c):
+            lo, hi = chunks[c]
+            tt(T.m1[:, lo:hi], ind("M", W, "Lns", lo, hi), T.V[:, lo:hi], ALU.min, ["M", "Lns", ("V", lo, hi)], [("m1", lo, hi)])
+            mm(T["B%d" % c][:], T.BO[:], T.m1[:, lo:hi], True, True, ["BO", ("m1", lo, hi)], ["B%d" % c])
+
+        ts(T.yi[:], T.ns[:], 4, None, ALU.arith_shift_right, None, ["ns"], ["yi"])
+        if t > 0:
+            tt(T.e[:], T.t2[:], T.B5[:, 0:128], ALU.add, ["B5", "t2"], ["e"])
+        ts(sc, T.yi[:], -8191.0 / 512, None, ALU.mult, None, ["yi"], [SC])
+        mm(T.B7[:, 0:128], T.RF[:], T.e[:], True, True, ["RF", "e"], ["B7"])
+        op2(0)
+        tt(T.f1[:], T.ns[:], sc, ALU.add, [SC, "ns"], ["f1"])
+        if not last:
+            oc = 256 + 128 * (t % 2)
+            old, OLD = T.B6[:, oc:oc + 128], ("B6", oc, oc + 128)
+            tt(T.dn[:], old, T.ns[:], ALU.subtract, [OLD, "ns"], ["dn"])
+        ts(T.Lp[:], T.f1[:], 512.0, None, ALU.mult, None, ["f1"], ["Lp"])
+        cp(T.Le[:], T.B7[:, 0:128], ["B7"], ["Le"])
+        op2(1)
+        op2(2)
+        op2(3)
+        for h in range(2):
+            lo, hi = 1024 * h, 1024 * h + 1024
+            act(T.pg[:, lo:hi], ind("P", W, "Lp", lo, hi), AF.Copy, ["P", "Lp"], [("pg", lo, hi)])
+            listpass("B%d" % (4 + h), h, "WS", "pg")
+
+        def n1copy(h):
+            act(T.n1s[:, 64 * h:64 * h + 64], T["B%d" % (4 + h)][:, 64 * h:64 * h + 64], AF.Identity,
+                ["B%d" % (4 + h)], [("n1s", 64 * h, 64 * h + 64)], bias=-float(S))
+
+        if not last:
+            win = "win%d" % t
+            dma("s", [dmi], [(win, 0, K)], [(T[win][0:112, 0:K], T[dmi][16:128, :]), (T[win][112:128, 0:K], T[dmi][0:16, :])])
+            if t < 2:
+                S2, w2 = BASE + K * ((t + 1) % 2), "win%d" % (t + 1)
+                dma("s", [("M", S2, S2 + K)], [(w2, K, 2 * K)], [(T[w2][:, K:2 * K], T.M[:, S2:S2 + K])])
+        n1copy(0)
+        th, ab = (7, 13) if t == 0 else (8, 14)
+        done1 = False
+        op3a = OPT["op3l"] if last else OPT["op3a"]
+        for c, (lo, hi) in enumerate(chunks):
+            if c in op3a:
+                act(T.mk[:, lo:hi], T["B%d" % c][:], AF.Abs, ["B%d" % c, R(ab)], [("mk", lo, hi)], bias=C(ab), scale=32.0)
+                if not done1:
+                    n1copy(1)
+                    done1 = True
+            else:
+                ts(T.mk[:, lo:hi], T["B%d" % c][:], C(th), None, ALU.is_equal, None, ["B%d" % c, R(th)], [("mk", lo, hi)])
+        if not done1:
+            n1copy(1)
+        for c, (lo, hi) in enumerate(chunks):
+            b = "B%d" % c
+            if c % 2 == 0:
+                h = c // 2
+                ts(T.Ln1[:, 64 * h:64 * h + 64], T.n1s[:, 64 * h:64 * h + 64], float(S), None, ALU.add, None,
+                   [("n1s", 64 * h, 64 * h + 64)], [("Ln1", 64 * h, 64 * h + 64)])
+            far = c in op3a
+            if far:
+                mm(T[b][:], T.BN[:], T.mk[:, lo:hi], True, False, ["BN", ("mk", lo, hi)], [b])
+            tt(T.m2[:, lo:hi], ind("M", W, "Ln1", lo, hi), T.mk[:, lo:hi], ALU.max if far else ALU.mult,
+               ["M", L("Ln1", lo, hi), ("mk", lo, hi)], [("m2", lo, hi)])
+            mm(T[b][:], T.BR[:], T.m2[:, lo:hi], not far, True, ["BR", ("m2", lo, hi)], [b])
+        if t == 0:
+            consts_abroad()
+        if t == 0:
+            cp(T[win][:, K:2 * K], T.M[:, S:S + K], [("M", S, S + K)], [(win, K, 2 * K)])
+        for c, (lo, hi) in enumerate(chunks):
+            if c in OPT["colv"]:
+                ts(T.col[:, lo:hi], ind(dmi, K, "Le", lo, hi), 0.25 / 32, None, ALU.max, None, [dmi, "Le"], [("col", lo, hi)])
+            else:
+                act(T.col[:, lo:hi], ind(dmi, K, "Le", lo, hi), AF.Abs, [dmi, "Le"], [("col", lo, hi)])
+
+        def zhalf(h):
+            o = T.B4[:, 64 * h:64 * h + 64]
+            mm(o, T.HI[:], T.ahi[:, 64 * h:64 * h + 64], True, False, ["HI", "ahi"], ["B4"])
+            mm(o, T.HI[:], T.alo[:, 64 * h:64 * h + 64], False, False, ["HI", "alo"], ["B4"])
+            listpass("B4", h, "WZ", "hit", first=False)
+
+        late = [] if last else list(OPT["vlate"])
+        for c, (lo, hi) in enumerate(chunks):
+            b = "B%d" % c
+            tt(T.hit[:, lo:hi], T.col[:, lo:hi], T[b][:], ALU.is_equal, [("col", lo, hi), b], [("hit", lo, hi)])
+            if c % 2 == 1:
+                zhalf(c // 2)
+            mm(T[b][:], T.HI[:], T.V[:, lo:hi], True, False, ["HI", ("V", lo, hi)], [b])
+            mm(T[b][:], T.ZT[:], T.hit[:, lo:hi], False, True, ["ZT", ("hit", lo, hi)], [b])
+            if c not in late:
+                vsign(c)
+
+        def op7(c):
+            lo, hi = chunks[c]
+            tt(T.acm[:, lo:hi], ind(acr, K, "Le", lo, hi), T.hit[:, lo:hi], ALU.mult, [acr, "Le", ("hit", lo, hi)], [("acm", lo, hi)])
+            if c % 2 == 1:
+                listpass("B5", c // 2, "WA", "acm")
+
+        pre = 1 if last else (0 if t == 0 else OPT["pre7"])
+        for c in range(pre):
+            op7(c)
+        if not last:
+            tt(T.f0[:], T.e[:], z, ALU.max, ["e", "B4"], ["f0"])
+        ts(nok, z, 0.0, None, ALU.is_gt, None, ["B4"], [NOK])
+        if not last:
+            cp(T.Lin[:], T.f0[:], ["f0"], ["Lin"])
+            tt(sc, T.dn[:], nok, ALU.mult, ["dn", NOK], [SC])
+            x = K - OPT["insv"]
+            for lo, hi, q in ((0, x // 2, "a"), (x // 2, x, "a"), (x, K, "v")):
+                if hi > lo:
+                    gather(q, T.M[:, S + lo:S + hi], ind(win, 2 * K, "Lin", lo, hi), [win, "Lin"], [("M", S + lo, S + hi)])
+            tt(old, T.ns[:], sc, ALU.add, [SC, "ns"], [OLD])
+            cp(T.hi[:, oc:oc + 128], old, [OLD], [("hi", oc, oc + 128)])
+            tt(T.lo[:, oc:oc + 128], old, T.hi[:, oc:oc + 128], ALU.subtract, [OLD, ("hi", oc, oc + 128)], [("lo", oc, oc + 128)])
+            p_rows()
+            op7(pre)
+        else:
+            op7(pre)
+            for i in range(16):
+                mm(T.B7[:, 0:128], T.WY[:, 15 - i:143 - i], T.V[:, 128 * i:128 * i + 128], i == 0, i == 15,
+                   ["WY", ("V", 128 * i, 128 * i + 128)], ["B7"])
+            act(T.ou[:], T.B7[:, 0:128], AF.Identity, ["B7"], ["ou"], bias=60.0)
+            dma("a", ["ou"], [], [(T.yu[:], T.ou[:])])
+        for c in range(pre + 1, 4):
+            op7(c)
+        tt(T.f1[:], T.n1s[:], nok, ALU.mult, ["n1s", NOK], ["f1"])
+        tt(T.t2[:], T.e[:], nok, ALU.mult, ["e", NOK], ["t2"])
+        ts(T.t1[:], T.f1[:], float(S), None, ALU.add, None, ["f1"], ["t1"])
+        if not last:
+            tt(T.ns[:], T.t1[:], T.B5[:, 0:128], ALU.add, ["t1", "B5"], ["ns"])
+            cp(T.Lns[:], T.ns[:], ["ns"], ["Lns"])
+        else:
+            tt(T.oy[:], T.t1[:], T.B5[:, 0:128], ALU.add, ["t1", "B5"], ["oy"])
+            dma("s", ["oy"], [], [(T.yn[:], T.oy[:])])
+            tt(T.e[:], T.t2[:], T.B5[:, 0:128], ALU.add, ["t2", "B5"], ["e"])
+            dma("a", ["e"], [], [(T.ye[:], T.e[:])])
+
+    g.wait_ge(T.sem.sent, sent[0])
+    for s, val in toks.items():
+        g.wait_ge(T.sem[s], val)

@@ -6,41 +6,52 @@ AF = ActivationFunctionType
 N, W, K, BASE, RO = 4, 8192, 2048, 4096, 4
 CH = 512
 OPT = {
-    "dm": [(0, 768, "a"), (768, 1536, "a"), (1536, 2048, "a")],
-    "op3a": (2, 3),
-    "insv": 512,
-    "colv": (),
-    "vlate": (3,),
-    "ac": (0, 2, -1, 3),
-    "v0": 4, "op3l": (2, 3),
-    "pre7": 1,
+    "dm": [(0, 768, "h"), (768, 1536, "d"), (1536, 2048, "d")],
+    "dm0": [(0, 768, "h"), (768, 1536, "d"), (1536, 2048, "d")],
+    "rot": [(0, 768), (768, 1536), (1536, 2048)],
+    "acway": "kkkk", "help": "a0 d0 a1 d1 a2 d2 d3", "gate": 99,
+    "fill": (1792, 3584, 7168),
+    "v0a": (2, 3),
+    "acpre": 1,
+    "acdir": (2, 3),
+    "idm": 2, "loads": "par u mnt i0 i1 ns e",
+    "first": "A0 a am V1 A1 B1 B3 V0 lm p o1 le d B0 B2 A2 o3 q2 P0 o2 q3 P1 C0 C1 C2 n0 D0 D1 n1 old late C3 D2 D3",
+    "next": "r0 E2 E0 F0 E1 F1 F2 r1 E3 i0 r2 k0 W0 F3 H0 G0 i1 k1 t0 sc nm t1 H1 hi I0 G1 W1 G2 s0 W2 A0 lo G3 B0 I1 x1 te W3 x0 B1 I2 em A1 s1 I3 a am B2 d A2 C1 p e B3 C0 lm P0 C2 C3 old le n0 P1 D1 D0 n1 D3 D2",
+    "last": "E0 F0 E1 E2 F1 W0 E3 F2 F3 W2 k0 W1 G0 G2 W3 k1 I0 t0 I1 G1 t1 te I2 y0 I3 u G3 y1",
+    "ins": [(0, 1024), (1024, 2048)],
 }
-ACCH = [(0, 1024), (1024, 2048)]
+OPT.update({
+    "dm": [(0, 768, "d"), (768, 1536, "d"), (1536, 2048, "d")], "dm0": [(0, 768, "d"), (768, 1536, "d"), (1536, 2048, "d")],
+    "loads": "par u mnt c0 c1 i0 i1 ns e",
+    "next": "E0 E1 F0 F1 E2 r0 E3 W1 F2 i0 r2 k0 F3 r1 G0 W0 H0 i1 k1 W2 old G2 sc nm t0 H1 hi t1 G3 lo A0 I0 G1 x1 x0 Av2 a1 I1 a0 A1 s1 W3 I2 s0 am1 am0 te em d I3 B1 B0 p1 p0 e B2 lm P0 C0 C1 B3 P1 n0 le D0 D1 Ca3 n1 Da3 Ca2 Da2",
+    "first": "V0 V1 ns B1 ee a o0 am l2 B2 d l3 o1 A2 A0 B0 p lm P0 Av1 B3 P1 q2 C2 o2 oa1 C1 g2 C0 C3 le o3 late n0 q3 n1 D0 D1 oa0 D2 D3",
+    "last": "E0 E1 F0 E2 F1 G0 E3 W0 k0 W1 F2 t0 F3 I1 W3 W2 G2 G1 k1 t1 I0 G3 te I3 y0 I2 y1 u",
+})
+ACCH = [(512 * i, 512 * i + 512) for i in range(4)]
 
 SCRATCH = {
     "M": ("sbuf", [128, W], "bfloat16"), "P": ("sbuf", [128, W], "bfloat16"),
-    "V": ("sbuf", [128, K], "bfloat16"), "m1": ("sbuf", [128, K], "bfloat16"),
-    "mk": ("sbuf", [128, K], "bfloat16"), "m2": ("sbuf", [128, K], "bfloat16"),
-    "col": ("sbuf", [128, K], "bfloat16"), "hit": ("sbuf", [128, K], "bfloat16"),
-    "acm": ("sbuf", [128, K], "float16"), "pg": ("sbuf", [128, K], "bfloat16"),
-    "aco": ("sbuf", [128, K], "int32"),
+    "acm": ("sbuf", [128, K], "float16"), "aco": ("sbuf", [128, K], "int32"),
     "xp": ("sbuf", [128, 2, 16, 16], "int32"), "xpf": ("sbuf", [128, 16, 2, 16], "float32"),
-    "xpt": ("sbuf", [128, 512], "float32"), "pl": ("sbuf", [128, 512], "float32"), "Lt": ("sbuf", [128, 32], "uint16"),
+    "xpt": ("sbuf", [128, 512], "float32"), "Lt": ("sbuf", [128, 32], "uint16"),
     "xm": ("sbuf", [128, 2, 4, 16], "int32"), "xmf": ("sbuf", [128, 4, 2, 16], "float32"), "xmt": ("sbuf", [128, 128], "float32"),
-    "ui": ("sbuf", [128, K], "int32"), "ur": ("sbuf", [128, K], "bfloat16"),
-    "ei": ("sbuf", [128, 128], "int32"),
+    "ui": ("sbuf", [128, CH], "int32"), "ur": ("sbuf", [128, CH], "bfloat16"),
+    "x4": ("sbuf", [128, CH], "bfloat16"), "E4": ("sbuf", [128, CH], "bfloat16"),
+    "ei": ("sbuf", [128, 128], "int32"), "ni": ("sbuf", [128, 128], "int32"),
     "hi": ("sbuf", [128, 512], "bfloat16"), "lo": ("sbuf", [128, 512], "bfloat16"),
-    "ns": ("sbuf", [128, 128], "int32"), "yi": ("sbuf", [128, 128], "int32"),
-    "xg": ("sbuf", [128, 128], "float32"), "xs": ("sbuf", [128, 144], "float32"),
-    "ci": ("sbuf", [128, 4], "int32"), "cj": ("sbuf", [128, 8], "int32"), "cf": ("sbuf", [128, 16], "float32"),
-    "ahi": ("sbuf", [128, 128], "bfloat16"), "alo": ("sbuf", [128, 128], "bfloat16"),
-    "WS": ("sbuf", [128, 144], "bfloat16"), "WZ": ("sbuf", [128, 144], "bfloat16"),
-    "WA": ("sbuf", [128, 144], "float16"), "WY": ("sbuf", [128, 144], "bfloat16"),
-    "RF": ("sbuf", [128, 128], "float32"),
+    "ci": ("sbuf", [128, 4], "int32"), "cj": ("sbuf", [128, 4], "int32"), "cf": ("sbuf", [128, 8], "float32"),
+    "xs": ("sbuf", [128, 256], "bfloat16"), "xg": ("sbuf", [128, 256], "bfloat16"),
+    "J": ("sbuf", [128, 256], "float32"), "BB": ("sbuf", [128, 256], "bfloat16"), "WW": ("sbuf", [128, 256], "bfloat16"),
+    "WZ": ("sbuf", [128, 144], "bfloat16"), "WA": ("sbuf", [128, 144], "float16"), "WY": ("sbuf", [128, 256], "bfloat16"),
+    "cn": ("sbuf", [128, 128], "float32"),
 }
-for _n in ("BO", "BR", "BN", "ZT", "HI", "G8", "za", "zr"):
+for _n in ("V", "m1", "mk", "m2", "col", "hit", "pg"):
+    SCRATCH[_n] = ("sbuf", [128, K], "bfloat16")
+for _n in ("Ib", "B75", "BE", "ZT", "zr", "nok"):
     SCRATCH[_n] = ("sbuf", [128, 128], "bfloat16")
-for _n in ("e", "n1s", "dn", "f0", "f1", "f2", "t1", "t2", "oy", "ou"):
+for _n in ("M16", "D512", "ah"):
+    SCRATCH[_n] = ("sbuf", [128, 128], "float16")
+for _n in ("NI", "z0", "zc", "e", "nsx", "f0", "t1", "t2", "sc", "dd", "oy", "oe", "ou"):
     SCRATCH[_n] = ("sbuf", [128, 128], "float32")
 for _n in ("Lns", "Lp", "Ln1", "Le", "Lin", "Lm"):
     SCRATCH[_n] = ("sbuf", [128, 128], "uint16")
@@ -53,45 +64,70 @@ for _t in range(RO - 1):
 for _t in range(8):
     SCRATCH["B%d" % _t] = ("psum", [128, CH], "float32")
 
-SEMAPHORES = (["cv", "ca", "cp", "cg", "sent", "hsent"] + ["dm%d" % t for t in range(RO)] + ["acs%d" % t for t in range(3)]
-              + ["h%d" % t for t in range(len(ACCH))] + ["d%d" % i for i in range(48)])
+SEMAPHORES = (["cv", "ca", "cp", "cg", "sent", "hsent"] + ["dm%d_%d" % (t, i) for t in range(RO) for i in range(4)]
+              + ["hd%d_%d" % (t, i) for t in range(RO) for i in range(4)] + ["acs%d" % t for t in range(3)] + ["h%d" % t for t in range(len(ACCH))] + ["d%d" % i for i in range(64)])
 
 
-def helper_of(T, topo, r):
+def via(T, topo, r, way):
     c = T.cores[r]
-    for h in topo.cores_of(c):
-        if T.rank_of(h) is None and topo.die(h) != topo.die(c) and all(topo.may_write(h, o) for o in T.cores if o != c):
-            return h
-    raise ValueError("no helper")
+    if way == "d":
+        return c
+    free = [h for h in topo.cores_of(c) if T.rank_of(h) is None and (topo.die(h) == topo.die(c)) == (way == "s")
+            and all(topo.may_write(h, o) for o in T.cores if o != c)]
+    return free[1 if way == "k" else 0]
+
+
+def on_chip(T, topo, r, h):
+    return topo.mask(T.cores[r], h) & ~topo.mask(T.cores[r], T.cores[(r + 1) % N])
+
+
+def ac_way(s, i):
+    return "d" if s == 0 and i in OPT["acdir"] else OPT["acway"][i]
+
+
+LOG = []
+OPS = []
 
 
 def bits(m):
     return bin(m).count("1")
 
 
-def helper_program(g, core, T, topo, r):
-    src = T.cores[r]
-    far = T.cores[(r + 1) % N]
-    m_in = topo.mask(src, core) & ~topo.mask(src, far)
-    total = 0
-    for s in range(3):
+def helper_program(g, core, T, topo, r, way):
+    n_in = bits(on_chip(T, topo, r, core))
+    total = [0]
+    have = []
+
+    def hand(s, arrived, out, in_, sem):
         dst = T.cores[(r - 1 - s) % N]
         rid, pid, _ = topo.addr(dst)
-        m = topo.mask(core, dst)
-        for i, (a, b) in enumerate(ACCH):
-            if s == 0:
-                g.wait_ge(T.sem["h%d" % i], bits(m_in))
-            g.remote_dma(T["acr%d" % s][:, a:b], T.aco[:, a:b], T.sem["acs%d" % s], T.sem.hsent, pid, rid, m)
-            total += bits(m)
-    g.wait_ge(T.sem.hsent, total)
+        if arrived not in have:
+            g.wait_ge(T.sem[arrived], n_in)
+            have.append(arrived)
+        g.remote_dma(out, in_, T.sem[sem], T.sem.hsent, pid, rid, topo.mask(core, dst))
+        total[0] += bits(topo.mask(core, dst))
+
+    for name in OPT["help"].split():
+        t = int(name[-1])
+        if name[0] == "a":
+            for i, (a, b) in enumerate(ACCH):
+                if ac_way(t, i) == way:
+                    hand(t, "h%d" % i, T["acr%d" % t][:, a:b], T.aco[:, a:b], "acs%d" % t)
+        else:
+            for i, (a, b, w) in enumerate(OPT["dm0" if t == 0 else "dm"]):
+                if w == way:
+                    hand(t % 3, "hd%d_%d" % (t, i), T["dmi%d" % t][:, a:b], T["dmo%d" % t][:, a:b], "dm%d_%d" % (t, i))
+    if total[0]:
+        g.wait_ge(T.sem.hsent, total[0])
 
 
 def rank_program(g, core, T, topo):
     r = T.rank_of(core)
     if r is None:
         for q in range(N):
-            if helper_of(T, topo, q) == core:
-                helper_program(g, core, T, topo, q)
+            for way in "hks":
+                if via(T, topo, q, way) == core:
+                    helper_program(g, core, T, topo, q, way)
         return
 
     Q = {"v": g.vector, "a": g.scalar, "p": g.tensor, "s": g.sync, "g": g}
@@ -126,7 +162,11 @@ def rank_program(g, core, T, topo):
                 Q[q].wait_ge(T.sem[s], v)
                 waited[q][s] = v
 
+    cur = [None]
+
     def note(q, reads, writes, tok):
+        if cur[0]:
+            LOG.append(cur[0] + ([rng(x) for x in reads], [rng(x) for x in writes]))
         toks[tok[0]] = max(toks.get(tok[0], 0), tok[1])
         for x in writes:
             n, lo, hi = rng(x)
@@ -138,354 +178,359 @@ def rank_program(g, core, T, topo):
     def op(q, reads, writes, fn):
         sync(q, reads, writes)
         cnt[q] += 1
-        fn().then_inc(T.sem["c" + q], 1)
+        ins = fn()
+        ins.then_inc(T.sem["c" + q], 1)
+        OPS.append((cur[0], q, [ins], [rng(x) for x in reads], [rng(x) for x in writes]))
         note(q, reads, writes, ("c" + q, cnt[q]))
 
     def dma(q, reads, writes, pairs):
         sync(q, reads, writes)
         s = "d%d" % nd[0]
         nd[0] += 1
-        for o, i in pairs:
-            Q[q].dma_start(o, i).then_inc(T.sem[s], 16)
+        ins = [Q[q].dma_start(o, i) for o, i in pairs]
+        for i in ins:
+            i.then_inc(T.sem[s], 16)
+        OPS.append((cur[0], q, ins, [rng(x) for x in reads], [rng(x) for x in writes]))
         note("dma", reads, writes, (s, 16 * len(pairs)))
 
     sent = [0]
 
     def remote(reads, out, in_, sem, dst, m):
         sync("g", reads, [])
+        if cur[0]:
+            LOG.append(cur[0] + ([rng(x) for x in reads], []))
         rid, pid, _ = topo.addr(dst)
-        g.remote_dma(out, in_, T.sem[sem], T.sem.sent, pid, rid, m)
+        ins = g.remote_dma(out, in_, T.sem[sem], T.sem.sent, pid, rid, m)
+        OPS.append((cur[0], "g", [ins], [rng(x) for x in reads], []))
         sent[0] += bits(m)
+
+    def gate(q, reads):
+        sync(q, reads, [])
+        OPS.append((cur[0], q, [], [rng(x) for x in reads], []))
+        if cur[0]:
+            LOG.append(cur[0] + ([rng(x) for x in reads], []))
 
     v, a, pe = g.vector, g.scalar, g.tensor
 
-    def ts(out, in0, s1, s2, o0, o1, reads, writes):
-        if s2 is None:
-            op("v", reads, writes, lambda: v.tensor_scalar(out, in0, s1, None, o0))
+    def ap(x):
+        if isinstance(x, str):
+            return T[x][:]
+        if len(x) == 3:
+            return T[x[0]][:, x[1]:x[2]]
+        return T[x[0]][:, 0:x[1]].indirect(T[x[2]][:, x[3] // 16:x[4] // 16])
+
+    def rd(*xs):
+        out = []
+        for x in xs:
+            if isinstance(x, str) or (isinstance(x, tuple) and len(x) == 3):
+                out.append(x)
+            elif isinstance(x, tuple):
+                out += [(x[0], 0, x[1]), (x[2], x[3] // 16, x[4] // 16)]
+        return out
+
+    def sca(x):
+        return ap(x) if isinstance(x, tuple) else x
+
+    def ts(out, in0, s1, o0, s2=None, o1=None):
+        if o1 is None:
+            op("v", rd(in0, s1), [out], lambda: v.tensor_scalar(ap(out), ap(in0), sca(s1), None, o0))
         else:
-            op("v", reads, writes, lambda: v.tensor_scalar(out, in0, s1, s2, o0, o1))
+            op("v", rd(in0, s1, s2), [out], lambda: v.tensor_scalar(ap(out), ap(in0), sca(s1), sca(s2), o0, o1))
 
-    def tt(out, in0, in1, o, reads, writes):
-        op("v", reads, writes, lambda: v.tensor_tensor(out, in0, in1, o))
+    def tt(out, in0, in1, o):
+        op("v", rd(in0, in1), [out], lambda: v.tensor_tensor(ap(out), ap(in0), ap(in1), o))
 
-    def cp(out, in_, reads, writes):
-        op("v", reads, writes, lambda: v.tensor_copy(out, in_))
+    def cp(out, in_):
+        op("v", rd(in_), [out], lambda: v.tensor_copy(ap(out), ap(in_)))
 
-    def act(out, in_, f, reads, writes, bias=0.0, scale=1.0):
-        op("a", reads, writes, lambda: a.activation(out, in_, f, bias=bias, scale=scale))
+    def act(out, in_, f=AF.Copy, bias=0.0, scale=1.0):
+        op("a", rd(in_, bias, scale), [out], lambda: a.activation(ap(out), ap(in_), f, bias=sca(bias), scale=sca(scale)))
 
-    def gather(q, out, in_, reads, writes):
-        if q == "a":
-            act(out, in_, AF.Copy, reads, writes)
-        else:
-            cp(out, in_, reads, writes)
+    def mm(out, *terms, first=True, final=True):
+        for i, (l, x) in enumerate(terms):
+            op("p", rd(l, x), [out], lambda: pe.matmul(ap(out), ap(l), ap(x), first and i == 0, final and i == len(terms) - 1))
 
-    def mm(out, l, rh, st, sp, reads, writes):
-        op("p", reads, writes, lambda: pe.matmul(out, l, rh, st, sp))
-
-    def ind(win, width, lst, lo, hi):
-        return T[win][:, 0:width].indirect(T[lst][:, lo // 16:hi // 16])
-
-    def L(lst, lo, hi):
-        return (lst, lo // 16, hi // 16)
-
-    def listpass(bank, half, Wn, src, first=True):
-        o = T[bank][:, 64 * half:64 * half + 64]
+    def listpass(out, Wn, at, src, h, first=True):
         for i in range(16):
-            mm(o, T[Wn][:, 15 - i:143 - i], T[src][:, 1024 * half + i:1024 * (half + 1):16], first and i == 0, i == 15,
-               [Wn, (src, 1024 * half, 1024 * (half + 1))], [bank])
+            op("p", [Wn, (src, 1024 * h, 1024 * h + 1024)], [out], lambda: pe.matmul(
+                ap(out), T[Wn][:, at - i:at - i + 128], T[src][:, 1024 * h + i:1024 * h + 1024:16], first and i == 0, i == 15))
 
-    hp = helper_of(T, topo, r)
-    DM = OPT["dm"]
     for t in range(RO):
-        src = T.cores[(r + 1 + t % 3) % N]
-        note("rem", [], ["dmi%d" % t], ("dm%d" % t, len(DM) * bits(topo.mask(src, core))))
+        for i, (lo, hi, w) in enumerate(OPT["dm0" if t == 0 else "dm"]):
+            src = via(T, topo, (r + 1 + t % 3) % N, w)
+            note("rem", [], [("dmi%d" % t, lo, hi)], ("dm%d_%d" % (t, i), bits(topo.mask(src, core))))
     for s in range(3):
-        src = helper_of(T, topo, (r + 1 + s) % N)
-        note("rem", [], ["acr%d" % s], ("acs%d" % s, len(ACCH) * bits(topo.mask(src, core))))
+        note("rem", [], ["acr%d" % s], ("acs%d" % s, sum(
+            bits(topo.mask(via(T, topo, (r + 1 + s) % N, ac_way(s, i)), core)) for i in range(len(ACCH)))))
 
-    def ld_idm(q, c):
-        dma(q, [], [("M", K * c, K * c + K)], [(T.M[:, K * c:K * c + K], T.idm[:, K * c:K * c + K])])
-
-    def ld_ac(i):
+    def ld_ac(q, i):
         lo, hi = ACCH[i]
-        dma("s", [], [("aco", lo, hi)], [(T.aco[:, lo:hi], T.ac[:, lo:hi])])
+        dma(q, [], [("aco", lo, hi)], [(T.aco[:, lo:hi], T.ac[:, lo:hi])])
 
-    AO = OPT["ac"]
-    dma("a", [], ["xp"], [(T.xp[:, j, :, :], T.par[j:8:2, :]) for j in range(2)])
-    dma("s", [], ["ui"], [(T.ui[0:8, :], T.u0[:])])
-    dma("s", [], ["xm"], [(T.xm[:, j, :, :], T.mnt[j:8:2, :]) for j in range(2)])
-    dma("a", [], ["ns"], [(T.ns[:], T.ns0[:])])
-    dma("a", [], ["ei"], [(T.ei[:], T.e0[:])])
-    for i in range(2):
-        if AO[i] == 0:
-            ld_ac(i)
-    ld_idm("a", 2)
-    ld_idm("s", 3)
-    ld_idm("a", 0)
-    ld_idm("s", 1)
-    for i in range(2):
-        if AO[i] == 1:
-            ld_ac(i)
-    op("v", [], [("P", 0, W // 2)], lambda: v.memset(T.P[:, 0:W // 2], 0.0))
-    op("g", [], ["ci"], lambda: g.iota(T.ci[:, 0:3], [[-16, 3]], 144, 1))
-    op("g", [], ["xs"], lambda: g.iota(T.xs[:], [[1, 144]], -15, 0, allow_small_or_imprecise_dtypes=True))
-    op("g", [], ["xg"], lambda: g.iota(T.xg[:], [[16, 8], [0, 16]], 0, 0, allow_small_or_imprecise_dtypes=True))
-    op("g", [], ["ahi"], lambda: g.iota(T.ahi[:], [[32, 128]], 2 * K, 0, allow_small_or_imprecise_dtypes=True))
-    op("g", [], [("P", W // 2, W)], lambda: g.iota(T.P[:, W // 2:W], [[0, W // 2]], 0, 0, allow_small_or_imprecise_dtypes=True))
-    m_on = topo.mask(core, hp) & ~topo.mask(core, T.cores[(r + 1) % N])
+    def ld_old(t):
+        S = BASE + K * (t % 2)
+        if t < 2:
+            dma("s", [], [("win%d" % t, K, 2 * K)], [(T["win%d" % t][:, K:2 * K], T.idm[:, S:S + K])])
+        else:
+            dma("s", [("M", S, S + K)], [("win%d" % t, K, 2 * K)], [(T["win%d" % t][:, K:2 * K], T.M[:, S:S + K])])
+
+    x = W // OPT["idm"]
+    loads = {"par": ("xp", [(T.xp[:, j, :, :], T.par[j:8:2, :]) for j in range(2)]), "u": ("ui", [(T.ui[0:32, :], T.u0[:])]),
+             "mnt": ("xm", [(T.xm[:, j, :, :], T.mnt[j:8:2, :]) for j in range(2)]),
+             "ns": ("ni", [(T.ni[:], T.ns0[:])]), "e": ("ei", [(T.ei[:], T.e0[:])])}
+    for c in range(OPT["idm"]):
+        loads["i%d" % c] = (("M", x * c, x * c + x), [(T.M[:, x * c:x * c + x], T.idm[:, x * c:x * c + x])])
+    for c, (lo, hi) in enumerate(ACCH):
+        loads["c%d" % c] = (("aco", lo, hi), [(T.aco[:, lo:hi], T.ac[:, lo:hi])])
+    for name in OPT["loads"].split():
+        if name[0] == "+":
+            gate("s", [loads[name[1:]][0]])
+        else:
+            dma("s", [], [loads[name][0]], loads[name][1])
+
+    f0, f1, f2 = OPT["fill"]
+    for lo, hi in ((0, f0), (f0, f1)):
+        op("v", [], [("P", lo, hi)], lambda: v.memset(T.P[:, lo:hi], 0.0))
+    for lo in range(f1, f2, f0):
+        act(("P", lo, min(lo + f0, f2)), ("P", 0, min(f0, f2 - lo)))
+    small = dict(allow_small_or_imprecise_dtypes=True)
+    op("g", [], ["ci"], lambda: g.iota(T.ci[:, 0:1], [[0, 1]], 0, 1))
+    op("g", [], ["xs"], lambda: g.iota(T.xs[:], [[0, 2], [1, 128]], 0, 0, **small))
+    op("g", [], ["x4"], lambda: g.iota(T.x4[0:32, :], [[1, 4], [4, 8], [0, 16]], 0, 0, **small))
+    op("g", [], ["xg"], lambda: g.iota(T.xg[:], [[0, 2], [16, 8], [0, 16]], 0, 0, **small))
+    op("g", [], ["z0"], lambda: g.iota(T.z0[:], [[16, 128]], K, 0, **small))
+    if f2 < W:
+        op("g", [], [("P", f2, W)], lambda: g.iota(T.P[:, f2:W], [[0, W - f2]], 0, 0, **small))
 
     def ac_on(i):
         lo, hi = ACCH[i]
-        remote([("aco", lo, hi)], T.aco[:, lo:hi], T.aco[:, lo:hi], "h%d" % i, hp, m_on)
+        hp = via(T, topo, r, OPT["acway"][i])
+        remote([("aco", lo, hi)], T.aco[:, lo:hi], T.aco[:, lo:hi], "h%d" % i, hp, on_chip(T, topo, r, hp))
 
-    for i in range(2):
-        if AO[2 + i] == 0:
-            ac_on(i)
 
-    ts(T.cj[:, 0:3], T.ci[:, 0:3], 127, None, ALU.bitwise_and, None, ["ci"], [("cj", 0, 3)])
-    ts(T.cj[:, 3:6], T.ci[:, 0:3], 112, None, ALU.bitwise_and, None, ["ci"], [("cj", 3, 6)])
-    ts(T.cj[:, 6:7], T.ci[:, 0:1], 15, None, ALU.bitwise_and, None, ["ci"], [("cj", 6, 7)])
-    cp(T.cf[:, 0:7], T.cj[:, 0:7], ["cj"], [("cf", 0, 7)])
-    C = lambda j: T.cf[:, j:j + 1]
-    R = lambda j: ("cf", j, j + 1)
-    xm_ = T.xs[:, 15:143]
-    ts(C(11), C(1), 16.0, None, ALU.mult, None, [R(1)], [R(11)])
-    ts(C(15), C(6), 32.0, None, ALU.mult, None, [R(6)], [R(15)])
-    ts(T.G8[0:8, :], T.xg[0:8, :], T.cf[0:8, 11:12], None, ALU.is_equal, None, ["xg", R(11)], ["G8"])
-    ts(T.Lt[:], T.xs[:, 15:47], C(15), None, ALU.add, None, ["xs", R(15)], ["Lt"])
-
-    def consts_climb():
-        ts(T.RF[:], xm_, C(0), None, ALU.is_equal, None, ["xs", R(0)], ["RF"])
-        ts(T.BO[:], T.xg[:], C(4), None, ALU.is_equal, None, ["xg", R(4)], ["BO"])
-        ts(T.WS[:], T.xs[:], C(4), None, ALU.is_equal, None, ["xs", R(4)], ["WS"])
-        ts(C(7), C(6), 1.0 / 32, 0.75 / 32 - 7.5, ALU.mult, ALU.add, [R(6)], [R(7)])
-        ts(C(13), C(6), -1.0, 240.0 - 0.75, ALU.mult, ALU.add, [R(6)], [R(13)])
-        ts(T.BR[:], T.xg[:], C(3), None, ALU.is_equal, None, ["xg", R(3)], ["BR"])
-        ts(T.BN[:], T.xg[:], C(3), -1.0, ALU.is_equal, ALU.mult, ["xg", R(3)], ["BN"])
-
-    def consts_abroad():
-        ts(C(8), C(6), 1.0 / 32, 0.75 / 32 - 15.0, ALU.mult, ALU.add, [R(6)], [R(8)])
-        ts(C(9), C(6), 2.0, None, ALU.mult, None, [R(6)], [R(9)])
-        ts(C(10), C(6), 0.5, None, ALU.mult, None, [R(6)], [R(10)])
-        ts(C(14), C(6), -1.0, 480.0 - 0.75, ALU.mult, ALU.add, [R(6)], [R(14)])
-        ts(T.WZ[:], T.xs[:], C(5), -4096.0, ALU.is_equal, ALU.mult, ["xs", R(5)], ["WZ"])
-        ts(T.WA[:], T.xs[:], C(5), None, ALU.is_equal, None, ["xs", R(5)], ["WA"])
-        ts(T.za[:], T.xg[:], C(5), None, ALU.is_equal, None, ["xg", R(5)], ["za"])
-        ts(T.zr[:], xm_, C(2), 2.0, ALU.is_equal, ALU.mult, ["xs", R(2)], ["zr"])
-        ts(T.HI[:], xm_, C(1), 0.5, ALU.is_equal, ALU.mult, ["xs", R(1)], ["HI"])
-        ts(T.alo[:], T.xg[:], 0.0, C(9), ALU.mult, ALU.add, ["xg", R(9)], ["alo"])
-        ts(T.WY[:], T.xs[:], C(4), C(10), ALU.is_equal, ALU.mult, ["xs", R(4), R(10)], ["WY"])
-        tt(T.ZT[:], T.zr[:], T.za[:], ALU.subtract, ["zr", "za"], ["ZT"])
+    PP, PG, PI, NPI, P32, NPB, END, EN2 = [("cf", j, j + 1) for j in range(8)]
+    ts(("cj", 0, 1), ("ci", 0, 1), 112, ALU.bitwise_and)
+    ts(("cj", 1, 2), ("ci", 0, 1), 15, ALU.bitwise_and)
+    cp(PP, ("ci", 0, 1))
+    cp(("cf", 1, 3), ("cj", 0, 2))
+    ts(P32, PI, 32.0, ALU.mult)
+    ts(NPI, PI, -1.0, ALU.mult)
+    ts("Lt", ("xs", 0, 32), P32, ALU.add)
+    op("v", ["x4", PP], ["E4"], lambda: v.tensor_scalar(T.E4[0:32, :], T.x4[0:32, :], T.cf[0:32, 0:1], None, ALU.is_equal))
+    I32, RF = ("J", 0, 128), ("J", 112, 240)
+    BO, BR = ("BB", 0, 128), ("BB", 112, 240)
 
     def p_rows():
         dma("s", ["hi", "lo"], ["P"], [(T.P[0:128:16, :], T.hi[:]), (T.P[1:128:16, :], T.lo[:])])
 
     for j in range(2):
-        cp(T.xpf[:, :, j, :], T.xp[:, j, :, :], ["xp"], [("xpf", j, j + 1)])
-    for j in range(2):
-        cp(T.xmf[:, :, j, :], T.xm[:, j, :, :], ["xm"], [("xmf", j, j + 1)])
+        op("v", ["xp"], [("xpf", j, j + 1)], lambda: v.tensor_scalar(T.xpf[:, :, j, :], T.xp[:, j, :, :], -7.5, None, ALU.add))
     op("v", ["xpf"], ["xpt"], lambda: v.transpose(T.xpt[:], T.xpf[:]))
-    op("v", ["xmf"], ["xmt"], lambda: v.transpose(T.xmt[:], T.xmf[:]))
-    cp(T.pl[:], ind("xpt", 512, "Lt", 0, 512), ["xpt", "Lt"], ["pl"])
-    for b in range(4):
-        cp(T.Lm[:, b:128:4], T.xmt[:, 32 * b:32 * b + 32], ["xmt"], [("Lm", b, b + 1)])
-    cp(T.hi[:], T.pl[:], ["pl"], ["hi"])
-    cp(T.B6[:, 256:512], T.pl[:, 256:512], ["pl"], [("B6", 256, 512)])
-    tt(T.lo[:], T.pl[:], T.hi[:], ALU.subtract, ["pl", "hi"], ["lo"])
-    p_rows()
-    for i in range(2):
-        if AO[i] == 2:
-            ld_ac(i)
-    if AO[2] == -1:
-        sync("g", ["lo"], [])
-        ac_on(0)
-    cp(T.ur[0:8, :], T.ui[0:8, :], ["ui"], ["ur"])
+    act("hi", ("xpt", 512, "Lt", 0, 512))
+    op("v", ["ui"], ["ur"], lambda: v.tensor_copy(T.ur[0:32, :], T.ui[0:32, :]))
     for c in range(4):
-        mm(T["B%d" % c][:], T.G8[0:8, :], T.ur[0:8, CH * c:CH * c + CH], True, True, ["G8", "ur"], ["B%d" % c])
-    cp(T.e[:], T.ei[:], ["ei"], ["e"])
-    cp(T.Lns[:], T.ns[:], ["ns"], ["Lns"])
-    consts_climb()
-
-    def conv(q, lo, hi):
-        o, w = T.M[:, lo:hi], ("M", lo, hi)
-        if q == "a":
-            act(o, o, AF.Identity, [w], [w], bias=0.75 / 32, scale=1.0 / 32)
-        else:
-            ts(o, o, 0.75, 1.0 / 32, ALU.add, ALU.mult, [w], [w])
-
-    for c in (2, 3, 0):
-        conv("a", K * c, K * c + K)
-    conv("a", K, K + 640)
-    for c in range(OPT["v0"]):
-        ts(T.V[:, CH * c:CH * c + CH], T["B%d" % c][:], C(6), 0.5, ALU.is_equal, ALU.subtract,
-           ["B%d" % c, R(6)], [("V", CH * c, CH * c + CH)])
-    conv("v", K + 640, 2 * K)
-    for c in range(OPT["v0"], 4):
-        ts(T.V[:, CH * c:CH * c + CH], T["B%d" % c][:], C(6), 0.5, ALU.is_equal, ALU.subtract,
-           ["B%d" % c, R(6)], [("V", CH * c, CH * c + CH)])
-
+        op("p", ["E4", "ur"], ["B%d" % c], lambda: pe.matmul(T["B%d" % c][:], T.E4[0:32, 128 * c:128 * c + 128], T.ur[0:32, :], True, True))
+    for j in range(2):
+        op("v", ["xm"], [("xmf", j, j + 1)], lambda: v.tensor_copy(T.xmf[:, :, j, :], T.xm[:, j, :, :]))
+    tt("lo", ("xpt", 512, "Lt", 0, 512), "hi", ALU.subtract)
+    p_rows()
+    op("v", ["xmf"], ["xmt"], lambda: v.transpose(T.xmt[:], T.xmf[:]))
+    for b in range(4):
+        op("v", ["xmt"], [("Lm", b, b + 1)], lambda: v.tensor_copy(T.Lm[:, b:128:4], T.xmt[:, 32 * b:32 * b + 32]))
+    note("v", [], ["Lm"], ("cv", cnt["v"]))
     chunks = [(CH * c, CH * c + CH) for c in range(4)]
-    z, nok, sc = T.B4[:, 0:128], T.B6[:, 0:128], T.B6[:, 128:256]
-    NOK, SC = ("B6", 0, 128), ("B6", 128, 256)
-    late = []
+    for c in OPT["v0a"]:
+        act(("mk",) + chunks[c], "B%d" % c, AF.Abs, bias=NPI)
+    for c in OPT["v0a"]:
+        act(("V",) + chunks[c], ("mk",) + chunks[c], AF.Sigmoid, bias=128.0, scale=-256.0)
+    ts("J", "xs", PP, ALU.is_equal)
+    ts("BB", "xg", PG, ALU.is_equal)
+    ts("WW", "xs", PG, ALU.is_equal)
+    ts("M16", I32, -16.0, ALU.mult)
+    ts("D512", I32, 1.0 / 512, ALU.mult)
+    ts(NPB, PI, -16384.0, ALU.mult)
+    ts(END, PI, 0.0, ALU.is_equal, 2.0 ** -18, ALU.mult)
+    ts(EN2, PI, 15.0, ALU.is_equal, 2.0 ** -18, ALU.mult)
+    tt(END, END, EN2, ALU.add)
+    act("BE", BR, scale=END)
+    act("B75", BR, scale=0.9375)
+    act("NI", I32, scale=-1.0)
+    act("Ib", I32)
+    act("zr", ("J", 16, 144), scale=2.0)
+    act("WZ", ("WW", 0, 144), scale=-8192.0)
+    act("WY", "WW", scale=PI)
+    for j in range(2):
+        op("v", [], [("cn", 64 * j, 64 * j + 64)], lambda: v.memset(T.cn[:, 64 * j:64 * j + 64], 7.5 - BASE - K * j))
 
-    def vsign(c):
-        lo, hi = chunks[c]
-        act(T.V[:, lo:hi], T["B%d" % c][:], AF.Sign, ["B%d" % c], [("V", lo, hi)])
+    LP, EE, LE, UU = [("B7", 128 * j, 128 * j + 128) for j in range(4)]
+    DD, NP = ("B6", 0, 128), ("B6", 128, 256)
 
-    for t in range(RO):
+    def step(t, name):
         last = t == RO - 1
         S = BASE + K * (t % 2)
-        dmo, dmi, acr = "dmo%d" % t, "dmi%d" % t, "acr%d" % (t % 3)
-        dst = T.cores[(r - 1 - t % 3) % N]
-        for i, (lo, hi, q) in enumerate(DM):
-            gather(q, T[dmo][:, lo:hi], ind("M", W, "Lm", lo, hi), ["M", "Lm"], [(dmo, lo, hi)])
-            remote([(dmo, lo, hi)], T[dmi][:, lo:hi], T[dmo][:, lo:hi], "dm%d" % t, dst, topo.mask(core, dst))
-            if t == 0:
-                for j in range(2):
-                    if AO[j] == 3 + i:
-                        sync("s", [(dmo, lo, hi)], [])
-                        ld_ac(j)
-                for j in range(2):
-                    if AO[2 + j] == i + 1:
-                        ac_on(j)
-        for c in late:
-            vsign(c)
-
-        def op2(c):
-            lo, hi = chunks[c]
-            tt(T.m1[:, lo:hi], ind("M", W, "Lns", lo, hi), T.V[:, lo:hi], ALU.min, ["M", "Lns", ("V", lo, hi)], [("m1", lo, hi)])
-            mm(T["B%d" % c][:], T.BO[:], T.m1[:, lo:hi], True, True, ["BO", ("m1", lo, hi)], ["B%d" % c])
-
-        ts(T.yi[:], T.ns[:], 4, None, ALU.arith_shift_right, None, ["ns"], ["yi"])
-        if t > 0:
-            tt(T.e[:], T.t2[:], T.B5[:, 0:128], ALU.add, ["B5", "t2"], ["e"])
-        ts(sc, T.yi[:], -8191.0 / 512, None, ALU.mult, None, ["yi"], [SC])
-        mm(T.B7[:, 0:128], T.RF[:], T.e[:], True, True, ["RF", "e"], ["B7"])
-        op2(0)
-        tt(T.f1[:], T.ns[:], sc, ALU.add, [SC, "ns"], ["f1"])
-        if not last:
-            oc = 256 + 128 * (t % 2)
-            old, OLD = T.B6[:, oc:oc + 128], ("B6", oc, oc + 128)
-            tt(T.dn[:], old, T.ns[:], ALU.subtract, [OLD, "ns"], ["dn"])
-        ts(T.Lp[:], T.f1[:], 512.0, None, ALU.mult, None, ["f1"], ["Lp"])
-        cp(T.Le[:], T.B7[:, 0:128], ["B7"], ["Le"])
-        op2(1)
-        op2(2)
-        op2(3)
-        for h in range(2):
-            lo, hi = 1024 * h, 1024 * h + 1024
-            act(T.pg[:, lo:hi], ind("P", W, "Lp", lo, hi), AF.Copy, ["P", "Lp"], [("pg", lo, hi)])
-            listpass("B%d" % (4 + h), h, "WS", "pg")
-
-        def n1copy(h):
-            act(T.n1s[:, 64 * h:64 * h + 64], T["B%d" % (4 + h)][:, 64 * h:64 * h + 64], AF.Identity,
-                ["B%d" % (4 + h)], [("n1s", 64 * h, 64 * h + 64)], bias=-float(S))
-
-        if not last:
-            win = "win%d" % t
-            dma("s", [dmi], [(win, 0, K)], [(T[win][0:112, 0:K], T[dmi][16:128, :]), (T[win][112:128, 0:K], T[dmi][0:16, :])])
-            if t < 2:
-                S2, w2 = BASE + K * ((t + 1) % 2), "win%d" % (t + 1)
-                dma("s", [("M", S2, S2 + K)], [(w2, K, 2 * K)], [(T[w2][:, K:2 * K], T.M[:, S2:S2 + K])])
-        n1copy(0)
-        th, ab = (7, 13) if t == 0 else (8, 14)
-        done1 = False
-        op3a = OPT["op3l"] if last else OPT["op3a"]
-        for c, (lo, hi) in enumerate(chunks):
-            if c in op3a:
-                act(T.mk[:, lo:hi], T["B%d" % c][:], AF.Abs, ["B%d" % c, R(ab)], [("mk", lo, hi)], bias=C(ab), scale=32.0)
-                if not done1:
-                    n1copy(1)
-                    done1 = True
+        oc = 256 + 128 * (t % 2)
+        dmo, dmi, acr, win = "dmo%d" % t, "dmi%d" % t, "acr%d" % (t % 3), "win%d" % t
+        k, c = (name[:-1], int(name[-1])) if name[-1].isdigit() else (name, 0)
+        lo, hi = chunks[c]
+        b = "B%d" % c
+        DM = OPT["dm0" if t == 0 else "dm"]
+        h0, h1 = 64 * c, 64 * c + 64
+        n1, z, X = [lambda h, j=j: ("B%d" % (4 + h), 64 * j, 64 * j + 64) for j in range(3)]
+        if k == "A" or k == "Av":
+            lo, hi, w = DM[c]
+            (act if k == "A" else cp)((dmo, lo, hi), ("M", W, "Lm", lo, hi))
+            if w == "d":
+                dst = T.cores[(r - 1 - t % 3) % N]
+                remote([(dmo, lo, hi)], T[dmi][:, lo:hi], T[dmo][:, lo:hi], "dm%d_%d" % (t, c), dst, topo.mask(core, dst))
             else:
-                ts(T.mk[:, lo:hi], T["B%d" % c][:], C(th), None, ALU.is_equal, None, ["B%d" % c, R(th)], [("mk", lo, hi)])
-        if not done1:
-            n1copy(1)
-        for c, (lo, hi) in enumerate(chunks):
-            b = "B%d" % c
-            if c % 2 == 0:
-                h = c // 2
-                ts(T.Ln1[:, 64 * h:64 * h + 64], T.n1s[:, 64 * h:64 * h + 64], float(S), None, ALU.add, None,
-                   [("n1s", 64 * h, 64 * h + 64)], [("Ln1", 64 * h, 64 * h + 64)])
-            far = c in op3a
-            if far:
-                mm(T[b][:], T.BN[:], T.mk[:, lo:hi], True, False, ["BN", ("mk", lo, hi)], [b])
-            tt(T.m2[:, lo:hi], ind("M", W, "Ln1", lo, hi), T.mk[:, lo:hi], ALU.max if far else ALU.mult,
-               ["M", L("Ln1", lo, hi), ("mk", lo, hi)], [("m2", lo, hi)])
-            mm(T[b][:], T.BR[:], T.m2[:, lo:hi], not far, True, ["BR", ("m2", lo, hi)], [b])
-        if t == 0:
-            consts_abroad()
-        if t == 0:
-            cp(T[win][:, K:2 * K], T.M[:, S:S + K], [("M", S, S + K)], [(win, K, 2 * K)])
-        for c, (lo, hi) in enumerate(chunks):
-            if c in OPT["colv"]:
-                ts(T.col[:, lo:hi], ind(dmi, K, "Le", lo, hi), 0.25 / 32, None, ALU.max, None, [dmi, "Le"], [("col", lo, hi)])
+                hp = via(T, topo, r, w)
+                remote([(dmo, lo, hi)], T[dmo][:, lo:hi], T[dmo][:, lo:hi], "hd%d_%d" % (t, c), hp, on_chip(T, topo, r, hp))
+        elif k == "o":
+            ac_on(c)
+        elif k == "q":
+            lo, hi = ACCH[c]
+            dst = T.cores[(r - 1) % N]
+            remote([("aco", lo, hi)], T.acr0[:, lo:hi], T.aco[:, lo:hi], "acs0", dst, topo.mask(core, dst))
+        elif k == "B":
+            tt(("m1", lo, hi), ("M", W, "Lns", lo, hi), ("V", lo, hi), ALU.mult)
+            mm(b, (BO, ("m1", lo, hi)))
+        elif k == "C":
+            ts(("mk", lo, hi), b, PI, ALU.is_equal)
+            mm(b, ("B75", ("mk", lo, hi)), final=False)
+        elif k == "D":
+            tt(("m2", lo, hi), ("M", W, "Ln1", lo, hi), ("mk", lo, hi), ALU.mult)
+            mm(b, (BR, ("m2", lo, hi)), first=False)
+        elif k == "Ca":
+            act(("mk", lo, hi), b, AF.Abs, bias=NPB, scale=16384.0)
+            mm(b, (BR, ("mk", lo, hi)), final=False)
+        elif k == "Da":
+            tt(("m2", lo, hi), ("M", W, "Ln1", lo, hi), ("mk", lo, hi), ALU.subtract)
+            mm(b, (BR, ("m2", lo, hi)), ("BE", ("mk", lo, hi)), first=False)
+        elif k in ("a", "am", "p"):
+            if not name[-1].isdigit():
+                h0, h1 = 0, 128
+            if k == "a":
+                ts(("ah", h0, h1), ("nsx", h0, h1), 1.0 / 16, ALU.mult, 1536.0, ALU.add)
+            elif k == "am":
+                mm(("B7", h0, h1), (I32, ("nsx", h0, h1)), ("M16", ("ah", h0, h1)), ("D512", ("ah", h0, h1)))
             else:
-                act(T.col[:, lo:hi], ind(dmi, K, "Le", lo, hi), AF.Abs, [dmi, "Le"], [("col", lo, hi)])
-
-        def zhalf(h):
-            o = T.B4[:, 64 * h:64 * h + 64]
-            mm(o, T.HI[:], T.ahi[:, 64 * h:64 * h + 64], True, False, ["HI", "ahi"], ["B4"])
-            mm(o, T.HI[:], T.alo[:, 64 * h:64 * h + 64], False, False, ["HI", "alo"], ["B4"])
-            listpass("B4", h, "WZ", "hit", first=False)
-
-        late = [] if last else list(OPT["vlate"])
-        for c, (lo, hi) in enumerate(chunks):
-            b = "B%d" % c
-            tt(T.hit[:, lo:hi], T.col[:, lo:hi], T[b][:], ALU.is_equal, [("col", lo, hi), b], [("hit", lo, hi)])
+                ts(("Lp", h0, h1), ("B7", h0, h1), 24580.5, ALU.add, 512.0, ALU.mult)
+        elif k == "P":
+            mm(n1(c), (I32, ("cn", 64 * (t % 2), 64 * (t % 2) + 64)), final=False)
+            act(("pg", 1024 * c, 1024 * c + 1024), ("P", W, "Lp", 1024 * c, 1024 * c + 1024))
+            listpass(n1(c), "WW", 128, "pg", c, first=False)
+        elif k == "n":
+            ts(("Ln1", h0, h1), n1(c), float(S), ALU.add)
+        elif k == "d":
+            mm(DD, ("Ib", ("hi", oc, oc + 128)), ("Ib", ("lo", oc, oc + 128)), ("NI", "nsx"))
+        elif k == "lm":
+            mm(LE, (RF, "e"))
+        elif k == "le":
+            cp("Le", LE)
+        elif k == "r":
+            lo, hi = OPT["rot"][c]
+            dma("s", [(dmi, lo, hi)], [(win, lo, hi)],
+                [(T[win][0:112, lo:hi], T[dmi][16:128, lo:hi]), (T[win][112:128, lo:hi], T[dmi][0:16, lo:hi])])
+        elif k == "old":
+            ld_old(t)
+        elif k == "oa":
+            act((win, K + 1024 * c, K + 1024 * c + 1024), ("M", S + 1024 * c, S + 1024 * c + 1024))
+        elif k == "ov":
+            cp((win, K + 1024 * c, K + 1024 * c + 1024), ("M", S + 1024 * c, S + 1024 * c + 1024))
+        elif k == "l":
+            ld_ac("s", c)
+        elif k == "g":
+            gate("s", [("dmo0",) + DM[c][:2]])
+        elif k == "ns":
+            cp("Lns", "ni")
+            ts("nsx", "ni", -7.5, ALU.add)
+        elif k == "ee":
+            cp("e", "ei")
+        elif k == "E":
+            act(("col", lo, hi), (dmi, K, "Le", lo, hi), AF.Abs, bias=0.9375)
+        elif k == "F":
             if c % 2 == 1:
-                zhalf(c // 2)
-            mm(T[b][:], T.HI[:], T.V[:, lo:hi], True, False, ["HI", ("V", lo, hi)], [b])
-            mm(T[b][:], T.ZT[:], T.hit[:, lo:hi], False, True, ["ZT", ("hit", lo, hi)], [b])
-            if c not in late:
-                vsign(c)
-
-        def op7(c):
-            lo, hi = chunks[c]
-            tt(T.acm[:, lo:hi], ind(acr, K, "Le", lo, hi), T.hit[:, lo:hi], ALU.mult, [acr, "Le", ("hit", lo, hi)], [("acm", lo, hi)])
+                mm(z(c // 2), (I32, ("zc", 32 * c - 32, 32 * c + 32)), final=False)
+            tt(("hit", lo, hi), ("col", lo, hi), b, ALU.is_equal)
             if c % 2 == 1:
-                listpass("B5", c // 2, "WA", "acm")
-
-        pre = 1 if last else (0 if t == 0 else OPT["pre7"])
-        for c in range(pre):
-            op7(c)
-        if not last:
-            tt(T.f0[:], T.e[:], z, ALU.max, ["e", "B4"], ["f0"])
-        ts(nok, z, 0.0, None, ALU.is_gt, None, ["B4"], [NOK])
-        if not last:
-            cp(T.Lin[:], T.f0[:], ["f0"], ["Lin"])
-            tt(sc, T.dn[:], nok, ALU.mult, ["dn", NOK], [SC])
-            x = K - OPT["insv"]
-            for lo, hi, q in ((0, x // 2, "a"), (x // 2, x, "a"), (x, K, "v")):
-                if hi > lo:
-                    gather(q, T.M[:, S + lo:S + hi], ind(win, 2 * K, "Lin", lo, hi), [win, "Lin"], [("M", S + lo, S + hi)])
-            tt(old, T.ns[:], sc, ALU.add, [SC, "ns"], [OLD])
-            cp(T.hi[:, oc:oc + 128], old, [OLD], [("hi", oc, oc + 128)])
-            tt(T.lo[:, oc:oc + 128], old, T.hi[:, oc:oc + 128], ALU.subtract, [OLD, ("hi", oc, oc + 128)], [("lo", oc, oc + 128)])
+                listpass(z(c // 2), "WZ", 16, "hit", c // 2, first=False)
+        elif k == "W":
+            mm(b, ("Ib", ("V", lo, hi)), ("ZT", ("hit", lo, hi)))
+        elif k == "i":
+            tt(("f0", h0, h1), ("e", h0, h1), z(c), ALU.max)
+            cp(("Lin", h0, h1), ("f0", h0, h1))
+        elif k == "k":
+            act(("nok", h0, h1), z(c), AF.Sigmoid)
+        elif k == "kv":
+            ts(("nok", h0, h1), z(c), 0.0, ALU.is_gt)
+        elif k == "t":
+            tt(("t1", h0, h1), n1(c), ("nok", h0, h1), ALU.mult)
+            mm(X(c), (I32, ("t1", h0, h1)), final=False)
+        elif k == "te":
+            tt("t2", "e", "nok", ALU.mult)
+            if last:
+                tt("dd", "t2", "t1", ALU.subtract)
+        elif k == "sc":
+            tt("sc", DD, "nok", ALU.mult)
+        elif k == "nm":
+            mm(NP, (I32, "nsx"), (I32, "sc"))
+        elif k == "hi":
+            act(("hi", oc, oc + 128), NP)
+        elif k == "lo":
+            tt(("lo", oc, oc + 128), NP, ("hi", oc, oc + 128), ALU.subtract)
             p_rows()
-            op7(pre)
-        else:
-            op7(pre)
+        elif k == "H" or k == "Hv":
+            lo, hi = OPT["ins"][c]
+            (act if k == "H" else cp)(("M", S + lo, S + hi), (win, 2 * K, "Lin", lo, hi))
+        elif k == "I":
+            act(("V", lo, hi), b, AF.Sigmoid, bias=-128.0, scale=256.0)
+        elif k == "Iv":
+            ts(("V", lo, hi), b, 0.5, ALU.is_gt)
+        elif k == "G":
+            tt(("acm", lo, hi), (acr, K, "Le", lo, hi), ("hit", lo, hi), ALU.mult)
+            if c % 2 == 1:
+                listpass(X(c // 2), "WA", 16, "acm", c // 2, first=False)
+        elif k == "s":
+            ts(("Lns", h0, h1), X(c), float(S), ALU.add)
+        elif k == "x":
+            act(("nsx", h0, h1), X(c), AF.Identity, bias=S - 7.5)
+        elif k == "em":
+            mm(EE, (I32, "nsx"), ("NI", "t1"), (I32, "t2"))
+        elif k == "e":
+            act("e", EE, AF.Identity, bias=7.5 - S)
+        elif k == "u":
             for i in range(16):
-                mm(T.B7[:, 0:128], T.WY[:, 15 - i:143 - i], T.V[:, 128 * i:128 * i + 128], i == 0, i == 15,
-                   ["WY", ("V", 128 * i, 128 * i + 128)], ["B7"])
-            act(T.ou[:], T.B7[:, 0:128], AF.Identity, ["B7"], ["ou"], bias=60.0)
+                mm(UU, (("WY", 128 - i, 256 - i), ("V", 128 * i, 128 * i + 128)), first=i == 0, final=i == 15)
+            act("ou", UU)
             dma("a", ["ou"], [], [(T.yu[:], T.ou[:])])
-        for c in range(pre + 1, 4):
-            op7(c)
-        tt(T.f1[:], T.n1s[:], nok, ALU.mult, ["n1s", NOK], ["f1"])
-        tt(T.t2[:], T.e[:], nok, ALU.mult, ["e", NOK], ["t2"])
-        ts(T.t1[:], T.f1[:], float(S), None, ALU.add, None, ["f1"], ["t1"])
-        if not last:
-            tt(T.ns[:], T.t1[:], T.B5[:, 0:128], ALU.add, ["t1", "B5"], ["ns"])
-            cp(T.Lns[:], T.ns[:], ["ns"], ["Lns"])
+        elif k == "y":
+            ts(("oy", h0, h1), X(c), float(S), ALU.add)
+            if c == 1:
+                dma("s", ["oy"], [], [(T.yn[:], T.oy[:])])
+            tt(("oe", h0, h1), X(c), ("dd", h0, h1), ALU.add)
+            if c == 1:
+                dma("a", ["oe"], [], [(T.ye[:], T.oe[:])])
+        elif k == "V":
+            ts(("V", lo, hi), b, PI, ALU.is_equal)
+        elif k == "late":
+            ts("zc", "z0", PI, ALU.add)
+            cp("WA", ("WW", 0, 144))
+            tt("ZT", "zr", ("BB", 16, 144), ALU.subtract)
         else:
-            tt(T.oy[:], T.t1[:], T.B5[:, 0:128], ALU.add, ["t1", "B5"], ["oy"])
-            dma("s", ["oy"], [], [(T.yn[:], T.oy[:])])
-            tt(T.e[:], T.t2[:], T.B5[:, 0:128], ALU.add, ["t2", "B5"], ["e"])
-            dma("a", ["e"], [], [(T.ye[:], T.e[:])])
+            raise ValueError(name)
+
+    for name in OPT["first"].split():
+        cur[0] = (0, "first", name)
+        step(0, name)
+    for t in range(RO):
+        last = t == RO - 1
+        key = "last" if last else "next"
+        for name in OPT[key].split():
+            nxt = name[0] in "ABCDPap" or name in ("n0", "n1", "d", "old")
+            if not (name in ("d", "old") and t + 1 == RO - 1):
+                cur[0] = (t, key, name)
+                step(t + 1 if nxt else t, name)
+    cur[0] = None
 
     g.wait_ge(T.sem.sent, sent[0])
     for s, val in toks.items():

@@ -1,59 +1,46 @@
-from concourse.bass import DstId, RemoteDMATransfer
-from concourse.mybir import dt, AluOpType, AxisListType, ActivationFunctionType
+from concourse.mybir import AluOpType, ActivationFunctionType
 
 ALU = AluOpType
 AF = ActivationFunctionType
 N, W, K, BASE, RO = 4, 8192, 2048, 4096, 4
 CH = 512
-OPT = {
-    "dm": [(0, 768, "h"), (768, 1536, "d"), (1536, 2048, "d")],
-    "dm0": [(0, 768, "h"), (768, 1536, "d"), (1536, 2048, "d")],
-    "rot": [(0, 768), (768, 1536), (1536, 2048)],
-    "acway": "kkkk", "help": "a0 d0 a1 d1 a2 d2 d3", "gate": 99,
-    "fill": (1792, 3584, 7168),
-    "v0a": (2, 3),
-    "acpre": 1,
-    "acdir": (2, 3),
-    "idm": 2, "loads": "par u mnt i0 i1 ns e",
-    "first": "A0 a am V1 A1 B1 B3 V0 lm p o1 le d B0 B2 A2 o3 q2 P0 o2 q3 P1 C0 C1 C2 n0 D0 D1 n1 old late C3 D2 D3",
-    "next": "r0 E2 E0 F0 E1 F1 F2 r1 E3 i0 r2 k0 W0 F3 H0 G0 i1 k1 t0 sc nm t1 H1 hi I0 G1 W1 G2 s0 W2 A0 lo G3 B0 I1 x1 te W3 x0 B1 I2 em A1 s1 I3 a am B2 d A2 C1 p e B3 C0 lm P0 C2 C3 old le n0 P1 D1 D0 n1 D3 D2",
-    "last": "E0 F0 E1 E2 F1 W0 E3 F2 F3 W2 k0 W1 G0 G2 W3 k1 I0 t0 I1 G1 t1 te I2 y0 I3 u G3 y1",
-    "ins": [(0, 1024), (1024, 2048)],
-}
-OPT.update({
-    "dm": [(0, 768, "d"), (768, 1536, "d"), (1536, 2048, "d")], "dm0": [(0, 768, "d"), (768, 1536, "d"), (1536, 2048, "d")],
-    "loads": "par u mnt c0 c1 i0 i1 ns e",
-    "next": "E0 E1 F0 F1 E2 r0 E3 W1 F2 i0 r2 k0 F3 r1 G0 W0 H0 i1 k1 W2 old G2 sc nm t0 H1 hi t1 G3 lo A0 I0 G1 x1 x0 Av2 a1 I1 a0 A1 s1 W3 I2 s0 am1 am0 te em d I3 B1 B0 p1 p0 e B2 lm P0 C0 C1 B3 P1 n0 le D0 D1 Ca3 n1 Da3 Ca2 Da2",
-    "first": "V0 V1 ns B1 ee a o0 am l2 B2 d l3 o1 A2 A0 B0 p lm P0 Av1 B3 P1 q2 C2 o2 oa1 C1 g2 C0 C3 le o3 late n0 q3 n1 D0 D1 oa0 D2 D3",
-    "last": "E0 E1 F0 E2 F1 G0 E3 W0 k0 W1 F2 t0 F3 I1 W3 W2 G2 G1 k1 t1 I0 G3 te I3 y0 I2 y1 u",
-})
+FAR, BIG, UP, OFF = 8192.0, 2.0 ** 40, 2.0 ** 22, 0.75
+TABLE = [(0, 768), (768, 2048)]
+INSTALL = [(0, 1024), (1024, 1792), (1792, 2048)]
 ACCH = [(512 * i, 512 * i + 512) for i in range(4)]
+ACDIR = (2, 3)
+ORDER = {
+    "first": "+par k0 w0 w1 wg6 wv4 w2 +u k2 +mnt k3 +i0 Va3 k1 +i1 w3 k4 wv5 wg7 V1 +c0 o0 V0 +ns A0 V2 ns B3 B0 B2 +e ee A1 xo P0 lm N0 Cv0 k5 +c1 o1 "
+             "B1 op0 P1 st N1 C1 n0 og1 Cv2 og0 +c3 D0 q3 +c2 q2 C3 n1 le k6 D1 o3 o2",
+    "next": "m1 d2 d3 E1 F1 W1 E0 E3 F0 E2 F3 zm0 F2 y0 I1 og1 k7 i0 zm1 i1 zv1 z0 y1 r0 r1 Hv2 Hv1 H0 yb W3 I3 G0 pm np pd W0 W2 A0 G1 em0 G3 e0 G2 m0 "
+            "sm0 s0 I0 A1 og0 em1 B0 e1 lm sm1 B1 s1 I2 P0 le B3 N0 B2 P1 Cv0 N1 n0 D0 C1 C2 st n1 C3 D1 op1",
+    "last": "um E0 d2 d3 E1 E2 F0 m0 E3 F1 G0 y0 zm0 m1 z0 sm0 F2 uo F3 zm1 z1 y1 yb G1 em0 ym yu sd0 sm1 sd1 G2 G3 s0 em1 s1 e0 e1",
+}
 
 SCRATCH = {
     "M": ("sbuf", [128, W], "bfloat16"), "P": ("sbuf", [128, W], "bfloat16"),
     "acm": ("sbuf", [128, K], "float16"), "aco": ("sbuf", [128, K], "int32"),
-    "xp": ("sbuf", [128, 2, 16, 16], "int32"), "xpf": ("sbuf", [128, 16, 2, 16], "float32"),
-    "xpt": ("sbuf", [128, 512], "float32"), "Lt": ("sbuf", [128, 32], "uint16"),
+    "pi": ("sbuf", [128, 512], "int32"),
     "xm": ("sbuf", [128, 2, 4, 16], "int32"), "xmf": ("sbuf", [128, 4, 2, 16], "float32"), "xmt": ("sbuf", [128, 128], "float32"),
-    "ui": ("sbuf", [128, CH], "int32"), "ur": ("sbuf", [128, CH], "bfloat16"),
-    "x4": ("sbuf", [128, CH], "bfloat16"), "E4": ("sbuf", [128, CH], "bfloat16"),
-    "ei": ("sbuf", [128, 128], "int32"), "ni": ("sbuf", [128, 128], "int32"),
-    "hi": ("sbuf", [128, 512], "bfloat16"), "lo": ("sbuf", [128, 512], "bfloat16"),
-    "ci": ("sbuf", [128, 4], "int32"), "cj": ("sbuf", [128, 4], "int32"), "cf": ("sbuf", [128, 8], "float32"),
-    "xs": ("sbuf", [128, 256], "bfloat16"), "xg": ("sbuf", [128, 256], "bfloat16"),
-    "J": ("sbuf", [128, 256], "float32"), "BB": ("sbuf", [128, 256], "bfloat16"), "WW": ("sbuf", [128, 256], "bfloat16"),
-    "WZ": ("sbuf", [128, 144], "bfloat16"), "WA": ("sbuf", [128, 144], "float16"), "WY": ("sbuf", [128, 256], "bfloat16"),
-    "cn": ("sbuf", [128, 128], "float32"),
+    "ui": ("sbuf", [128, CH], "int32"), "ei": ("sbuf", [128, 128], "int32"), "ni": ("sbuf", [128, 128], "int32"),
+    "cj": ("sbuf", [128, 6], "int32"), "cf": ("sbuf", [128, 12], "float32"),
+    "J16": ("sbuf", [128, 256], "float16"), "WA": ("sbuf", [128, 144], "float16"),
 }
 for _n in ("V", "m1", "mk", "m2", "col", "hit", "pg"):
     SCRATCH[_n] = ("sbuf", [128, K], "bfloat16")
-for _n in ("Ib", "B75", "BE", "ZT", "zr", "nok"):
+for _n in ("ur", "x4", "E4", "hi", "lo", "xh"):
+    SCRATCH[_n] = ("sbuf", [128, CH], "bfloat16")
+for _n in ("xs", "xg", "J", "BB", "WW", "nst", "op0", "op1"):
+    SCRATCH[_n] = ("sbuf", [128, 256], "bfloat16")
+for _n in ("WZ0", "WZ1", "WK", "WP", "WU"):
+    SCRATCH[_n] = ("sbuf", [128, 144], "bfloat16")
+for _n in ("ZT", "zr", "NI", "KB", "KN", "I2K", "zl", "zb", "uo"):
     SCRATCH[_n] = ("sbuf", [128, 128], "bfloat16")
-for _n in ("M16", "D512", "ah"):
+for _n in ("NI16", "zc", "e", "f0"):
     SCRATCH[_n] = ("sbuf", [128, 128], "float16")
-for _n in ("NI", "z0", "zc", "e", "nsx", "f0", "t1", "t2", "sc", "dd", "oy", "oe", "ou"):
+for _n in ("z0", "dd", "oy", "oe", "ou"):
     SCRATCH[_n] = ("sbuf", [128, 128], "float32")
-for _n in ("Lns", "Lp", "Ln1", "Le", "Lin", "Lm"):
+for _n in ("Lns", "Ln1", "Le", "Lin", "Lm"):
     SCRATCH[_n] = ("sbuf", [128, 128], "uint16")
 for _t in range(RO):
     SCRATCH["dmo%d" % _t] = ("sbuf", [128, K], "bfloat16")
@@ -65,69 +52,43 @@ for _t in range(8):
     SCRATCH["B%d" % _t] = ("psum", [128, CH], "float32")
 
 SEMAPHORES = (["cv", "ca", "cp", "cg", "sent", "hsent"] + ["dm%d_%d" % (t, i) for t in range(RO) for i in range(4)]
-              + ["hd%d_%d" % (t, i) for t in range(RO) for i in range(4)] + ["acs%d" % t for t in range(3)] + ["h%d" % t for t in range(len(ACCH))] + ["d%d" % i for i in range(64)])
+              + ["acs%d" % t for t in range(N - 1)] + ["h%d" % t for t in range(4)] + ["d%d" % i for i in range(48)])
 
 
-def via(T, topo, r, way):
+def helper(T, topo, r):
     c = T.cores[r]
-    if way == "d":
-        return c
-    free = [h for h in topo.cores_of(c) if T.rank_of(h) is None and (topo.die(h) == topo.die(c)) == (way == "s")
-            and all(topo.may_write(h, o) for o in T.cores if o != c)]
-    return free[1 if way == "k" else 0]
+    return [h for h in topo.cores_of(c) if T.rank_of(h) is None and topo.die(h) != topo.die(c)
+            and all(topo.may_write(h, o) for o in T.cores if o != c)][-1]
 
 
 def on_chip(T, topo, r, h):
     return topo.mask(T.cores[r], h) & ~topo.mask(T.cores[r], T.cores[(r + 1) % N])
 
 
-def ac_way(s, i):
-    return "d" if s == 0 and i in OPT["acdir"] else OPT["acway"][i]
-
-
-LOG = []
-OPS = []
-
-
 def bits(m):
     return bin(m).count("1")
 
 
-def helper_program(g, core, T, topo, r, way):
-    n_in = bits(on_chip(T, topo, r, core))
-    total = [0]
-    have = []
-
-    def hand(s, arrived, out, in_, sem):
+def helper_program(g, core, T, topo, r):
+    total = 0
+    for s in range(N - 1):
         dst = T.cores[(r - 1 - s) % N]
         rid, pid, _ = topo.addr(dst)
-        if arrived not in have:
-            g.wait_ge(T.sem[arrived], n_in)
-            have.append(arrived)
-        g.remote_dma(out, in_, T.sem[sem], T.sem.hsent, pid, rid, topo.mask(core, dst))
-        total[0] += bits(topo.mask(core, dst))
-
-    for name in OPT["help"].split():
-        t = int(name[-1])
-        if name[0] == "a":
-            for i, (a, b) in enumerate(ACCH):
-                if ac_way(t, i) == way:
-                    hand(t, "h%d" % i, T["acr%d" % t][:, a:b], T.aco[:, a:b], "acs%d" % t)
-        else:
-            for i, (a, b, w) in enumerate(OPT["dm0" if t == 0 else "dm"]):
-                if w == way:
-                    hand(t % 3, "hd%d_%d" % (t, i), T["dmi%d" % t][:, a:b], T["dmo%d" % t][:, a:b], "dm%d_%d" % (t, i))
-    if total[0]:
-        g.wait_ge(T.sem.hsent, total[0])
+        for i, (a, b) in enumerate(ACCH):
+            if s == (1 if i in ACDIR else 0):
+                g.wait_ge(T.sem["h%d" % i], bits(on_chip(T, topo, r, core)))
+            if s or i not in ACDIR:
+                g.remote_dma(T["acr%d" % s][:, a:b], T.aco[:, a:b], T.sem["acs%d" % s], T.sem.hsent, pid, rid, topo.mask(core, dst))
+                total += bits(topo.mask(core, dst))
+    g.wait_ge(T.sem.hsent, total)
 
 
 def rank_program(g, core, T, topo):
     r = T.rank_of(core)
     if r is None:
         for q in range(N):
-            for way in "hks":
-                if via(T, topo, q, way) == core:
-                    helper_program(g, core, T, topo, q, way)
+            if helper(T, topo, q) == core:
+                helper_program(g, core, T, topo, q)
         return
 
     Q = {"v": g.vector, "a": g.scalar, "p": g.tensor, "s": g.sync, "g": g}
@@ -138,9 +99,7 @@ def rank_program(g, core, T, topo):
     nd = [0]
 
     def rng(x):
-        if isinstance(x, str):
-            return (x, 0, 1 << 30)
-        return x
+        return (x, 0, 1 << 30) if isinstance(x, str) else x
 
     def sync(q, reads, writes):
         need = {}
@@ -162,11 +121,7 @@ def rank_program(g, core, T, topo):
                 Q[q].wait_ge(T.sem[s], v)
                 waited[q][s] = v
 
-    cur = [None]
-
     def note(q, reads, writes, tok):
-        if cur[0]:
-            LOG.append(cur[0] + ([rng(x) for x in reads], [rng(x) for x in writes]))
         toks[tok[0]] = max(toks.get(tok[0], 0), tok[1])
         for x in writes:
             n, lo, hi = rng(x)
@@ -178,37 +133,24 @@ def rank_program(g, core, T, topo):
     def op(q, reads, writes, fn):
         sync(q, reads, writes)
         cnt[q] += 1
-        ins = fn()
-        ins.then_inc(T.sem["c" + q], 1)
-        OPS.append((cur[0], q, [ins], [rng(x) for x in reads], [rng(x) for x in writes]))
+        fn().then_inc(T.sem["c" + q], 1)
         note(q, reads, writes, ("c" + q, cnt[q]))
 
     def dma(q, reads, writes, pairs):
         sync(q, reads, writes)
         s = "d%d" % nd[0]
         nd[0] += 1
-        ins = [Q[q].dma_start(o, i) for o, i in pairs]
-        for i in ins:
-            i.then_inc(T.sem[s], 16)
-        OPS.append((cur[0], q, ins, [rng(x) for x in reads], [rng(x) for x in writes]))
+        for o, i in pairs:
+            Q[q].dma_start(o, i).then_inc(T.sem[s], 16)
         note("dma", reads, writes, (s, 16 * len(pairs)))
 
     sent = [0]
 
     def remote(reads, out, in_, sem, dst, m):
         sync("g", reads, [])
-        if cur[0]:
-            LOG.append(cur[0] + ([rng(x) for x in reads], []))
         rid, pid, _ = topo.addr(dst)
-        ins = g.remote_dma(out, in_, T.sem[sem], T.sem.sent, pid, rid, m)
-        OPS.append((cur[0], "g", [ins], [rng(x) for x in reads], []))
+        g.remote_dma(out, in_, T.sem[sem], T.sem.sent, pid, rid, m)
         sent[0] += bits(m)
-
-    def gate(q, reads):
-        sync(q, reads, [])
-        OPS.append((cur[0], q, [], [rng(x) for x in reads], []))
-        if cur[0]:
-            LOG.append(cur[0] + ([rng(x) for x in reads], []))
 
     v, a, pe = g.vector, g.scalar, g.tensor
 
@@ -250,287 +192,253 @@ def rank_program(g, core, T, topo):
         for i, (l, x) in enumerate(terms):
             op("p", rd(l, x), [out], lambda: pe.matmul(ap(out), ap(l), ap(x), first and i == 0, final and i == len(terms) - 1))
 
-    def listpass(out, Wn, at, src, h, first=True):
+    def listpass(out, Wn, src, h, first=True, final=True):
         for i in range(16):
             op("p", [Wn, (src, 1024 * h, 1024 * h + 1024)], [out], lambda: pe.matmul(
-                ap(out), T[Wn][:, at - i:at - i + 128], T[src][:, 1024 * h + i:1024 * h + 1024:16], first and i == 0, i == 15))
+                ap(out), T[Wn][:, 16 - i:144 - i], T[src][:, 1024 * h + i:1024 * h + 1024:16], first and i == 0, final and i == 15))
+
+    def blockpass(out, Wn, src, rows=range(16)):
+        mm(out, *[((Wn, 16 - i, 144 - i), (src, 128 * i, 128 * i + 128)) for i in rows], first=0 in rows, final=15 in rows)
 
     for t in range(RO):
-        for i, (lo, hi, w) in enumerate(OPT["dm0" if t == 0 else "dm"]):
-            src = via(T, topo, (r + 1 + t % 3) % N, w)
-            note("rem", [], [("dmi%d" % t, lo, hi)], ("dm%d_%d" % (t, i), bits(topo.mask(src, core))))
-    for s in range(3):
+        for i, (lo, hi) in enumerate(TABLE):
+            note("rem", [], [("dmi%d" % t, lo, hi)], ("dm%d_%d" % (t, i), bits(topo.mask(T.cores[(r + 1 + t % 3) % N], core))))
+    for s in range(N - 1):
+        q = (r + 1 + s) % N
         note("rem", [], ["acr%d" % s], ("acs%d" % s, sum(
-            bits(topo.mask(via(T, topo, (r + 1 + s) % N, ac_way(s, i)), core)) for i in range(len(ACCH)))))
+            bits(topo.mask(T.cores[q] if s == 0 and i in ACDIR else helper(T, topo, q), core)) for i in range(len(ACCH)))))
 
-    def ld_ac(q, i):
-        lo, hi = ACCH[i]
-        dma(q, [], [("aco", lo, hi)], [(T.aco[:, lo:hi], T.ac[:, lo:hi])])
-
-    def ld_old(t):
-        S = BASE + K * (t % 2)
-        if t < 2:
-            dma("s", [], [("win%d" % t, K, 2 * K)], [(T["win%d" % t][:, K:2 * K], T.idm[:, S:S + K])])
-        else:
-            dma("s", [("M", S, S + K)], [("win%d" % t, K, 2 * K)], [(T["win%d" % t][:, K:2 * K], T.M[:, S:S + K])])
-
-    x = W // OPT["idm"]
-    loads = {"par": ("xp", [(T.xp[:, j, :, :], T.par[j:8:2, :]) for j in range(2)]), "u": ("ui", [(T.ui[0:32, :], T.u0[:])]),
+    loads = {"par": ("pi", [(T.pi[:], T.par[:])]), "u": ("ui", [(T.ui[0:32, :], T.u0[:])]),
              "mnt": ("xm", [(T.xm[:, j, :, :], T.mnt[j:8:2, :]) for j in range(2)]),
              "ns": ("ni", [(T.ni[:], T.ns0[:])]), "e": ("ei", [(T.ei[:], T.e0[:])])}
-    for c in range(OPT["idm"]):
-        loads["i%d" % c] = (("M", x * c, x * c + x), [(T.M[:, x * c:x * c + x], T.idm[:, x * c:x * c + x])])
+    for c in range(2):
+        loads["i%d" % c] = (("M", BASE * c, BASE * c + BASE), [(T.M[:, BASE * c:BASE * c + BASE], T.idm[:, BASE * c:BASE * c + BASE])])
     for c, (lo, hi) in enumerate(ACCH):
         loads["c%d" % c] = (("aco", lo, hi), [(T.aco[:, lo:hi], T.ac[:, lo:hi])])
-    for name in OPT["loads"].split():
-        if name[0] == "+":
-            gate("s", [loads[name[1:]][0]])
-        else:
-            dma("s", [], [loads[name][0]], loads[name][1])
 
-    f0, f1, f2 = OPT["fill"]
-    for lo, hi in ((0, f0), (f0, f1)):
-        op("v", [], [("P", lo, hi)], lambda: v.memset(T.P[:, lo:hi], 0.0))
-    for lo in range(f1, f2, f0):
-        act(("P", lo, min(lo + f0, f2)), ("P", 0, min(f0, f2 - lo)))
     small = dict(allow_small_or_imprecise_dtypes=True)
-    op("g", [], ["ci"], lambda: g.iota(T.ci[:, 0:1], [[0, 1]], 0, 1))
+
+    def count_p(lo, hi):
+        op("g", [], [("P", lo, hi)], lambda: g.iota(T.P[:, lo:hi], [[0, (hi - lo) // 128], [1, 128]], 0, 0, **small))
+
+    op("g", [], [("cj", 0, 2)], lambda: g.iota(T.cj[:, 0:2], [[1, 2]], 0, 1))
+    count_p(0, 256)
     op("g", [], ["xs"], lambda: g.iota(T.xs[:], [[0, 2], [1, 128]], 0, 0, **small))
     op("g", [], ["x4"], lambda: g.iota(T.x4[0:32, :], [[1, 4], [4, 8], [0, 16]], 0, 0, **small))
+    op("g", [], ["xh"], lambda: g.iota(T.xh[:], [[128, 4], [0, 128]], 0, 0, **small))
     op("g", [], ["xg"], lambda: g.iota(T.xg[:], [[0, 2], [16, 8], [0, 16]], 0, 0, **small))
-    op("g", [], ["z0"], lambda: g.iota(T.z0[:], [[16, 128]], K, 0, **small))
-    if f2 < W:
-        op("g", [], [("P", f2, W)], lambda: g.iota(T.P[:, f2:W], [[0, W - f2]], 0, 0, **small))
+    op("g", [], ["z0"], lambda: g.iota(T.z0[:], [[16, 128]], -K, 0, **small))
 
-    def ac_on(i):
-        lo, hi = ACCH[i]
-        hp = via(T, topo, r, OPT["acway"][i])
-        remote([("aco", lo, hi)], T.aco[:, lo:hi], T.aco[:, lo:hi], "h%d" % i, hp, on_chip(T, topo, r, hp))
-
-
-    PP, PG, PI, NPI, P32, NPB, END, EN2 = [("cf", j, j + 1) for j in range(8)]
-    ts(("cj", 0, 1), ("ci", 0, 1), 112, ALU.bitwise_and)
-    ts(("cj", 1, 2), ("ci", 0, 1), 15, ALU.bitwise_and)
-    cp(PP, ("ci", 0, 1))
-    cp(("cf", 1, 3), ("cj", 0, 2))
-    ts(P32, PI, 32.0, ALU.mult)
-    ts(NPI, PI, -1.0, ALU.mult)
-    ts("Lt", ("xs", 0, 32), P32, ALU.add)
-    op("v", ["x4", PP], ["E4"], lambda: v.tensor_scalar(T.E4[0:32, :], T.x4[0:32, :], T.cf[0:32, 0:1], None, ALU.is_equal))
-    I32, RF = ("J", 0, 128), ("J", 112, 240)
-    BO, BR = ("BB", 0, 128), ("BB", 112, 240)
-
-    def p_rows():
-        dma("s", ["hi", "lo"], ["P"], [(T.P[0:128:16, :], T.hi[:]), (T.P[1:128:16, :], T.lo[:])])
-
-    for j in range(2):
-        op("v", ["xp"], [("xpf", j, j + 1)], lambda: v.tensor_scalar(T.xpf[:, :, j, :], T.xp[:, j, :, :], -7.5, None, ALU.add))
-    op("v", ["xpf"], ["xpt"], lambda: v.transpose(T.xpt[:], T.xpf[:]))
-    act("hi", ("xpt", 512, "Lt", 0, 512))
-    op("v", ["ui"], ["ur"], lambda: v.tensor_copy(T.ur[0:32, :], T.ui[0:32, :]))
-    for c in range(4):
-        op("p", ["E4", "ur"], ["B%d" % c], lambda: pe.matmul(T["B%d" % c][:], T.E4[0:32, 128 * c:128 * c + 128], T.ur[0:32, :], True, True))
-    for j in range(2):
-        op("v", ["xm"], [("xmf", j, j + 1)], lambda: v.tensor_copy(T.xmf[:, :, j, :], T.xm[:, j, :, :]))
-    tt("lo", ("xpt", 512, "Lt", 0, 512), "hi", ALU.subtract)
-    p_rows()
-    op("v", ["xmf"], ["xmt"], lambda: v.transpose(T.xmt[:], T.xmf[:]))
-    for b in range(4):
-        op("v", ["xmt"], [("Lm", b, b + 1)], lambda: v.tensor_copy(T.Lm[:, b:128:4], T.xmt[:, 32 * b:32 * b + 32]))
-    note("v", [], ["Lm"], ("cv", cnt["v"]))
+    PP, _, PG, PI, OD, SG, SP, SC, SK, BC, NPI, P5 = [("cf", j, j + 1) for j in range(12)]
     chunks = [(CH * c, CH * c + CH) for c in range(4)]
-    for c in OPT["v0a"]:
-        act(("mk",) + chunks[c], "B%d" % c, AF.Abs, bias=NPI)
-    for c in OPT["v0a"]:
-        act(("V",) + chunks[c], ("mk",) + chunks[c], AF.Sigmoid, bias=128.0, scale=-256.0)
-    ts("J", "xs", PP, ALU.is_equal)
-    ts("BB", "xg", PG, ALU.is_equal)
-    ts("WW", "xs", PG, ALU.is_equal)
-    ts("M16", I32, -16.0, ALU.mult)
-    ts("D512", I32, 1.0 / 512, ALU.mult)
-    ts(NPB, PI, -16384.0, ALU.mult)
-    ts(END, PI, 0.0, ALU.is_equal, 2.0 ** -18, ALU.mult)
-    ts(EN2, PI, 15.0, ALU.is_equal, 2.0 ** -18, ALU.mult)
-    tt(END, END, EN2, ALU.add)
-    act("BE", BR, scale=END)
-    act("B75", BR, scale=0.9375)
-    act("NI", I32, scale=-1.0)
-    act("Ib", I32)
-    act("zr", ("J", 16, 144), scale=2.0)
-    act("WZ", ("WW", 0, 144), scale=-8192.0)
-    act("WY", "WW", scale=PI)
-    for j in range(2):
-        op("v", [], [("cn", 64 * j, 64 * j + 64)], lambda: v.memset(T.cn[:, 64 * j:64 * j + 64], 7.5 - BASE - K * j))
+    Ib, I16, RF = ("J", 0, 128), ("J16", 0, 128), ("J16", 112, 240)
+    BO, BR = ("BB", 0, 128), ("BB", 112, 240)
+    HERE, BACK = ("WW", 112, 256), ("WW", 0, 144)
 
-    LP, EE, LE, UU = [("B7", 128 * j, 128 * j + 128) for j in range(4)]
-    DD, NP = ("B6", 0, 128), ("B6", 128, 256)
+    def prepare(c):
+        if c == 0:
+            for j, src, m in ((2, 0, 112), (3, 0, 15), (4, 0, 1), (5, 1, 2)):
+                ts(("cj", j, j + 1), ("cj", src, src + 1), m, ALU.bitwise_and)
+            cp(("cf", 0, 6), "cj")
+            ts(P5, PI, 512.0, ALU.mult)
+            ts(NPI, PI, -1.0, ALU.mult)
+        elif c == 1:
+            cp("hi", "pi")
+            tt("lo", "pi", "hi", ALU.subtract)
+            ts("xh", "xh", P5, ALU.add)
+        elif c == 2:
+            op("v", ["x4", PP], ["E4"], lambda: v.tensor_scalar(T.E4[0:32, :], T.x4[0:32, :], T.cf[0:32, 0:1], None, ALU.is_equal))
+            op("v", ["ui"], ["ur"], lambda: v.tensor_copy(T.ur[0:32, :], T.ui[0:32, :]))
+            for j in range(4):
+                op("p", ["E4", "ur"], ["B%d" % j], lambda: pe.matmul(T["B%d" % j][:], T.E4[0:32, 128 * j:128 * j + 128], T.ur[0:32, :], True, True))
+        elif c == 3:
+            for j in range(2):
+                op("v", ["xm"], [("xmf", j, j + 1)], lambda: v.tensor_copy(T.xmf[:, :, j, :], T.xm[:, j, :, :]))
+            op("v", ["xmf"], ["xmt"], lambda: v.transpose(T.xmt[:], T.xmf[:]))
+            for j in range(4):
+                op("v", ["xmt"], [("Lm", j, j + 1)], lambda: v.tensor_copy(T.Lm[:, j:128:4], T.xmt[:, 32 * j:32 * j + 32]))
+            note("v", [], ["Lm"], ("cv", cnt["v"]))
+        elif c == 4:
+            ts("BB", "xg", PG, ALU.is_equal)
+            ts("WW", "xs", PG, ALU.is_equal)
+            ts("J16", "xs", PP, ALU.is_equal)
+            ts(SP, PI, 4.0, ALU.is_lt, OD, ALU.mult)
+            ts(SC, SG, -FAR, ALU.mult, FAR, ALU.add)
+            ts(BC, NPI, SC, ALU.mult, -OFF, ALU.add)
+            act("WP", HERE, scale=SP)
+        elif c == 5:
+            ts("J", "xs", PP, ALU.is_equal)
+            ts("zc", "z0", PI, ALU.add)
+            ts("NI16", I16, -1.0, ALU.mult)
+            cp("WA", BACK)
+            ts("zr", ("J", 16, 144), 2.0, ALU.mult)
+            tt("ZT", "zr", ("BB", 16, 144), ALU.subtract)
+        elif c == 6:
+            act("WZ0", BACK, scale=BASE // K * UP)
+            for name, scale in (("KB", BIG), ("KN", -BIG), ("NI", -1.0), ("I2K", float(K))):
+                act(name, Ib, scale=scale)
+        else:
+            ts(SK, PI, 1.0, ALU.add)
+            act("WZ1", BACK, scale=(BASE // K + 1) * UP)
+            act("WK", BACK, scale=SK)
+            act("WU", HERE, scale=SK)
 
     def step(t, name):
         last = t == RO - 1
         S = BASE + K * (t % 2)
-        oc = 256 + 128 * (t % 2)
-        dmo, dmi, acr, win = "dmo%d" % t, "dmi%d" % t, "acr%d" % (t % 3), "win%d" % t
+        dmo, dmi, acr, win, opt = "dmo%d" % t, "dmi%d" % t, "acr%d" % (t % 3), "win%d" % t, "op%d" % (t % 2)
+        if name[0] == "+":
+            return dma("s", [], [loads[name[1:]][0]], loads[name[1:]][1])
         k, c = (name[:-1], int(name[-1])) if name[-1].isdigit() else (name, 0)
+        if k == "k":
+            return prepare(c)
+        if k == "wg":
+            return count_p(1024 * c, 1024 * c + 1024)
+        if k == "w" or k == "wv":
+            for lo, hi in ((1024 * c, 1024 * c + 1024),) if c else ((256, 512), (512, 1024)):
+                (act if k == "w" else cp)(("P", lo, hi), ("P", 0, hi - lo))
+            return
         lo, hi = chunks[c]
         b = "B%d" % c
-        DM = OPT["dm0" if t == 0 else "dm"]
+        x0, x1 = 1024 * c, 1024 * c + 1024
         h0, h1 = 64 * c, 64 * c + 64
-        n1, z, X = [lambda h, j=j: ("B%d" % (4 + h), 64 * j, 64 * j + 64) for j in range(3)]
+        n1 = ("B%d" % (4 + c), 0, 64)
+        z, ee = ("B%d" % (6 + c), 0, 64), ("B%d" % (6 + c), 64, 128)
+        ZB, UO, LE, NP = ("B0", 0, 128), ("B6", 128, 256), ("B6", 256, 384), ("B7", 128, 384)
+        WZ = "WZ%d" % (t % 2)
+        gone = [("KB", ("zl", h0, h1)), ("KN", ("zl", h0, h1))]
+        goneb = [("KB", "zb"), ("KN", "zb")]
         if k == "A" or k == "Av":
-            lo, hi, w = DM[c]
+            lo, hi = TABLE[c]
             (act if k == "A" else cp)((dmo, lo, hi), ("M", W, "Lm", lo, hi))
-            if w == "d":
-                dst = T.cores[(r - 1 - t % 3) % N]
-                remote([(dmo, lo, hi)], T[dmi][:, lo:hi], T[dmo][:, lo:hi], "dm%d_%d" % (t, c), dst, topo.mask(core, dst))
-            else:
-                hp = via(T, topo, r, w)
-                remote([(dmo, lo, hi)], T[dmo][:, lo:hi], T[dmo][:, lo:hi], "hd%d_%d" % (t, c), hp, on_chip(T, topo, r, hp))
+            dst = T.cores[(r - 1 - t % 3) % N]
+            remote([(dmo, lo, hi)], T[dmi][:, lo:hi], T[dmo][:, lo:hi], "dm%d_%d" % (t, c), dst, topo.mask(core, dst))
         elif k == "o":
-            ac_on(c)
+            lo, hi = ACCH[c]
+            hp = helper(T, topo, r)
+            remote([("aco", lo, hi)], T.aco[:, lo:hi], T.aco[:, lo:hi], "h%d" % c, hp, on_chip(T, topo, r, hp))
         elif k == "q":
             lo, hi = ACCH[c]
             dst = T.cores[(r - 1) % N]
             remote([("aco", lo, hi)], T.acr0[:, lo:hi], T.aco[:, lo:hi], "acs0", dst, topo.mask(core, dst))
+        elif k == "xo":
+            dma("s", ["hi", "lo", "xh"], ["P"], [(T.P[j:128:16, :], T[src][:]) for j, src in ((1, "hi"), (3, "lo"), (5, "xh"))])
+        elif k == "op":
+            at = BASE + K * c
+            dma("s", [("P", at, at + K)], ["op%d" % c], [(T["op%d" % c][:, 128 * d:128 * d + 128], T.P[1 + 2 * d:128:16, at:at + K]) for d in range(2)])
+        elif k == "ns":
+            cp("Lns", "ni")
+        elif k == "ee":
+            cp("e", "ei")
+        elif k == "V":
+            ts(("V", lo, hi), b, PI, ALU.is_equal)
+        elif k == "Va":
+            act(("mk", lo, hi), b, AF.Abs, bias=NPI)
+            act(("V", lo, hi), ("mk", lo, hi), AF.Sigmoid, bias=128.0, scale=-256.0)
         elif k == "B":
             tt(("m1", lo, hi), ("M", W, "Lns", lo, hi), ("V", lo, hi), ALU.mult)
             mm(b, (BO, ("m1", lo, hi)))
-        elif k == "C":
-            ts(("mk", lo, hi), b, PI, ALU.is_equal)
-            mm(b, ("B75", ("mk", lo, hi)), final=False)
-        elif k == "D":
-            tt(("m2", lo, hi), ("M", W, "Ln1", lo, hi), ("mk", lo, hi), ALU.mult)
-            mm(b, (BR, ("m2", lo, hi)), first=False)
-        elif k == "Ca":
-            act(("mk", lo, hi), b, AF.Abs, bias=NPB, scale=16384.0)
-            mm(b, (BR, ("mk", lo, hi)), final=False)
-        elif k == "Da":
-            tt(("m2", lo, hi), ("M", W, "Ln1", lo, hi), ("mk", lo, hi), ALU.subtract)
-            mm(b, (BR, ("m2", lo, hi)), ("BE", ("mk", lo, hi)), first=False)
-        elif k in ("a", "am", "p"):
-            if not name[-1].isdigit():
-                h0, h1 = 0, 128
-            if k == "a":
-                ts(("ah", h0, h1), ("nsx", h0, h1), 1.0 / 16, ALU.mult, 1536.0, ALU.add)
-            elif k == "am":
-                mm(("B7", h0, h1), (I32, ("nsx", h0, h1)), ("M16", ("ah", h0, h1)), ("D512", ("ah", h0, h1)))
-            else:
-                ts(("Lp", h0, h1), ("B7", h0, h1), 24580.5, ALU.add, 512.0, ALU.mult)
         elif k == "P":
-            mm(n1(c), (I32, ("cn", 64 * (t % 2), 64 * (t % 2) + 64)), final=False)
-            act(("pg", 1024 * c, 1024 * c + 1024), ("P", W, "Lp", 1024 * c, 1024 * c + 1024))
-            listpass(n1(c), "WW", 128, "pg", c, first=False)
+            act(("pg", x0, x1), ("P", W, "Lns", x0, x1))
+        elif k == "N" or k == "m":
+            listpass(n1, "WP", "pg", c, final=k == "N")
         elif k == "n":
-            ts(("Ln1", h0, h1), n1(c), float(S), ALU.add)
-        elif k == "d":
-            mm(DD, ("Ib", ("hi", oc, oc + 128)), ("Ib", ("lo", oc, oc + 128)), ("NI", "nsx"))
+            cp(("Ln1", h0, h1), n1)
+        elif k == "st":
+            dma("s", ["pg"], ["nst"], [(T.nst[:, 128 * d:128 * d + 128], T.pg[5 + 2 * d:128:16, :]) for d in range(2)])
+        elif k == "C":
+            act(("mk", lo, hi), b, AF.Identity, bias=BC, scale=SC)
+        elif k == "Cv":
+            ts(("mk", lo, hi), b, SC, ALU.mult, BC, ALU.add)
+        elif k == "D" or k == "d":
+            tt(("m2", lo, hi), ("M", W, "Ln1", lo, hi), ("mk", lo, hi), ALU.subtract)
+            mm(b, (BR, ("m2", lo, hi)))
         elif k == "lm":
             mm(LE, (RF, "e"))
         elif k == "le":
             cp("Le", LE)
         elif k == "r":
-            lo, hi = OPT["rot"][c]
-            dma("s", [(dmi, lo, hi)], [(win, lo, hi)],
-                [(T[win][0:112, lo:hi], T[dmi][16:128, lo:hi]), (T[win][112:128, lo:hi], T[dmi][0:16, lo:hi])])
-        elif k == "old":
-            ld_old(t)
-        elif k == "oa":
-            act((win, K + 1024 * c, K + 1024 * c + 1024), ("M", S + 1024 * c, S + 1024 * c + 1024))
-        elif k == "ov":
-            cp((win, K + 1024 * c, K + 1024 * c + 1024), ("M", S + 1024 * c, S + 1024 * c + 1024))
-        elif k == "l":
-            ld_ac("s", c)
-        elif k == "g":
-            gate("s", [("dmo0",) + DM[c][:2]])
-        elif k == "ns":
-            cp("Lns", "ni")
-            ts("nsx", "ni", -7.5, ALU.add)
-        elif k == "ee":
-            cp("e", "ei")
+            lo, hi = TABLE[c]
+            dma("s", [(dmi, lo, hi)], [(win, K + lo, K + hi)],
+                [(T[win][0:112, K + lo:K + hi], T[dmi][16:128, lo:hi]), (T[win][112:128, K + lo:K + hi], T[dmi][0:16, lo:hi])])
+        elif k == "og":
+            op("g", [("M", S + x0, S + x1)], [(win, x0, x1)],
+               lambda: g.affine_select(T[win][:, x0:x1], T.M[:, S + x0:S + x1], [[0, x1 - x0]], ALU.is_ge, 0.0, 0, 0))
         elif k == "E":
-            act(("col", lo, hi), (dmi, K, "Le", lo, hi), AF.Abs, bias=0.9375)
+            act(("col", lo, hi), (dmi, K, "Le", lo, hi), AF.Abs, bias=OFF)
         elif k == "F":
-            if c % 2 == 1:
-                mm(z(c // 2), (I32, ("zc", 32 * c - 32, 32 * c + 32)), final=False)
             tt(("hit", lo, hi), ("col", lo, hi), b, ALU.is_equal)
-            if c % 2 == 1:
-                listpass(z(c // 2), "WZ", 16, "hit", c // 2, first=False)
-        elif k == "W":
-            mm(b, ("Ib", ("V", lo, hi)), ("ZT", ("hit", lo, hi)))
+        elif k == "zm":
+            mm(z, (I16, ("zc", h0, h1)), final=False)
+            listpass(z, WZ, "hit", c, first=False)
+        elif k == "z":
+            act(("zl", h0, h1), z, AF.Relu, scale=1 / UP)
+        elif k == "zv":
+            ts(("zl", h0, h1), z, 1 / UP, ALU.mult, 0.0, ALU.max)
         elif k == "i":
-            tt(("f0", h0, h1), ("e", h0, h1), z(c), ALU.max)
-            cp(("Lin", h0, h1), ("f0", h0, h1))
-        elif k == "k":
-            act(("nok", h0, h1), z(c), AF.Sigmoid)
-        elif k == "kv":
-            ts(("nok", h0, h1), z(c), 0.0, ALU.is_gt)
-        elif k == "t":
-            tt(("t1", h0, h1), n1(c), ("nok", h0, h1), ALU.mult)
-            mm(X(c), (I32, ("t1", h0, h1)), final=False)
-        elif k == "te":
-            tt("t2", "e", "nok", ALU.mult)
-            if last:
-                tt("dd", "t2", "t1", ALU.subtract)
-        elif k == "sc":
-            tt("sc", DD, "nok", ALU.mult)
-        elif k == "nm":
-            mm(NP, (I32, "nsx"), (I32, "sc"))
-        elif k == "hi":
-            act(("hi", oc, oc + 128), NP)
-        elif k == "lo":
-            tt(("lo", oc, oc + 128), NP, ("hi", oc, oc + 128), ALU.subtract)
-            p_rows()
+            tt(("f0", h0, h1), ("e", h0, h1), z, ALU.min)
+            ts(("Lin", h0, h1), ("f0", h0, h1), float(K), ALU.add)
         elif k == "H" or k == "Hv":
-            lo, hi = OPT["ins"][c]
+            lo, hi = INSTALL[c]
             (act if k == "H" else cp)(("M", S + lo, S + hi), (win, 2 * K, "Lin", lo, hi))
+        elif k == "y":
+            blockpass(ZB, "WK" if last else WZ, "hit", range(8 * c, 8 * c + 8))
+        elif k == "yb":
+            act("zb", ZB)
+        elif k == "pm":
+            for d in (0, 128):
+                mm(("B7", 128 + d, 256 + d), (Ib, (opt, d, d + 128)), ("NI", ("nst", d, d + 128)), *goneb, (Ib, ("nst", d, d + 128)))
+        elif k == "np":
+            act(opt, NP)
+        elif k == "pd":
+            dma("s", [opt], [("P", S, S + K)], [(T.P[1 + 2 * d:128:16, S:S + K], T[opt][:, 128 * d:128 * d + 128]) for d in range(2)])
+        elif k == "W":
+            mm(b, (Ib, ("V", lo, hi)), ("ZT", ("hit", lo, hi)))
         elif k == "I":
             act(("V", lo, hi), b, AF.Sigmoid, bias=-128.0, scale=256.0)
-        elif k == "Iv":
-            ts(("V", lo, hi), b, 0.5, ALU.is_gt)
         elif k == "G":
             tt(("acm", lo, hi), (acr, K, "Le", lo, hi), ("hit", lo, hi), ALU.mult)
-            if c % 2 == 1:
-                listpass(X(c // 2), "WA", 16, "acm", c // 2, first=False)
-        elif k == "s":
-            ts(("Lns", h0, h1), X(c), float(S), ALU.add)
-        elif k == "x":
-            act(("nsx", h0, h1), X(c), AF.Identity, bias=S - 7.5)
         elif k == "em":
-            mm(EE, (I32, "nsx"), ("NI", "t1"), (I32, "t2"))
+            mm(ee, (I16, ("e", h0, h1)), *gone, final=False)
+            listpass(ee, "WA", "acm", c, first=False)
         elif k == "e":
-            act("e", EE, AF.Identity, bias=7.5 - S)
-        elif k == "u":
-            for i in range(16):
-                mm(UU, (("WY", 128 - i, 256 - i), ("V", 128 * i, 128 * i + 128)), first=i == 0, final=i == 15)
-            act("ou", UU)
+            if last:
+                act(("oe", h0, h1), ee)
+                if c == 1:
+                    dma("a", ["oe"], [], [(T.ye[:], T.oe[:])])
+            else:
+                cp(("e", h0, h1), ee)
+        elif k == "sm":
+            more = [] if last else [(I16, ("e", h0, h1))]
+            mm(n1, ("NI16", ("e", h0, h1)), *gone, *more, ("I2K", ("zl", h0, h1)), first=False)
+        elif k == "sd":
+            act(("dd", h0, h1), n1)
+        elif k == "s":
+            if last:
+                tt(("oy", h0, h1), ("dd", h0, h1), ee, ALU.add)
+                if c == 1:
+                    dma("s", ["oy"], [], [(T.yn[:], T.oy[:])])
+            else:
+                cp(("Lns", h0, h1), n1)
+        elif k == "um":
+            blockpass(UO, "WU", "V")
+        elif k == "uo":
+            act("uo", UO)
+        elif k == "ym":
+            mm(LE, (Ib, "uo"), *goneb, (Ib, "zb"))
+        elif k == "yu":
+            act("ou", LE, AF.Identity, bias=-1.0)
             dma("a", ["ou"], [], [(T.yu[:], T.ou[:])])
-        elif k == "y":
-            ts(("oy", h0, h1), X(c), float(S), ALU.add)
-            if c == 1:
-                dma("s", ["oy"], [], [(T.yn[:], T.oy[:])])
-            tt(("oe", h0, h1), X(c), ("dd", h0, h1), ALU.add)
-            if c == 1:
-                dma("a", ["oe"], [], [(T.ye[:], T.oe[:])])
-        elif k == "V":
-            ts(("V", lo, hi), b, PI, ALU.is_equal)
-        elif k == "late":
-            ts("zc", "z0", PI, ALU.add)
-            cp("WA", ("WW", 0, 144))
-            tt("ZT", "zr", ("BB", 16, 144), ALU.subtract)
         else:
             raise ValueError(name)
 
-    for name in OPT["first"].split():
-        cur[0] = (0, "first", name)
-        step(0, name)
-    for t in range(RO):
-        last = t == RO - 1
-        key = "last" if last else "next"
-        for name in OPT[key].split():
-            nxt = name[0] in "ABCDPap" or name in ("n0", "n1", "d", "old")
-            if not (name in ("d", "old") and t + 1 == RO - 1):
-                cur[0] = (t, key, name)
-                step(t + 1 if nxt else t, name)
-    cur[0] = None
+    for phase in [("first", 0)] + [("next", t) for t in range(RO - 1)] + [("last", RO - 1)]:
+        key, t = phase
+        for name in ORDER[key].split():
+            nxt = key == "next" and (name[0] in "ABCDNP" or name.rstrip("01") in ("n", "st", "og"))
+            once = key == "next" and name in ("k7", "op1")
+            if not (once and t) and not (name.rstrip("01") in ("st", "og") and t + nxt == RO - 1):
+                step(t + nxt, name)
 
     g.wait_ge(T.sem.sent, sent[0])
     for s, val in toks.items():

@@ -6,38 +6,40 @@ N, W, K, BASE, RO = 4, 8192, 2048, 4096, 4
 CH = 512
 FAR, BIG, UP, OFF = 8192.0, 2.0 ** 40, 2.0 ** 22, 0.75
 TABLE = [(0, 768), (768, 2048)]
-INSTALL = [(0, 1024), (1024, 1792), (1792, 2048)]
-ACCH = [(512 * i, 512 * i + 512) for i in range(4)]
-ACDIR = (2, 3)
+INSTALL = [(0, 1024), (1024, 1920), (1920, 2048)]
+ACCH = [(0, 256), (256, 1024), (1024, 2048)]
+ACDIR = (2,)
+HALVES = [(0, 1024), (1024, 2048)]
 ORDER = {
-    "first": "+par k0 w0 w1 wg6 wv4 w2 +u k2 +mnt k3 +i0 Va3 k1 +i1 w3 k4 wv5 wg7 V1 +c0 o0 V0 +ns A0 V2 ns B3 B0 B2 +e ee A1 xo P0 lm N0 Cv0 k5 +c1 o1 "
-             "B1 op0 P1 st N1 C1 n0 og1 Cv2 og0 +c3 D0 q3 +c2 q2 C3 n1 le k6 D1 o3 o2",
-    "next": "m1 d2 d3 E1 F1 W1 E0 E3 F0 E2 F3 zm0 F2 y0 I1 og1 k7 i0 zm1 i1 zv1 z0 y1 r0 r1 Hv2 Hv1 H0 yb W3 I3 G0 pm np pd W0 W2 A0 G1 em0 G3 e0 G2 m0 "
-            "sm0 s0 I0 A1 og0 em1 B0 e1 lm sm1 B1 s1 I2 P0 le B3 N0 B2 P1 Cv0 N1 n0 D0 C1 C2 st n1 C3 D1 op1",
-    "last": "um E0 d2 d3 E1 E2 F0 m0 E3 F1 G0 y0 zm0 m1 z0 sm0 F2 uo F3 zm1 z1 y1 yb G1 em0 ym yu sd0 sm1 sd1 G2 G3 s0 em1 s1 e0 e1",
+    "first": "#x4 +mnt w0 k0 wv3 w7 xm0 +u ur wv4 wv2 k2 +par w1 #xg xm1 hi #z0 #xh wv5 +i0 k4 +i1 wg6 V2 +c0 o0 +ns V1 +e k9 k3 A0 k8 ee ns V3 k6 Av1 "
+             "b2 lm +c1 og0 xo Vv0 op0 b3 +c2 b1 P0 B1 C1 P1 lev B2 N0 b0 B0 o1 st C2 k5 B3 N1 nv0 og1 Cv0 D1 C3 D0 n1 q2",
+    "next0": "r0 E1 m1 E0 d3 F1 W1 o2 E3 F0 E2 zm0 d2 r1 og0 y0 F3 i0 H0 F2 og1 zv0 Iv1 zm1 i1 Hv1 y1 yb W3 H2 G0 I3 pm np m0 pd W2 G1 A0 W0 A1 G3 em0 "
+             "zv1 ev0 sm0 I0 G2 em1 I2 sv0 b0 B0 ev1 sm1 b1 op1 P0 N0 B1 lm s1 P1 b2 Cv0 b3 C1 B2 N1 st k7 le C2 nv0 n1 B3 C3 D0 D1",
+    "next": "m1 d2 og1 d3 E1 F1 W1 E0 F0 zm0 y0 E3 F3 E2 F2 zm1 I1 r0 og0 i0 r1 H0 z0 y1 yb G0 W3 i1 zv1 pm H2 Hv1 W2 G1 npv pd I3 G3 A0 W0 I0 em0 e0 "
+            "m0 sm0 A1 G2 em1 b1 Iv2 sv0 b0 B0 ev1 P0 sm1 lm B1 sv1 P1 st Cv0 C1 N0 b2 B2 N1 C2 le n1 nv0 b3 B3 D0 D1 C3",
+    "last": "um m0 E0 m1 E1 d2 uo d3 F0 E2 F1 zm0 y0 E3 G0 z0 F2 sm0 F3 y1 zm1 sd0 yb G1 em0 G2 G3 z1 sm1 sd1 ym yu s0 em1 e0 s1 e1",
 }
+PHASES = [("first", 0), ("next0", 0), ("next", 1), ("next", 2), ("last", 3)]
 
 SCRATCH = {
     "M": ("sbuf", [128, W], "bfloat16"), "P": ("sbuf", [128, W], "bfloat16"),
-    "acm": ("sbuf", [128, K], "float16"), "aco": ("sbuf", [128, K], "int32"),
-    "pi": ("sbuf", [128, 512], "int32"),
+    "acm": ("sbuf", [128, K], "float16"), "aco": ("sbuf", [128, K], "int32"), "pi": ("sbuf", [128, 512], "int32"),
     "xm": ("sbuf", [128, 2, 4, 16], "int32"), "xmf": ("sbuf", [128, 4, 2, 16], "float32"), "xmt": ("sbuf", [128, 128], "float32"),
     "ui": ("sbuf", [128, CH], "int32"), "ei": ("sbuf", [128, 128], "int32"), "ni": ("sbuf", [128, 128], "int32"),
-    "cj": ("sbuf", [128, 6], "int32"), "cf": ("sbuf", [128, 12], "float32"),
-    "J16": ("sbuf", [128, 256], "float16"), "WA": ("sbuf", [128, 144], "float16"),
+    "cj": ("sbuf", [128, 9], "int32"), "cf": ("sbuf", [128, 17], "float32"),
 }
 for _n in ("V", "m1", "mk", "m2", "col", "hit", "pg"):
     SCRATCH[_n] = ("sbuf", [128, K], "bfloat16")
 for _n in ("ur", "x4", "E4", "hi", "lo", "xh"):
     SCRATCH[_n] = ("sbuf", [128, CH], "bfloat16")
-for _n in ("xs", "xg", "J", "BB", "WW", "nst", "op0", "op1"):
+for _n in ("xg", "J", "BB", "WW", "nst", "op0", "op1"):
     SCRATCH[_n] = ("sbuf", [128, 256], "bfloat16")
-for _n in ("WZ0", "WZ1", "WK", "WP", "WU"):
+for _n in ("WZ", "WK", "WP"):
     SCRATCH[_n] = ("sbuf", [128, 144], "bfloat16")
-for _n in ("ZT", "zr", "NI", "KB", "KN", "I2K", "zl", "zb", "uo"):
+for _n in ("ZT", "NI", "KB", "KN", "I2K", "zl", "uo"):
     SCRATCH[_n] = ("sbuf", [128, 128], "bfloat16")
-for _n in ("NI16", "zc", "e", "f0"):
-    SCRATCH[_n] = ("sbuf", [128, 128], "float16")
+for _n, _w in (("zc", 128), ("e", 128), ("zd", 64)):
+    SCRATCH[_n] = ("sbuf", [128, _w], "float16")
 for _n in ("z0", "dd", "oy", "oe", "ou"):
     SCRATCH[_n] = ("sbuf", [128, 128], "float32")
 for _n in ("Lns", "Ln1", "Le", "Lin", "Lm"):
@@ -45,14 +47,18 @@ for _n in ("Lns", "Ln1", "Le", "Lin", "Lm"):
 for _t in range(RO):
     SCRATCH["dmo%d" % _t] = ("sbuf", [128, K], "bfloat16")
     SCRATCH["dmi%d" % _t] = ("sbuf", [128, K], "bfloat16")
+    SCRATCH["zb%d" % _t] = ("sbuf", [128, 128], "bfloat16")
 for _t in range(RO - 1):
     SCRATCH["win%d" % _t] = ("sbuf", [128, 2 * K], "bfloat16")
     SCRATCH["acr%d" % _t] = ("sbuf", [128, K], "int32")
-for _t in range(8):
+for _t in range(2):
+    SCRATCH["Q%d" % _t] = ("psum", [128, 2 * CH], "float32")
+for _t in range(4, 8):
     SCRATCH["B%d" % _t] = ("psum", [128, CH], "float32")
 
-SEMAPHORES = (["cv", "ca", "cp", "cg", "sent", "hsent"] + ["dm%d_%d" % (t, i) for t in range(RO) for i in range(4)]
-              + ["acs%d" % t for t in range(N - 1)] + ["h%d" % t for t in range(4)] + ["d%d" % i for i in range(48)])
+SEMAPHORES = (["cv", "ca", "cp", "cg", "sent", "hsent"] + ["dm%d_%d" % (t, i) for t in range(RO) for i in range(len(TABLE))]
+              + ["acs%d_%d" % (t, i) for t in range(N - 1) for i in range(len(ACCH))] + ["h%d" % i for i in range(len(ACCH))]
+              + ["d%d" % i for i in range(48)])
 
 
 def helper(T, topo, r):
@@ -74,11 +80,11 @@ def helper_program(g, core, T, topo, r):
     for s in range(N - 1):
         dst = T.cores[(r - 1 - s) % N]
         rid, pid, _ = topo.addr(dst)
-        for i, (a, b) in enumerate(ACCH):
-            if s == (1 if i in ACDIR else 0):
-                g.wait_ge(T.sem["h%d" % i], bits(on_chip(T, topo, r, core)))
+        for i, (a, b) in enumerate(HALVES if s else ACCH):
+            if (a, b) in ACCH and s == (1 if ACCH.index((a, b)) in ACDIR else 0):
+                g.wait_ge(T.sem["h%d" % ACCH.index((a, b))], bits(on_chip(T, topo, r, core)))
             if s or i not in ACDIR:
-                g.remote_dma(T["acr%d" % s][:, a:b], T.aco[:, a:b], T.sem["acs%d" % s], T.sem.hsent, pid, rid, topo.mask(core, dst))
+                g.remote_dma(T["acr%d" % s][:, a:b], T.aco[:, a:b], T.sem["acs%d_%d" % (s, i)], T.sem.hsent, pid, rid, topo.mask(core, dst))
                 total += bits(topo.mask(core, dst))
     g.wait_ge(T.sem.hsent, total)
 
@@ -111,7 +117,8 @@ def rank_program(g, core, T, topo):
                     if q == "p" and q2 == "p":
                         continue
                     whole = ps and q2 != q
-                    if not whole and (h2 <= lo or hi <= l2):
+                    unit = CH if whole else 1
+                    if (h2 - 1) // unit < lo // unit or (hi - 1) // unit < l2 // unit:
                         continue
                     if kind == "r" and k2 == "r" and not whole:
                         continue
@@ -188,6 +195,9 @@ def rank_program(g, core, T, topo):
     def act(out, in_, f=AF.Copy, bias=0.0, scale=1.0):
         op("a", rd(in_, bias, scale), [out], lambda: a.activation(ap(out), ap(in_), f, bias=sca(bias), scale=sca(scale)))
 
+    def gcopy(out, in_):
+        op("g", [in_], [out], lambda: g.affine_select(ap(out), ap(in_), [[0, out[2] - out[1]]], ALU.is_ge, 0.0, 0, 0))
+
     def mm(out, *terms, first=True, final=True):
         for i, (l, x) in enumerate(terms):
             op("p", rd(l, x), [out], lambda: pe.matmul(ap(out), ap(l), ap(x), first and i == 0, final and i == len(terms) - 1))
@@ -205,8 +215,9 @@ def rank_program(g, core, T, topo):
             note("rem", [], [("dmi%d" % t, lo, hi)], ("dm%d_%d" % (t, i), bits(topo.mask(T.cores[(r + 1 + t % 3) % N], core))))
     for s in range(N - 1):
         q = (r + 1 + s) % N
-        note("rem", [], ["acr%d" % s], ("acs%d" % s, sum(
-            bits(topo.mask(T.cores[q] if s == 0 and i in ACDIR else helper(T, topo, q), core)) for i in range(len(ACCH)))))
+        for i, (lo, hi) in enumerate(HALVES if s else ACCH):
+            src = T.cores[q] if s == 0 and i in ACDIR else helper(T, topo, q)
+            note("rem", [], [("acr%d" % s, lo, hi)], ("acs%d_%d" % (s, i), bits(topo.mask(src, core))))
 
     loads = {"par": ("pi", [(T.pi[:], T.par[:])]), "u": ("ui", [(T.ui[0:32, :], T.u0[:])]),
              "mnt": ("xm", [(T.xm[:, j, :, :], T.mnt[j:8:2, :]) for j in range(2)]),
@@ -221,96 +232,97 @@ def rank_program(g, core, T, topo):
     def count_p(lo, hi):
         op("g", [], [("P", lo, hi)], lambda: g.iota(T.P[:, lo:hi], [[0, (hi - lo) // 128], [1, 128]], 0, 0, **small))
 
-    op("g", [], [("cj", 0, 2)], lambda: g.iota(T.cj[:, 0:2], [[1, 2]], 0, 1))
+    op("g", [], [("cj", 0, 4)], lambda: g.iota(T.cj[:, 0:4], [[1, 4]], 0, 1))
     count_p(0, 256)
-    op("g", [], ["xs"], lambda: g.iota(T.xs[:], [[0, 2], [1, 128]], 0, 0, **small))
-    op("g", [], ["x4"], lambda: g.iota(T.x4[0:32, :], [[1, 4], [4, 8], [0, 16]], 0, 0, **small))
-    op("g", [], ["xh"], lambda: g.iota(T.xh[:], [[128, 4], [0, 128]], 0, 0, **small))
-    op("g", [], ["xg"], lambda: g.iota(T.xg[:], [[0, 2], [16, 8], [0, 16]], 0, 0, **small))
-    op("g", [], ["z0"], lambda: g.iota(T.z0[:], [[16, 128]], -K, 0, **small))
+    counters = {"x4": (T.x4[0:32, :], [[1, 4], [4, 8], [0, 16]], 0), "xh": (T.xh[:], [[128, 4], [0, 128]], 0),
+                "xg": (T.xg[:], [[0, 2], [16, 8], [0, 16]], 0), "z0": (T.z0[:], [[16, 128]], 0)}
 
-    PP, _, PG, PI, OD, SG, SP, SC, SK, BC, NPI, P5 = [("cf", j, j + 1) for j in range(12)]
-    chunks = [(CH * c, CH * c + CH) for c in range(4)]
-    Ib, I16, RF = ("J", 0, 128), ("J16", 0, 128), ("J16", 112, 240)
+    PP, PG, PI, SC, SN, SP, SK, BC, BV, P5 = [("cf", j, j + 1) for j in (0, 4, 5, 9, 11, 12, 13, 14, 15, 16)]
+    Ib, RF = ("J", 0, 128), ("J", 112, 240)
     BO, BR = ("BB", 0, 128), ("BB", 112, 240)
     HERE, BACK = ("WW", 112, 256), ("WW", 0, 144)
 
+    def banks(c0, c1):
+        return ("Q%d" % (c0 // 2), CH * (c0 % 2), CH * (c1 % 2) + CH)
+
     def prepare(c):
         if c == 0:
-            for j, src, m in ((2, 0, 112), (3, 0, 15), (4, 0, 1), (5, 1, 2)):
-                ts(("cj", j, j + 1), ("cj", src, src + 1), m, ALU.bitwise_and)
-            cp(("cf", 0, 6), "cj")
+            ts(("cj", 4, 5), ("cj", 0, 1), 112, ALU.bitwise_and)
+            ts(("cj", 5, 6), ("cj", 0, 1), 15, ALU.bitwise_and)
+            ts(("cj", 6, 9), ("cj", 1, 4), 2, ALU.bitwise_and)
+            cp(("cf", 0, 9), "cj")
             ts(P5, PI, 512.0, ALU.mult)
-            ts(NPI, PI, -1.0, ALU.mult)
-        elif c == 1:
-            cp("hi", "pi")
-            tt("lo", "pi", "hi", ALU.subtract)
+            ts(BV, PI, -FAR, ALU.mult, -FAR, ALU.add)
+            ts(SK, PI, 1.0, ALU.add)
+            ts("J", ("P", 0, 256), PP, ALU.is_equal)
+            ts("WW", ("P", 0, 256), PG, ALU.is_equal)
+        elif c == 8:
+            tt("lo", "pi", "B7", ALU.subtract)
+        elif c == 9:
             ts("xh", "xh", P5, ALU.add)
         elif c == 2:
             op("v", ["x4", PP], ["E4"], lambda: v.tensor_scalar(T.E4[0:32, :], T.x4[0:32, :], T.cf[0:32, 0:1], None, ALU.is_equal))
-            op("v", ["ui"], ["ur"], lambda: v.tensor_copy(T.ur[0:32, :], T.ui[0:32, :]))
             for j in range(4):
-                op("p", ["E4", "ur"], ["B%d" % j], lambda: pe.matmul(T["B%d" % j][:], T.E4[0:32, 128 * j:128 * j + 128], T.ur[0:32, :], True, True))
+                op("p", ["E4", "ur"], [banks(j, j)], lambda: pe.matmul(ap(banks(j, j)), T.E4[0:32, 128 * j:128 * j + 128], T.ur[0:32, :], True, True))
         elif c == 3:
-            for j in range(2):
-                op("v", ["xm"], [("xmf", j, j + 1)], lambda: v.tensor_copy(T.xmf[:, :, j, :], T.xm[:, j, :, :]))
             op("v", ["xmf"], ["xmt"], lambda: v.transpose(T.xmt[:], T.xmf[:]))
             for j in range(4):
                 op("v", ["xmt"], [("Lm", j, j + 1)], lambda: v.tensor_copy(T.Lm[:, j:128:4], T.xmt[:, 32 * j:32 * j + 32]))
             note("v", [], ["Lm"], ("cv", cnt["v"]))
         elif c == 4:
             ts("BB", "xg", PG, ALU.is_equal)
-            ts("WW", "xs", PG, ALU.is_equal)
-            ts("J16", "xs", PP, ALU.is_equal)
-            ts(SP, PI, 4.0, ALU.is_lt, OD, ALU.mult)
-            ts(SC, SG, -FAR, ALU.mult, FAR, ALU.add)
-            ts(BC, NPI, SC, ALU.mult, -OFF, ALU.add)
+            ts(SP, PI, 2.0, ALU.is_lt)
+            ts(("cf", 9, 12), ("cf", 6, 9), -FAR, ALU.mult, FAR, ALU.add)
+            ts(BC, SN, PI, ALU.mult, -OFF, ALU.add)
             act("WP", HERE, scale=SP)
         elif c == 5:
-            ts("J", "xs", PP, ALU.is_equal)
             ts("zc", "z0", PI, ALU.add)
-            ts("NI16", I16, -1.0, ALU.mult)
-            cp("WA", BACK)
-            ts("zr", ("J", 16, 144), 2.0, ALU.mult)
-            tt("ZT", "zr", ("BB", 16, 144), ALU.subtract)
+            op("v", [], ["zd"], lambda: v.memset(T.zd[:], 1 - UP / K))
+            mm(("B6", 0, 128), (Ib, ("BB", 16, 144)), ("KN", ("J", 16, 144)))
+            act("ZT", ("B6", 0, 128), scale=FAR)
         elif c == 6:
-            act("WZ0", BACK, scale=BASE // K * UP)
+            act("WZ", BACK, scale=UP)
+            act("WK", BACK, scale=SK)
             for name, scale in (("KB", BIG), ("KN", -BIG), ("NI", -1.0), ("I2K", float(K))):
                 act(name, Ib, scale=scale)
         else:
-            ts(SK, PI, 1.0, ALU.add)
-            act("WZ1", BACK, scale=(BASE // K + 1) * UP)
-            act("WK", BACK, scale=SK)
-            act("WU", HERE, scale=SK)
+            dma("s", ["ur"], ["uo"], [(T.uo[:], T.ur[0:32, :])])
 
     def step(t, name):
         last = t == RO - 1
         S = BASE + K * (t % 2)
-        dmo, dmi, acr, win, opt = "dmo%d" % t, "dmi%d" % t, "acr%d" % (t % 3), "win%d" % t, "op%d" % (t % 2)
+        dmo, dmi, acr, win, opt, zb = "dmo%d" % t, "dmi%d" % t, "acr%d" % (t % 3), "win%d" % t, "op%d" % (t % 2), "zb%d" % t
         if name[0] == "+":
             return dma("s", [], [loads[name[1:]][0]], loads[name[1:]][1])
-        k, c = (name[:-1], int(name[-1])) if name[-1].isdigit() else (name, 0)
+        if name[0] == "#":
+            out, pattern, base = counters[name[1:]]
+            return op("g", [], [name[1:]], lambda: g.iota(out, pattern, base, 0, **small))
+        k = name.rstrip("0123456789")
+        c, c1 = int(name[len(k):][:1] or 0), int(name[len(k):][-1:] or 0)
+        vec = k[-1] == "v"
+        k = k.rstrip("v")
+        copy = cp if vec else act
         if k == "k":
             return prepare(c)
         if k == "wg":
             return count_p(1024 * c, 1024 * c + 1024)
-        if k == "w" or k == "wv":
+        if k == "w":
             for lo, hi in ((1024 * c, 1024 * c + 1024),) if c else ((256, 512), (512, 1024)):
-                (act if k == "w" else cp)(("P", lo, hi), ("P", 0, hi - lo))
+                copy(("P", lo, hi), ("P", 0, hi - lo))
             return
-        lo, hi = chunks[c]
-        b = "B%d" % c
+        lo, hi = CH * c, CH * c1 + CH
+        b = banks(c, c1)
+        each = [(banks(j, j), CH * j, CH * j + CH) for j in range(c, c1 + 1)]
         x0, x1 = 1024 * c, 1024 * c + 1024
         h0, h1 = 64 * c, 64 * c + 64
         n1 = ("B%d" % (4 + c), 0, 64)
         z, ee = ("B%d" % (6 + c), 0, 64), ("B%d" % (6 + c), 64, 128)
-        ZB, UO, LE, NP = ("B0", 0, 128), ("B6", 128, 256), ("B6", 256, 384), ("B7", 128, 384)
-        WZ = "WZ%d" % (t % 2)
+        ZB, UO, LE, NP = ("Q0", 0, 128), ("B6", 128, 256), ("B6", 256, 384), ("B7", 128, 384)
         gone = [("KB", ("zl", h0, h1)), ("KN", ("zl", h0, h1))]
-        goneb = [("KB", "zb"), ("KN", "zb")]
-        if k == "A" or k == "Av":
+        goneb = [("KB", zb), ("KN", zb)]
+        if k == "A":
             lo, hi = TABLE[c]
-            (act if k == "A" else cp)((dmo, lo, hi), ("M", W, "Lm", lo, hi))
+            copy((dmo, lo, hi), ("M", W, "Lm", lo, hi))
             dst = T.cores[(r - 1 - t % 3) % N]
             remote([(dmo, lo, hi)], T[dmi][:, lo:hi], T[dmo][:, lo:hi], "dm%d_%d" % (t, c), dst, topo.mask(core, dst))
         elif k == "o":
@@ -320,124 +332,145 @@ def rank_program(g, core, T, topo):
         elif k == "q":
             lo, hi = ACCH[c]
             dst = T.cores[(r - 1) % N]
-            remote([("aco", lo, hi)], T.acr0[:, lo:hi], T.aco[:, lo:hi], "acs0", dst, topo.mask(core, dst))
+            remote([("aco", lo, hi)], T.acr0[:, lo:hi], T.aco[:, lo:hi], "acs0_%d" % c, dst, topo.mask(core, dst))
         elif k == "xo":
-            dma("s", ["hi", "lo", "xh"], ["P"], [(T.P[j:128:16, :], T[src][:]) for j, src in ((1, "hi"), (3, "lo"), (5, "xh"))])
+            dma("s", ["hi", "lo", "xh"], ["P"], [(T.P[j:128:16, :], T[src][:]) for j, src in enumerate(("hi", "lo", "xh"))])
         elif k == "op":
             at = BASE + K * c
-            dma("s", [("P", at, at + K)], ["op%d" % c], [(T["op%d" % c][:, 128 * d:128 * d + 128], T.P[1 + 2 * d:128:16, at:at + K]) for d in range(2)])
+            dma("s", [("P", at, at + K)], ["op%d" % c], [(T["op%d" % c][:, 128 * d:128 * d + 128], T.P[d:128:16, at:at + K]) for d in range(2)])
+        elif k == "hi":
+            copy("hi", "pi")
+            mm("B7", (Ib, "hi"))
+        elif k == "ur":
+            if vec:
+                op("v", ["ui"], ["ur"], lambda: v.tensor_scalar(T.ur[0:32, :], T.ui[0:32, :], 1.0, None, ALU.add))
+            else:
+                op("a", ["ui"], ["ur"], lambda: a.activation(T.ur[0:32, :], T.ui[0:32, :], AF.Identity, bias=1.0, scale=1.0))
+        elif k == "xm":
+            if vec:
+                op("v", ["xm"], [("xmf", c, c + 1)], lambda: v.tensor_copy(T.xmf[:, :, c, :], T.xm[:, c, :, :]))
+            else:
+                op("a", ["xm"], [("xmf", c, c + 1)], lambda: a.activation(T.xmf[:, :, c, :], T.xm[:, c, :, :], AF.Copy, bias=0.0, scale=1.0))
         elif k == "ns":
-            cp("Lns", "ni")
+            copy("Lns", "ni")
         elif k == "ee":
-            cp("e", "ei")
+            copy("e", "ei")
         elif k == "V":
-            ts(("V", lo, hi), b, PI, ALU.is_equal)
-        elif k == "Va":
-            act(("mk", lo, hi), b, AF.Abs, bias=NPI)
-            act(("V", lo, hi), ("mk", lo, hi), AF.Sigmoid, bias=128.0, scale=-256.0)
+            if vec:
+                ts(("V", lo, hi), b, SK, ALU.not_equal, FAR, ALU.mult)
+            else:
+                act(("V", lo, hi), b, AF.Abs, bias=BV, scale=FAR)
+        elif k == "b":
+            for bj, l, h in each:
+                mm(bj, (BO, ("V", l, h)), final=False)
         elif k == "B":
-            tt(("m1", lo, hi), ("M", W, "Lns", lo, hi), ("V", lo, hi), ALU.mult)
-            mm(b, (BO, ("m1", lo, hi)))
+            tt(("m1", lo, hi), ("M", W, "Lns", lo, hi), ("V", lo, hi), ALU.subtract)
+            for bj, l, h in each:
+                mm(bj, (BO, ("m1", l, h)), first=False)
         elif k == "P":
-            act(("pg", x0, x1), ("P", W, "Lns", x0, x1))
+            copy(("pg", x0, x1), ("P", W, "Lns", x0, x1))
         elif k == "N" or k == "m":
             listpass(n1, "WP", "pg", c, final=k == "N")
         elif k == "n":
-            cp(("Ln1", h0, h1), n1)
+            copy(("Ln1", h0, h1), n1)
         elif k == "st":
-            dma("s", ["pg"], ["nst"], [(T.nst[:, 128 * d:128 * d + 128], T.pg[5 + 2 * d:128:16, :]) for d in range(2)])
+            dma("s", ["pg"], ["nst"], [(T.nst[:, 128 * d:128 * d + 128], T.pg[2 + d:128:16, :]) for d in range(2)])
         elif k == "C":
-            act(("mk", lo, hi), b, AF.Identity, bias=BC, scale=SC)
-        elif k == "Cv":
-            ts(("mk", lo, hi), b, SC, ALU.mult, BC, ALU.add)
+            if vec:
+                ts(("mk", lo, hi), b, SC, ALU.mult, BC, ALU.add)
+            else:
+                act(("mk", lo, hi), b, AF.Identity, bias=BC, scale=SC)
         elif k == "D" or k == "d":
             tt(("m2", lo, hi), ("M", W, "Ln1", lo, hi), ("mk", lo, hi), ALU.subtract)
-            mm(b, (BR, ("m2", lo, hi)))
+            for bj, l, h in each:
+                mm(bj, (BR, ("m2", l, h)))
         elif k == "lm":
             mm(LE, (RF, "e"))
         elif k == "le":
-            cp("Le", LE)
+            copy("Le", LE)
         elif k == "r":
             lo, hi = TABLE[c]
             dma("s", [(dmi, lo, hi)], [(win, K + lo, K + hi)],
                 [(T[win][0:112, K + lo:K + hi], T[dmi][16:128, lo:hi]), (T[win][112:128, K + lo:K + hi], T[dmi][0:16, lo:hi])])
         elif k == "og":
-            op("g", [("M", S + x0, S + x1)], [(win, x0, x1)],
-               lambda: g.affine_select(T[win][:, x0:x1], T.M[:, S + x0:S + x1], [[0, x1 - x0]], ALU.is_ge, 0.0, 0, 0))
+            gcopy((win, x0, x1), ("M", S + x0, S + x1))
         elif k == "E":
-            act(("col", lo, hi), (dmi, K, "Le", lo, hi), AF.Abs, bias=OFF)
+            if vec:
+                ts(("col", lo, hi), (dmi, K, "Le", lo, hi), OFF, ALU.add, 1 - OFF, ALU.max)
+            else:
+                act(("col", lo, hi), (dmi, K, "Le", lo, hi), AF.Abs, bias=OFF)
         elif k == "F":
             tt(("hit", lo, hi), ("col", lo, hi), b, ALU.is_equal)
         elif k == "zm":
-            mm(z, (I16, ("zc", h0, h1)), final=False)
-            listpass(z, WZ, "hit", c, first=False)
+            mm(z, (Ib, ("e", h0, h1)), ("I2K", "zd"), final=False)
+            listpass(z, "WZ", "hit", c, first=False)
         elif k == "z":
-            act(("zl", h0, h1), z, AF.Relu, scale=1 / UP)
-        elif k == "zv":
-            ts(("zl", h0, h1), z, 1 / UP, ALU.mult, 0.0, ALU.max)
+            if vec:
+                ts(("zl", h0, h1), z, 0.0, ALU.is_ge, float(S // K), ALU.mult)
+            else:
+                act(("zl", h0, h1), z, AF.Relu, bias=float(S // K), scale=1.5 * (S // K) / UP)
         elif k == "i":
-            tt(("f0", h0, h1), ("e", h0, h1), z, ALU.min)
-            ts(("Lin", h0, h1), ("f0", h0, h1), float(K), ALU.add)
-        elif k == "H" or k == "Hv":
+            tt(("Lin", h0, h1), ("zc", h0, h1), z, ALU.max)
+        elif k == "H":
             lo, hi = INSTALL[c]
-            (act if k == "H" else cp)(("M", S + lo, S + hi), (win, 2 * K, "Lin", lo, hi))
+            copy(("M", S + lo, S + hi), (win, 2 * K, "Lin", lo, hi))
         elif k == "y":
-            blockpass(ZB, "WK" if last else WZ, "hit", range(8 * c, 8 * c + 8))
+            blockpass(ZB, "WK", "hit", range(8 * c, 8 * c + 8))
         elif k == "yb":
-            act("zb", ZB)
+            copy(zb, ZB)
         elif k == "pm":
             for d in (0, 128):
                 mm(("B7", 128 + d, 256 + d), (Ib, (opt, d, d + 128)), ("NI", ("nst", d, d + 128)), *goneb, (Ib, ("nst", d, d + 128)))
         elif k == "np":
-            act(opt, NP)
+            copy(opt, NP)
         elif k == "pd":
-            dma("s", [opt], [("P", S, S + K)], [(T.P[1 + 2 * d:128:16, S:S + K], T[opt][:, 128 * d:128 * d + 128]) for d in range(2)])
+            dma("s", [opt], [("P", S, S + K)], [(T.P[d:128:16, S:S + K], T[opt][:, 128 * d:128 * d + 128]) for d in range(2)])
         elif k == "W":
-            mm(b, (Ib, ("V", lo, hi)), ("ZT", ("hit", lo, hi)))
+            for bj, l, h in each:
+                mm(bj, (Ib, ("V", l, h)), ("ZT", ("hit", l, h)))
         elif k == "I":
-            act(("V", lo, hi), b, AF.Sigmoid, bias=-128.0, scale=256.0)
+            if vec:
+                ts(("V", lo, hi), b, 0.0, ALU.max)
+            else:
+                act(("V", lo, hi), b, AF.Relu)
         elif k == "G":
             tt(("acm", lo, hi), (acr, K, "Le", lo, hi), ("hit", lo, hi), ALU.mult)
         elif k == "em":
-            mm(ee, (I16, ("e", h0, h1)), *gone, final=False)
-            listpass(ee, "WA", "acm", c, first=False)
+            mm(ee, (Ib, ("e", h0, h1)), *gone, final=False)
+            listpass(ee, "WW", "acm", c, first=False)
         elif k == "e":
-            if last:
-                act(("oe", h0, h1), ee)
-                if c == 1:
-                    dma("a", ["oe"], [], [(T.ye[:], T.oe[:])])
-            else:
-                cp(("e", h0, h1), ee)
+            copy(("oe" if last else "e", h0, h1), ee)
+            if last and c == 1:
+                dma("a", ["oe"], [], [(T.ye[:], T.oe[:])])
         elif k == "sm":
-            more = [] if last else [(I16, ("e", h0, h1))]
-            mm(n1, ("NI16", ("e", h0, h1)), *gone, *more, ("I2K", ("zl", h0, h1)), first=False)
+            more = [] if last else [(Ib, ("e", h0, h1))]
+            mm(n1, ("NI", ("e", h0, h1)), *gone, *more, ("I2K", ("zl", h0, h1)), first=False)
         elif k == "sd":
-            act(("dd", h0, h1), n1)
+            copy(("dd", h0, h1), n1)
         elif k == "s":
             if last:
                 tt(("oy", h0, h1), ("dd", h0, h1), ee, ALU.add)
                 if c == 1:
                     dma("s", ["oy"], [], [(T.yn[:], T.oy[:])])
             else:
-                cp(("Lns", h0, h1), n1)
+                copy(("Lns", h0, h1), n1)
         elif k == "um":
-            blockpass(UO, "WU", "V")
+            mm(UO, (Ib, "uo"), *[(x, "zb%d" % j) for j in range(RO - 1) for x in ("KB", "KN", Ib)])
         elif k == "uo":
-            act("uo", UO)
+            copy("uo", UO)
         elif k == "ym":
-            mm(LE, (Ib, "uo"), *goneb, (Ib, "zb"))
+            mm(LE, (Ib, "uo"), *goneb, (Ib, zb))
         elif k == "yu":
             act("ou", LE, AF.Identity, bias=-1.0)
             dma("a", ["ou"], [], [(T.yu[:], T.ou[:])])
         else:
             raise ValueError(name)
 
-    for phase in [("first", 0)] + [("next", t) for t in range(RO - 1)] + [("last", RO - 1)]:
-        key, t = phase
+    for key, t in PHASES:
         for name in ORDER[key].split():
-            nxt = key == "next" and (name[0] in "ABCDNP" or name.rstrip("01") in ("n", "st", "og"))
-            once = key == "next" and name in ("k7", "op1")
-            if not (once and t) and not (name.rstrip("01") in ("st", "og") and t + nxt == RO - 1):
+            stem = name.rstrip("01").rstrip("v")
+            nxt = key[:4] == "next" and (name[0] in "ABbCDNP" or stem in ("n", "st", "og"))
+            if not (stem in ("st", "og") and t + nxt == RO - 1):
                 step(t + nxt, name)
 
     g.wait_ge(T.sem.sent, sent[0])

from concourse.mybir import AluOpType, ActivationFunctionType

ALU = AluOpType
AF = ActivationFunctionType
N, W, K, BASE, RO = 4, 8192, 2048, 4096, 4
CH = 512
FAR, BIG, UP, OFF = 8192.0, 2.0 ** 40, 2.0 ** 22, 0.75
TABLE = [(0, 768), (768, 2048)]
INSTALL = [(0, 1024), (1024, 1920), (1920, 2048)]
ACCH = [(0, 256), (256, 1024), (1024, 2048)]
ACDIR = (2,)
HALVES = [(0, 1024), (1024, 2048)]
ORDER = {
    "first": "#x4 +mnt w0 k0 wv3 w7 xm0 +u ur wv4 wv2 k2 +par w1 #xg xm1 hi #z0 #xh wv5 +i0 k4 +i1 wg6 V2 +c0 o0 +ns V1 +e k9 k3 A0 k8 ee ns V3 k6 Av1 "
             "b2 lm +c1 og0 xo Vv0 op0 b3 +c2 b1 P0 B1 C1 P1 lev B2 N0 b0 B0 o1 st C2 k5 B3 N1 nv0 og1 Cv0 D1 C3 D0 n1 q2",
    "next0": "r0 E1 m1 E0 d3 F1 W1 o2 E3 F0 E2 zm0 d2 r1 og0 y0 F3 i0 H0 F2 og1 zv0 Iv1 zm1 i1 Hv1 y1 yb W3 H2 G0 I3 pm np m0 pd W2 G1 A0 W0 A1 G3 em0 "
             "zv1 ev0 sm0 I0 G2 em1 I2 sv0 b0 B0 ev1 sm1 b1 op1 P0 N0 B1 lm s1 P1 b2 Cv0 b3 C1 B2 N1 st k7 le C2 nv0 n1 B3 C3 D0 D1",
    "next": "m1 d2 og1 d3 E1 F1 W1 E0 F0 zm0 y0 E3 F3 E2 F2 zm1 I1 r0 og0 i0 r1 H0 z0 y1 yb G0 W3 i1 zv1 pm H2 Hv1 W2 G1 npv pd I3 G3 A0 W0 I0 em0 e0 "
            "m0 sm0 A1 G2 em1 b1 Iv2 sv0 b0 B0 ev1 P0 sm1 lm B1 sv1 P1 st Cv0 C1 N0 b2 B2 N1 C2 le n1 nv0 b3 B3 D0 D1 C3",
    "last": "um m0 E0 m1 E1 d2 uo d3 F0 E2 F1 zm0 y0 E3 G0 z0 F2 sm0 F3 y1 zm1 sd0 yb G1 em0 G2 G3 z1 sm1 sd1 ym yu s0 em1 e0 s1 e1",
}
PHASES = [("first", 0), ("next0", 0), ("next", 1), ("next", 2), ("last", 3)]

SCRATCH = {
    "M": ("sbuf", [128, W], "bfloat16"), "P": ("sbuf", [128, W], "bfloat16"),
    "acm": ("sbuf", [128, K], "float16"), "aco": ("sbuf", [128, K], "int32"), "pi": ("sbuf", [128, 512], "int32"),
    "xm": ("sbuf", [128, 2, 4, 16], "int32"), "xmf": ("sbuf", [128, 4, 2, 16], "float32"), "xmt": ("sbuf", [128, 128], "float32"),
    "ui": ("sbuf", [128, CH], "int32"), "ei": ("sbuf", [128, 128], "int32"), "ni": ("sbuf", [128, 128], "int32"),
    "cj": ("sbuf", [128, 9], "int32"), "cf": ("sbuf", [128, 17], "float32"),
}
for _n in ("V", "m1", "mk", "m2", "col", "hit", "pg"):
    SCRATCH[_n] = ("sbuf", [128, K], "bfloat16")
for _n in ("ur", "x4", "E4", "hi", "lo", "xh"):
    SCRATCH[_n] = ("sbuf", [128, CH], "bfloat16")
for _n in ("xg", "J", "BB", "WW", "nst", "op0", "op1"):
    SCRATCH[_n] = ("sbuf", [128, 256], "bfloat16")
for _n in ("WZ", "WK", "WP"):
    SCRATCH[_n] = ("sbuf", [128, 144], "bfloat16")
for _n in ("ZT", "NI", "KB", "KN", "I2K", "zl", "uo"):
    SCRATCH[_n] = ("sbuf", [128, 128], "bfloat16")
for _n, _w in (("zc", 128), ("e", 128), ("zd", 64)):
    SCRATCH[_n] = ("sbuf", [128, _w], "float16")
for _n in ("z0", "dd", "oy", "oe", "ou"):
    SCRATCH[_n] = ("sbuf", [128, 128], "float32")
for _n in ("Lns", "Ln1", "Le", "Lin", "Lm"):
    SCRATCH[_n] = ("sbuf", [128, 128], "uint16")
for _t in range(RO):
    SCRATCH["dmo%d" % _t] = ("sbuf", [128, K], "bfloat16")
    SCRATCH["dmi%d" % _t] = ("sbuf", [128, K], "bfloat16")
    SCRATCH["zb%d" % _t] = ("sbuf", [128, 128], "bfloat16")
for _t in range(RO - 1):
    SCRATCH["win%d" % _t] = ("sbuf", [128, 2 * K], "bfloat16")
    SCRATCH["acr%d" % _t] = ("sbuf", [128, K], "int32")
for _t in range(2):
    SCRATCH["Q%d" % _t] = ("psum", [128, 2 * CH], "float32")
for _t in range(4, 8):
    SCRATCH["B%d" % _t] = ("psum", [128, CH], "float32")

SEMAPHORES = (["cv", "ca", "cp", "cg", "sent", "hsent"] + ["dm%d_%d" % (t, i) for t in range(RO) for i in range(len(TABLE))]
              + ["acs%d_%d" % (t, i) for t in range(N - 1) for i in range(len(ACCH))] + ["h%d" % i for i in range(len(ACCH))]
              + ["d%d" % i for i in range(48)])


def helper(T, topo, r):
    c = T.cores[r]
    return [h for h in topo.cores_of(c) if T.rank_of(h) is None and topo.die(h) != topo.die(c)
            and all(topo.may_write(h, o) for o in T.cores if o != c)][-1]


def on_chip(T, topo, r, h):
    return topo.mask(T.cores[r], h) & ~topo.mask(T.cores[r], T.cores[(r + 1) % N])


def bits(m):
    return bin(m).count("1")


def helper_program(g, core, T, topo, r):
    total = 0
    for s in range(N - 1):
        dst = T.cores[(r - 1 - s) % N]
        rid, pid, _ = topo.addr(dst)
        for i, (a, b) in enumerate(HALVES if s else ACCH):
            if (a, b) in ACCH and s == (1 if ACCH.index((a, b)) in ACDIR else 0):
                g.wait_ge(T.sem["h%d" % ACCH.index((a, b))], bits(on_chip(T, topo, r, core)))
            if s or i not in ACDIR:
                g.remote_dma(T["acr%d" % s][:, a:b], T.aco[:, a:b], T.sem["acs%d_%d" % (s, i)], T.sem.hsent, pid, rid, topo.mask(core, dst))
                total += bits(topo.mask(core, dst))
    g.wait_ge(T.sem.hsent, total)


def rank_program(g, core, T, topo):
    r = T.rank_of(core)
    if r is None:
        for q in range(N):
            if helper(T, topo, q) == core:
                helper_program(g, core, T, topo, q)
        return

    Q = {"v": g.vector, "a": g.scalar, "p": g.tensor, "s": g.sync, "g": g}
    cnt = {"v": 0, "a": 0, "p": 0, "g": 0}
    waited = {q: {} for q in Q}
    regs = {}
    toks = {}
    nd = [0]

    def rng(x):
        return (x, 0, 1 << 30) if isinstance(x, str) else x

    def sync(q, reads, writes):
        need = {}
        for kind, lst in (("r", reads), ("w", writes)):
            for x in lst:
                n, lo, hi = rng(x)
                ps = SCRATCH[n][0] == "psum"
                for (l2, h2, k2, tok, q2) in regs.get(n, []):
                    if q == "p" and q2 == "p":
                        continue
                    whole = ps and q2 != q
                    unit = CH if whole else 1
                    if (h2 - 1) // unit < lo // unit or (hi - 1) // unit < l2 // unit:
                        continue
                    if kind == "r" and k2 == "r" and not whole:
                        continue
                    need[tok[0]] = max(need.get(tok[0], 0), tok[1])
        for s, v in need.items():
            if waited[q].get(s, 0) < v:
                Q[q].wait_ge(T.sem[s], v)
                waited[q][s] = v

    def note(q, reads, writes, tok):
        toks[tok[0]] = max(toks.get(tok[0], 0), tok[1])
        for x in writes:
            n, lo, hi = rng(x)
            regs[n] = [z for z in regs.get(n, []) if not (lo <= z[0] and z[1] <= hi)] + [(lo, hi, "w", tok, q)]
        for x in reads:
            n, lo, hi = rng(x)
            regs[n] = [z for z in regs.get(n, []) if not (z[2] == "r" and z[3][0] == tok[0] and lo <= z[0] and z[1] <= hi)] + [(lo, hi, "r", tok, q)]

    def op(q, reads, writes, fn):
        sync(q, reads, writes)
        cnt[q] += 1
        fn().then_inc(T.sem["c" + q], 1)
        note(q, reads, writes, ("c" + q, cnt[q]))

    def dma(q, reads, writes, pairs):
        sync(q, reads, writes)
        s = "d%d" % nd[0]
        nd[0] += 1
        for o, i in pairs:
            Q[q].dma_start(o, i).then_inc(T.sem[s], 16)
        note("dma", reads, writes, (s, 16 * len(pairs)))

    sent = [0]

    def remote(reads, out, in_, sem, dst, m):
        sync("g", reads, [])
        rid, pid, _ = topo.addr(dst)
        g.remote_dma(out, in_, T.sem[sem], T.sem.sent, pid, rid, m)
        sent[0] += bits(m)

    v, a, pe = g.vector, g.scalar, g.tensor

    def ap(x):
        if isinstance(x, str):
            return T[x][:]
        if len(x) == 3:
            return T[x[0]][:, x[1]:x[2]]
        return T[x[0]][:, 0:x[1]].indirect(T[x[2]][:, x[3] // 16:x[4] // 16])

    def rd(*xs):
        out = []
        for x in xs:
            if isinstance(x, str) or (isinstance(x, tuple) and len(x) == 3):
                out.append(x)
            elif isinstance(x, tuple):
                out += [(x[0], 0, x[1]), (x[2], x[3] // 16, x[4] // 16)]
        return out

    def sca(x):
        return ap(x) if isinstance(x, tuple) else x

    def ts(out, in0, s1, o0, s2=None, o1=None):
        if o1 is None:
            op("v", rd(in0, s1), [out], lambda: v.tensor_scalar(ap(out), ap(in0), sca(s1), None, o0))
        else:
            op("v", rd(in0, s1, s2), [out], lambda: v.tensor_scalar(ap(out), ap(in0), sca(s1), sca(s2), o0, o1))

    def tt(out, in0, in1, o):
        op("v", rd(in0, in1), [out], lambda: v.tensor_tensor(ap(out), ap(in0), ap(in1), o))

    def cp(out, in_):
        op("v", rd(in_), [out], lambda: v.tensor_copy(ap(out), ap(in_)))

    def act(out, in_, f=AF.Copy, bias=0.0, scale=1.0):
        op("a", rd(in_, bias, scale), [out], lambda: a.activation(ap(out), ap(in_), f, bias=sca(bias), scale=sca(scale)))

    def gcopy(out, in_):
        op("g", [in_], [out], lambda: g.affine_select(ap(out), ap(in_), [[0, out[2] - out[1]]], ALU.is_ge, 0.0, 0, 0))

    def mm(out, *terms, first=True, final=True):
        for i, (l, x) in enumerate(terms):
            op("p", rd(l, x), [out], lambda: pe.matmul(ap(out), ap(l), ap(x), first and i == 0, final and i == len(terms) - 1))

    def listpass(out, Wn, src, h, first=True, final=True):
        for i in range(16):
            op("p", [Wn, (src, 1024 * h, 1024 * h + 1024)], [out], lambda: pe.matmul(
                ap(out), T[Wn][:, 16 - i:144 - i], T[src][:, 1024 * h + i:1024 * h + 1024:16], first and i == 0, final and i == 15))

    def blockpass(out, Wn, src, rows=range(16)):
        mm(out, *[((Wn, 16 - i, 144 - i), (src, 128 * i, 128 * i + 128)) for i in rows], first=0 in rows, final=15 in rows)

    for t in range(RO):
        for i, (lo, hi) in enumerate(TABLE):
            note("rem", [], [("dmi%d" % t, lo, hi)], ("dm%d_%d" % (t, i), bits(topo.mask(T.cores[(r + 1 + t % 3) % N], core))))
    for s in range(N - 1):
        q = (r + 1 + s) % N
        for i, (lo, hi) in enumerate(HALVES if s else ACCH):
            src = T.cores[q] if s == 0 and i in ACDIR else helper(T, topo, q)
            note("rem", [], [("acr%d" % s, lo, hi)], ("acs%d_%d" % (s, i), bits(topo.mask(src, core))))

    loads = {"par": ("pi", [(T.pi[:], T.par[:])]), "u": ("ui", [(T.ui[0:32, :], T.u0[:])]),
             "mnt": ("xm", [(T.xm[:, j, :, :], T.mnt[j:8:2, :]) for j in range(2)]),
             "ns": ("ni", [(T.ni[:], T.ns0[:])]), "e": ("ei", [(T.ei[:], T.e0[:])])}
    for c in range(2):
        loads["i%d" % c] = (("M", BASE * c, BASE * c + BASE), [(T.M[:, BASE * c:BASE * c + BASE], T.idm[:, BASE * c:BASE * c + BASE])])
    for c, (lo, hi) in enumerate(ACCH):
        loads["c%d" % c] = (("aco", lo, hi), [(T.aco[:, lo:hi], T.ac[:, lo:hi])])

    small = dict(allow_small_or_imprecise_dtypes=True)

    def count_p(lo, hi):
        op("g", [], [("P", lo, hi)], lambda: g.iota(T.P[:, lo:hi], [[0, (hi - lo) // 128], [1, 128]], 0, 0, **small))

    op("g", [], [("cj", 0, 4)], lambda: g.iota(T.cj[:, 0:4], [[1, 4]], 0, 1))
    count_p(0, 256)
    counters = {"x4": (T.x4[0:32, :], [[1, 4], [4, 8], [0, 16]], 0), "xh": (T.xh[:], [[128, 4], [0, 128]], 0),
                "xg": (T.xg[:], [[0, 2], [16, 8], [0, 16]], 0), "z0": (T.z0[:], [[16, 128]], 0)}

    PP, PG, PI, SC, SN, SP, SK, BC, BV, P5 = [("cf", j, j + 1) for j in (0, 4, 5, 9, 11, 12, 13, 14, 15, 16)]
    Ib, RF = ("J", 0, 128), ("J", 112, 240)
    BO, BR = ("BB", 0, 128), ("BB", 112, 240)
    HERE, BACK = ("WW", 112, 256), ("WW", 0, 144)

    def banks(c0, c1):
        return ("Q%d" % (c0 // 2), CH * (c0 % 2), CH * (c1 % 2) + CH)

    def prepare(c):
        if c == 0:
            ts(("cj", 4, 5), ("cj", 0, 1), 112, ALU.bitwise_and)
            ts(("cj", 5, 6), ("cj", 0, 1), 15, ALU.bitwise_and)
            ts(("cj", 6, 9), ("cj", 1, 4), 2, ALU.bitwise_and)
            cp(("cf", 0, 9), "cj")
            ts(P5, PI, 512.0, ALU.mult)
            ts(BV, PI, -FAR, ALU.mult, -FAR, ALU.add)
            ts(SK, PI, 1.0, ALU.add)
            ts("J", ("P", 0, 256), PP, ALU.is_equal)
            ts("WW", ("P", 0, 256), PG, ALU.is_equal)
        elif c == 8:
            tt("lo", "pi", "B7", ALU.subtract)
        elif c == 9:
            ts("xh", "xh", P5, ALU.add)
        elif c == 2:
            op("v", ["x4", PP], ["E4"], lambda: v.tensor_scalar(T.E4[0:32, :], T.x4[0:32, :], T.cf[0:32, 0:1], None, ALU.is_equal))
            for j in range(4):
                op("p", ["E4", "ur"], [banks(j, j)], lambda: pe.matmul(ap(banks(j, j)), T.E4[0:32, 128 * j:128 * j + 128], T.ur[0:32, :], True, True))
        elif c == 3:
            op("v", ["xmf"], ["xmt"], lambda: v.transpose(T.xmt[:], T.xmf[:]))
            for j in range(4):
                op("v", ["xmt"], [("Lm", j, j + 1)], lambda: v.tensor_copy(T.Lm[:, j:128:4], T.xmt[:, 32 * j:32 * j + 32]))
            note("v", [], ["Lm"], ("cv", cnt["v"]))
        elif c == 4:
            ts("BB", "xg", PG, ALU.is_equal)
            ts(SP, PI, 2.0, ALU.is_lt)
            ts(("cf", 9, 12), ("cf", 6, 9), -FAR, ALU.mult, FAR, ALU.add)
            ts(BC, SN, PI, ALU.mult, -OFF, ALU.add)
            act("WP", HERE, scale=SP)
        elif c == 5:
            ts("zc", "z0", PI, ALU.add)
            op("v", [], ["zd"], lambda: v.memset(T.zd[:], 1 - UP / K))
            mm(("B6", 0, 128), (Ib, ("BB", 16, 144)), ("KN", ("J", 16, 144)))
            act("ZT", ("B6", 0, 128), scale=FAR)
        elif c == 6:
            act("WZ", BACK, scale=UP)
            act("WK", BACK, scale=SK)
            for name, scale in (("KB", BIG), ("KN", -BIG), ("NI", -1.0), ("I2K", float(K))):
                act(name, Ib, scale=scale)
        else:
            dma("s", ["ur"], ["uo"], [(T.uo[:], T.ur[0:32, :])])

    def step(t, name):
        last = t == RO - 1
        S = BASE + K * (t % 2)
        dmo, dmi, acr, win, opt, zb = "dmo%d" % t, "dmi%d" % t, "acr%d" % (t % 3), "win%d" % t, "op%d" % (t % 2), "zb%d" % t
        if name[0] == "+":
            return dma("s", [], [loads[name[1:]][0]], loads[name[1:]][1])
        if name[0] == "#":
            out, pattern, base = counters[name[1:]]
            return op("g", [], [name[1:]], lambda: g.iota(out, pattern, base, 0, **small))
        k = name.rstrip("0123456789")
        c, c1 = int(name[len(k):][:1] or 0), int(name[len(k):][-1:] or 0)
        vec = k[-1] == "v"
        k = k.rstrip("v")
        copy = cp if vec else act
        if k == "k":
            return prepare(c)
        if k == "wg":
            return count_p(1024 * c, 1024 * c + 1024)
        if k == "w":
            for lo, hi in ((1024 * c, 1024 * c + 1024),) if c else ((256, 512), (512, 1024)):
                copy(("P", lo, hi), ("P", 0, hi - lo))
            return
        lo, hi = CH * c, CH * c1 + CH
        b = banks(c, c1)
        each = [(banks(j, j), CH * j, CH * j + CH) for j in range(c, c1 + 1)]
        x0, x1 = 1024 * c, 1024 * c + 1024
        h0, h1 = 64 * c, 64 * c + 64
        n1 = ("B%d" % (4 + c), 0, 64)
        z, ee = ("B%d" % (6 + c), 0, 64), ("B%d" % (6 + c), 64, 128)
        ZB, UO, LE, NP = ("Q0", 0, 128), ("B6", 128, 256), ("B6", 256, 384), ("B7", 128, 384)
        gone = [("KB", ("zl", h0, h1)), ("KN", ("zl", h0, h1))]
        goneb = [("KB", zb), ("KN", zb)]
        if k == "A":
            lo, hi = TABLE[c]
            copy((dmo, lo, hi), ("M", W, "Lm", lo, hi))
            dst = T.cores[(r - 1 - t % 3) % N]
            remote([(dmo, lo, hi)], T[dmi][:, lo:hi], T[dmo][:, lo:hi], "dm%d_%d" % (t, c), dst, topo.mask(core, dst))
        elif k == "o":
            lo, hi = ACCH[c]
            hp = helper(T, topo, r)
            remote([("aco", lo, hi)], T.aco[:, lo:hi], T.aco[:, lo:hi], "h%d" % c, hp, on_chip(T, topo, r, hp))
        elif k == "q":
            lo, hi = ACCH[c]
            dst = T.cores[(r - 1) % N]
            remote([("aco", lo, hi)], T.acr0[:, lo:hi], T.aco[:, lo:hi], "acs0_%d" % c, dst, topo.mask(core, dst))
        elif k == "xo":
            dma("s", ["hi", "lo", "xh"], ["P"], [(T.P[j:128:16, :], T[src][:]) for j, src in enumerate(("hi", "lo", "xh"))])
        elif k == "op":
            at = BASE + K * c
            dma("s", [("P", at, at + K)], ["op%d" % c], [(T["op%d" % c][:, 128 * d:128 * d + 128], T.P[d:128:16, at:at + K]) for d in range(2)])
        elif k == "hi":
            copy("hi", "pi")
            mm("B7", (Ib, "hi"))
        elif k == "ur":
            if vec:
                op("v", ["ui"], ["ur"], lambda: v.tensor_scalar(T.ur[0:32, :], T.ui[0:32, :], 1.0, None, ALU.add))
            else:
                op("a", ["ui"], ["ur"], lambda: a.activation(T.ur[0:32, :], T.ui[0:32, :], AF.Identity, bias=1.0, scale=1.0))
        elif k == "xm":
            if vec:
                op("v", ["xm"], [("xmf", c, c + 1)], lambda: v.tensor_copy(T.xmf[:, :, c, :], T.xm[:, c, :, :]))
            else:
                op("a", ["xm"], [("xmf", c, c + 1)], lambda: a.activation(T.xmf[:, :, c, :], T.xm[:, c, :, :], AF.Copy, bias=0.0, scale=1.0))
        elif k == "ns":
            copy("Lns", "ni")
        elif k == "ee":
            copy("e", "ei")
        elif k == "V":
            if vec:
                ts(("V", lo, hi), b, SK, ALU.not_equal, FAR, ALU.mult)
            else:
                act(("V", lo, hi), b, AF.Abs, bias=BV, scale=FAR)
        elif k == "b":
            for bj, l, h in each:
                mm(bj, (BO, ("V", l, h)), final=False)
        elif k == "B":
            tt(("m1", lo, hi), ("M", W, "Lns", lo, hi), ("V", lo, hi), ALU.subtract)
            for bj, l, h in each:
                mm(bj, (BO, ("m1", l, h)), first=False)
        elif k == "P":
            copy(("pg", x0, x1), ("P", W, "Lns", x0, x1))
        elif k == "N" or k == "m":
            listpass(n1, "WP", "pg", c, final=k == "N")
        elif k == "n":
            copy(("Ln1", h0, h1), n1)
        elif k == "st":
            dma("s", ["pg"], ["nst"], [(T.nst[:, 128 * d:128 * d + 128], T.pg[2 + d:128:16, :]) for d in range(2)])
        elif k == "C":
            if vec:
                ts(("mk", lo, hi), b, SC, ALU.mult, BC, ALU.add)
            else:
                act(("mk", lo, hi), b, AF.Identity, bias=BC, scale=SC)
        elif k == "D" or k == "d":
            tt(("m2", lo, hi), ("M", W, "Ln1", lo, hi), ("mk", lo, hi), ALU.subtract)
            for bj, l, h in each:
                mm(bj, (BR, ("m2", l, h)))
        elif k == "lm":
            mm(LE, (RF, "e"))
        elif k == "le":
            copy("Le", LE)
        elif k == "r":
            lo, hi = TABLE[c]
            dma("s", [(dmi, lo, hi)], [(win, K + lo, K + hi)],
                [(T[win][0:112, K + lo:K + hi], T[dmi][16:128, lo:hi]), (T[win][112:128, K + lo:K + hi], T[dmi][0:16, lo:hi])])
        elif k == "og":
            gcopy((win, x0, x1), ("M", S + x0, S + x1))
        elif k == "E":
            if vec:
                ts(("col", lo, hi), (dmi, K, "Le", lo, hi), OFF, ALU.add, 1 - OFF, ALU.max)
            else:
                act(("col", lo, hi), (dmi, K, "Le", lo, hi), AF.Abs, bias=OFF)
        elif k == "F":
            tt(("hit", lo, hi), ("col", lo, hi), b, ALU.is_equal)
        elif k == "zm":
            mm(z, (Ib, ("e", h0, h1)), ("I2K", "zd"), final=False)
            listpass(z, "WZ", "hit", c, first=False)
        elif k == "z":
            if vec:
                ts(("zl", h0, h1), z, 0.0, ALU.is_ge, float(S // K), ALU.mult)
            else:
                act(("zl", h0, h1), z, AF.Relu, bias=float(S // K), scale=1.5 * (S // K) / UP)
        elif k == "i":
            tt(("Lin", h0, h1), ("zc", h0, h1), z, ALU.max)
        elif k == "H":
            lo, hi = INSTALL[c]
            copy(("M", S + lo, S + hi), (win, 2 * K, "Lin", lo, hi))
        elif k == "y":
            blockpass(ZB, "WK", "hit", range(8 * c, 8 * c + 8))
        elif k == "yb":
            copy(zb, ZB)
        elif k == "pm":
            for d in (0, 128):
                mm(("B7", 128 + d, 256 + d), (Ib, (opt, d, d + 128)), ("NI", ("nst", d, d + 128)), *goneb, (Ib, ("nst", d, d + 128)))
        elif k == "np":
            copy(opt, NP)
        elif k == "pd":
            dma("s", [opt], [("P", S, S + K)], [(T.P[d:128:16, S:S + K], T[opt][:, 128 * d:128 * d + 128]) for d in range(2)])
        elif k == "W":
            for bj, l, h in each:
                mm(bj, (Ib, ("V", l, h)), ("ZT", ("hit", l, h)))
        elif k == "I":
            if vec:
                ts(("V", lo, hi), b, 0.0, ALU.max)
            else:
                act(("V", lo, hi), b, AF.Relu)
        elif k == "G":
            tt(("acm", lo, hi), (acr, K, "Le", lo, hi), ("hit", lo, hi), ALU.mult)
        elif k == "em":
            mm(ee, (Ib, ("e", h0, h1)), *gone, final=False)
            listpass(ee, "WW", "acm", c, first=False)
        elif k == "e":
            copy(("oe" if last else "e", h0, h1), ee)
            if last and c == 1:
                dma("a", ["oe"], [], [(T.ye[:], T.oe[:])])
        elif k == "sm":
            more = [] if last else [(Ib, ("e", h0, h1))]
            mm(n1, ("NI", ("e", h0, h1)), *gone, *more, ("I2K", ("zl", h0, h1)), first=False)
        elif k == "sd":
            copy(("dd", h0, h1), n1)
        elif k == "s":
            if last:
                tt(("oy", h0, h1), ("dd", h0, h1), ee, ALU.add)
                if c == 1:
                    dma("s", ["oy"], [], [(T.yn[:], T.oy[:])])
            else:
                copy(("Lns", h0, h1), n1)
        elif k == "um":
            mm(UO, (Ib, "uo"), *[(x, "zb%d" % j) for j in range(RO - 1) for x in ("KB", "KN", Ib)])
        elif k == "uo":
            copy("uo", UO)
        elif k == "ym":
            mm(LE, (Ib, "uo"), *goneb, (Ib, zb))
        elif k == "yu":
            act("ou", LE, AF.Identity, bias=-1.0)
            dma("a", ["ou"], [], [(T.yu[:], T.ou[:])])
        else:
            raise ValueError(name)

    for key, t in PHASES:
        for name in ORDER[key].split():
            stem = name.rstrip("01").rstrip("v")
            nxt = key[:4] == "next" and (name[0] in "ABbCDNP" or stem in ("n", "st", "og"))
            if not (stem in ("st", "og") and t + nxt == RO - 1):
                step(t + nxt, name)

    g.wait_ge(T.sem.sent, sent[0])
    for s, val in toks.items():
        g.wait_ge(T.sem[s], val)
